import numpy as np
import ml_dtypes


def mxq(x, axis, fmt="e4m3"):
    dtype, down = {"e4m3": (ml_dtypes.float8_e4m3fn, 7), "e5m2": (ml_dtypes.float8_e5m2, 14)}[fmt]
    v = np.moveaxis(np.asarray(x, np.float32).astype(ml_dtypes.bfloat16).astype(np.float64), axis, -1)
    blocks = v.reshape(v.shape[:-1] + (-1, 32))
    amax = np.abs(blocks).max(-1, keepdims=True)
    byte = np.maximum(np.where(amax > 0, np.frexp(amax)[1] - 1 + 127, 0) - down, 1)
    scale = np.exp2(byte - 127.0)
    codes = (blocks / scale).astype(np.float32).astype(dtype).astype(np.float64)
    return np.moveaxis((codes * scale).reshape(v.shape), -1, axis)


WIDE = False


def mx_kscale(k):
    if not WIDE:
        return np.ones(k)
    levels = np.array([10, -10, 5, -5, 0])
    if k % 512:
        return np.exp2(np.random.permutation(np.resize(levels, k // 32))).repeat(32)
    a = np.empty((k // 512, 16))
    for p in range(k // 512):
        a[p, :8] = np.random.permutation(np.resize(levels, 8))
        for g in range(8):
            far = levels[np.abs(levels - a[p, g]) >= 10]
            a[p, g + 8] = far[np.random.randint(len(far))]
    return np.exp2(a.ravel()).repeat(32)


def f64(x):
    return np.asarray(x).astype(np.float64)


def striped(idx):
    return np.tile(idx.reshape(-1, 16).T, (8, 1)).astype(np.uint16)


def unstriped(offs):
    return offs[:16].T.reshape(-1).astype(np.int64)


def pack_weight(w):
    k, n = w.shape
    w = f64(np.asarray(w, np.float32).astype(ml_dtypes.bfloat16)).reshape(k // 32, 32, n)
    amax = np.abs(w).max(1)
    byte = np.clip(np.where(amax > 0, np.frexp(amax)[1] - 1 + 127 - 7, 1), 1, 254)
    scaled = (w * np.exp2(127.0 - byte)[:, None, :]).reshape(k, n).astype(np.float32)
    words = np.ascontiguousarray(scaled.reshape(k // 512, 128, 4, n).transpose(0, 1, 3, 2)).astype(ml_dtypes.float8_e4m3fn).view(np.uint8)
    return words, np.ascontiguousarray(byte.astype(np.uint8).reshape(k // 512, 16, n))


def unpack_weight(words, scales):
    g, p, n, _ = words.shape
    vals = np.ascontiguousarray(words).view(ml_dtypes.float8_e4m3fn).astype(np.float64) * np.repeat(np.exp2(scales.astype(np.float64) - 127.0), 8, axis=1)[..., None]
    return vals.transpose(0, 1, 3, 2).reshape(g * 512, n)


def planes(y):
    n, m = y.shape
    v = y.astype(np.float32).astype(ml_dtypes.bfloat16).astype(np.float64).reshape(n // 32, 32, m)
    top = np.abs(v).max(1)
    byte = np.clip(np.where(top > 0, np.frexp(top)[1] - 1 + 127 - 7, 1), 1, 254)
    codes = (v * np.exp2(127.0 - byte)[:, None, :]).reshape(n, m).astype(np.float32).astype(ml_dtypes.float8_e4m3fn).view(np.uint8)
    words = codes.reshape(n // 512, 128, 4, m).transpose(0, 1, 3, 2)
    return np.ascontiguousarray(words), np.ascontiguousarray(byte.astype(np.uint8).reshape(n // 512, 16, m))


K, T, S, V, H, N = 1024, 2048, 512, 256, 512, 512


def setup_inputs():
    n = np.random.standard_normal
    s = mx_kscale(K)[:, None]
    u = mx_kscale(H)
    near = np.random.permutation(S)
    packed_xT = pack_weight(n((K, T)) * s)
    return {
        "x_words": packed_xT[0],
        "x_scales": packed_xT[1],
        "w1": (n((K, H)) / np.sqrt(K) / s * u).astype(np.float32),
        "w2": (n((H, N)) / np.sqrt(H) / u[:, None]).astype(np.float32),
        "offs": striped(np.random.permutation(T)[:S]),
        "pos1": striped(near[:V]),
        "pos2": striped(near[V:]),
        "pos3": striped(np.random.permutation(S)[:V]),
        "pos4": striped(np.random.permutation(S)[:V]),
    }


def reference(x_words, x_scales, w1, w2, offs, pos1, pos2, pos3, pos4):
    xq = unpack_weight(x_words, x_scales)[:, unstriped(offs)]
    h = mxq(f64(w1), 0, "e4m3").T @ xq
    g0 = h[:, unstriped(pos1)]
    g1 = h[:, unstriped(pos2)]
    g2 = h[:, unstriped(pos3)]
    g3 = h[:, unstriped(pos4)]
    hi = np.maximum(np.maximum(np.maximum(g0, g1), g2), g3)
    lo = np.minimum(np.minimum(np.minimum(g0, g1), g2), g3)
    z = (g0 + g1 + g2 + g3 - hi - lo) / 2
    out_0 = mxq(f64(w2), 0, "e4m3").T @ mxq(z, 0, "e4m3")
    return (out_0,) + planes(out_0)

@@ -1,0 +1,227 @@
+from contextlib import ExitStack
+
+import concourse.mybir as mybir
+from concourse.masks import make_identity
+
+K, T, S, V, H, N = 1024, 2048, 512, 256, 512, 512
+FLOPS = 2 * K * H * S + 2 * H * N * V
+
+F32 = mybir.dt.float32
+BF16 = mybir.dt.bfloat16
+I32 = mybir.dt.int32
+U32 = mybir.dt.uint32
+U16 = mybir.dt.uint16
+U8 = mybir.dt.uint8
+FP8X4 = mybir.dt.float8_e4m3fn_x4
+ALU = mybir.AluOpType
+COPY = mybir.ActivationFunctionType.Copy
+
+P = 128
+PACK = 4
+K_PASS = P * PACK
+PASSES = K // K_PASS
+TILES = H // P
+HALVES = V // P
+PER_COLUMN = 16
+
+
+def tile_picked_ytrim_none_po_kernel(
+    tc, x_words, x_scales, w1, w2, offs, pos1, pos2, pos3, pos4, out_0, out_1, out_2
+):
+    nc = tc.nc
+    with ExitStack() as ctx:
+        keep = ctx.enter_context(tc.tile_pool(name="keep", bufs=1))
+        psum = ctx.enter_context(tc.psum_pool(name="psum", bufs=1))
+
+        def sb(shape, dtype, name):
+            return keep.tile(shape, dtype, name=name, align_bytes=64)
+
+        banks = [psum.tile([P, S], F32, name="bank%d" % i) for i in range(8)]
+        spent = {}
+
+        offs_sb = sb([P, S // PER_COLUMN], U16, "offs_sb")
+        nc.sync.dma_start(offs_sb[:], offs)
+
+        scale_table = sb([P, T], U8, "scale_table")
+        nc.vector.memset(scale_table[:].bitcast(I32), 0)
+
+        def load_words(g):
+            table = sb([P, T], U32, "word_table%d" % g)
+            nc.sync.dma_start(table[:].bitcast(I32), x_words[g].rearrange("p n t -> p (n t)").bitcast(I32))
+            return table
+
+        def load_w1(first, count):
+            raws = []
+            for g in range(PASSES):
+                raw = sb([P, PACK, count * P], F32, "w1_raw%d_%d" % (first, g))
+                rows = w1[g * K_PASS : (g + 1) * K_PASS, first * P : (first + count) * P]
+                nc.sync.dma_start(raw[:], rows.rearrange("(p j) c -> p j c", j=PACK))
+                raws.append(raw)
+            return [[raw[:, :, i * P : (i + 1) * P] for raw in raws] for i in range(count)]
+
+        word_tables = [load_words(0)]
+        for q in range(4):
+            nc.sync.dma_start(
+                scale_table[32 * q : 32 * q + 4 * PASSES, :].bitcast(I32),
+                x_scales[:, 4 * q : 4 * q + 4, :].bitcast(I32),
+            )
+        w1_raw = load_w1(0, 1)
+        word_tables.append(load_words(1))
+        pos_sb = []
+        for i, pos in enumerate((pos1, pos2, pos3, pos4)):
+            tile = sb([P, V // PER_COLUMN], U16, "pos_sb%d" % i)
+            nc.sync.dma_start(tile[:], pos)
+            pos_sb.append(tile)
+        w1_raw = w1_raw + load_w1(1, 1) + load_w1(2, 2)
+        w2_raw = sb([P, PACK, N], F32, "w2_raw")
+        nc.sync.dma_start(w2_raw[:], w2.rearrange("(p j) c -> p j c", j=PACK))
+
+        identity = sb([P, P], F32, "identity")
+        make_identity(nc, identity[:])
+
+        x_codes = [sb([P, S], U32, "x_codes%d" % g) for g in range(PASSES)]
+        x_plane = sb([P, S], U8, "x_plane")
+        nc.vector.tensor_copy(x_codes[0][:], word_tables[0][:].indirect(offs_sb[:]))
+        nc.vector.tensor_copy(x_plane[:], scale_table[:].indirect(offs_sb[:]))
+
+        def quantise_w1(c):
+            grouped = sb([P, PASSES, P * PACK], BF16, "w1_grouped%d" % c)
+            for g in range(PASSES):
+                nc.scalar.activation(
+                    grouped[:, g, :].rearrange("p (a i j) -> p a j i", i=4, j=PACK),
+                    w1_raw[c][g].rearrange("p j (a i) -> p a j i", i=4),
+                    COPY,
+                )
+            spent["w1_grouped%d" % c] = grouped[:].rearrange("p g n -> p (g n)")
+            codes = sb([P, PASSES * P], U32, "w1_codes%d" % c)
+            plane = sb([P, PASSES * P], U8, "w1_plane%d" % c)
+            nc.vector.quantize_mx(codes[:].bitcast(FP8X4), plane[:], grouped[:].rearrange("p g n -> p (g n)"))
+            return codes, plane
+
+        def first_product(c, codes, plane, pieces):
+            h = sb([P, S], F32, "h%d" % c)
+            width = S // pieces
+            for piece in range(pieces):
+                cols = slice(piece * width, (piece + 1) * width)
+                acc = banks[(c + piece + (c > 0)) % 2][:, 0:width]
+                for g in range(PASSES):
+                    nc.tensor.matmul_mx(
+                        acc,
+                        lhsT=codes[:, g * P : (g + 1) * P].bitcast(FP8X4),
+                        lhsT_scale=plane[:, g * P : (g + 1) * P],
+                        rhs=x_codes[g][:, cols].bitcast(FP8X4),
+                        rhs_scale=x_plane[4 * g : P, cols],
+                        start=(g == 0),
+                        stop=(g == PASSES - 1),
+                    )
+                nc.scalar.copy(h[:, cols], acc)
+            return h
+
+        first = quantise_w1(0)
+        for piece in range(2):
+            nc.vector.tensor_copy(
+                x_codes[1][:, piece * 256 : (piece + 1) * 256],
+                word_tables[1][:].indirect(offs_sb[:, piece * 16 : (piece + 1) * 16]),
+            )
+        h_tiles = [first_product(0, first[0], first[1], 2)]
+
+        z_rows = [sb([P, 2, H // 2], BF16, "z_rows%d" % half) for half in range(HALVES)]
+
+        def trim(unit, runs, reuse):
+            names = ("base", "e", "d", "f", "low", "high", "m1", "m2")
+            base, e, d, f, low, high, m1, m2 = [
+                spent[reuse[n]].bitcast(F32)[:, 0:V] if n in reuse else sb([P, V], F32, "%s_%d" % (n, unit))[:] for n in names
+            ]
+            spent["d"] = d
+            blocks = []
+            at = 0
+            for c, v0, count in runs:
+                cols = slice(at, at + count)
+                picks = [h_tiles[c][:].indirect(t[:, v0 // PER_COLUMN : (v0 + count) // PER_COLUMN]) for t in pos_sb]
+                nc.vector.tensor_copy(base[:, cols], picks[0])
+                nc.vector.tensor_tensor(d[:, cols], picks[2], base[:, cols], ALU.subtract)
+                nc.vector.tensor_tensor(f[:, cols], picks[3], base[:, cols], ALU.subtract)
+                nc.vector.tensor_tensor(e[:, cols], picks[1], base[:, cols], ALU.subtract)
+                for b in range(count // P):
+                    blocks.append((c, (v0 + b * P) // P, slice(at + b * P, at + (b + 1) * P)))
+                at = at + count
+            nc.vector.tensor_tensor(low, d, f, ALU.min)
+            nc.vector.tensor_tensor(high, d, f, ALU.max)
+            nc.vector.scalar_tensor_tensor(m1, e, 0.0, low, ALU.min, ALU.max)
+            nc.vector.scalar_tensor_tensor(m2, e, 0.0, high, ALU.max, ALU.min)
+            for b, (c, half, cols) in enumerate(blocks):
+                total = banks[2 * (unit % 2) + b][:, 0:P]
+                terms = (base, base, m1, m2)
+                for i, term in enumerate(terms):
+                    nc.tensor.matmul(
+                        total, term[:, cols], identity[:], start=(i == 0), stop=(i == len(terms) - 1), is_transpose=True
+                    )
+                nc.scalar.activation(
+                    z_rows[half][:, :, 64 * c : 64 * (c + 1)].rearrange("v u (q e) -> v u q e", e=2),
+                    total.rearrange("v (q u e) -> v u q e", u=2, e=2),
+                    COPY,
+                    scale=0.5,
+                )
+
+        out_codes = sb([P, V], U32, "out_codes")
+        out_plane = sb([P, V], U8, "out_plane")
+        out_rows = out_0.rearrange("(p t) v -> p t v", t=PACK)
+        out_words = out_1[0].rearrange("p n t -> p (n t)").bitcast(I32)
+
+        def second_product(half, w2_codes, w2_plane, mover):
+            cols = slice(half * P, (half + 1) * P)
+            turned = banks[4 + half][:, 0 : 2 * P].rearrange("p (u v) -> p u v", u=2)
+            for u in range(2):
+                nc.tensor.transpose(turned[:, u, :], z_rows[half][:, u, :].bitcast(F32), identity[:])
+            z_room = sb([P, P * 2 + P * PACK], BF16, "z_room%d" % half)
+            z_grouped = z_room[:, P * 2 :]
+            mover(
+                z_grouped.bitcast(F32).rearrange("p (v u) -> p v u", u=2),
+                turned.rearrange("p u v -> p v u"),
+            )
+            spent["z_room%d" % half] = z_room[:]
+            z_codes = sb([P, P], U32, "z_codes%d" % half)
+            z_plane = sb([P, P], U8, "z_plane%d" % half)
+            nc.vector.quantize_mx(z_codes[:].bitcast(FP8X4), z_plane[:], z_grouped)
+            y_acc = banks[6 + half][:].rearrange("p (t v) -> p t v", t=PACK)
+            for t in range(PACK):
+                nc.tensor.matmul_mx(
+                    y_acc[:, t, :],
+                    lhsT=w2_codes[:, t * P : (t + 1) * P].bitcast(FP8X4),
+                    lhsT_scale=w2_plane[:, t * P : (t + 1) * P],
+                    rhs=z_codes[:].bitcast(FP8X4),
+                    rhs_scale=z_plane[:],
+                    start=True,
+                    stop=True,
+                )
+            y_grouped = sb([P, P * PACK], BF16, "y_grouped%d" % half)
+            mover(y_grouped[:].rearrange("p (v t) -> p v t", t=PACK), y_acc.rearrange("p t v -> p v t"))
+            y = sb([P, PACK, P], F32, "y%d" % half)
+            nc.scalar.copy(y[:], y_acc)
+            nc.scalar.dma_start(out_rows[:, :, cols], y[:])
+            nc.vector.quantize_mx(out_codes[:, cols].bitcast(FP8X4), out_plane[:, cols], y_grouped[:])
+            nc.sync.dma_start(out_words[:, cols], out_codes[:, cols].bitcast(I32))
+
+        for c in (1, 2, 3):
+            codes, plane = quantise_w1(c)
+            h_tiles.append(first_product(c, codes, plane, 1))
+        trim(0, [(0, 0, V)], {})
+        trim(1, [(1, 0, V)], {"f": "w1_grouped2", "e": "w1_grouped3", "d": "d"})
+
+        w2_grouped = sb([P, N * PACK], BF16, "w2_grouped")
+        dealt = w2_grouped[:].rearrange("p (t m j) -> p m j t", t=PACK, j=PACK)
+        source = w2_raw[:].rearrange("p j (m t) -> p m j t", t=PACK)
+        for piece in range(4):
+            nc.scalar.copy(dealt[:, 32 * piece : 32 * (piece + 1)], source[:, 32 * piece : 32 * (piece + 1)])
+        spent["w2_grouped"] = w2_grouped[:]
+        w2_codes = sb([P, N], U32, "w2_codes")
+        w2_plane = sb([P, N], U8, "w2_plane")
+        nc.vector.quantize_mx(w2_codes[:].bitcast(FP8X4), w2_plane[:], w2_grouped[:])
+
+        trim(2, [(2, 0, P), (3, 0, P)], {"d": "d"})
+        second_product(0, w2_codes, w2_plane, nc.scalar.copy)
+        trim(3, [(2, P, P), (3, P, P)], {"f": "z_room0", "base": "w2_grouped", "d": "d"})
+        second_product(1, w2_codes, w2_plane, nc.vector.tensor_copy)
+        for q in range(4):
+            queue = nc.sync if q % 2 == 0 else nc.scalar
+            queue.dma_start(out_2[0][4 * q : 4 * q + 4, :].bitcast(I32), out_plane[32 * q : 32 * q + 4, :].bitcast(I32))

@@ -20,9 +20,11 @@ P = 128
 PACK = 4
 K_PASS = P * PACK
 PASSES = K // K_PASS
-TILES = H // P
-HALVES = V // P
-PER_COLUMN = 16
+QUADRANTS = 4
+ENTRIES = 16
+LINE = 4
+BANK = 512
+W2_PIECES = 4
 
 
 def tile_picked_ytrim_none_po_kernel(
@@ -33,13 +35,12 @@ def tile_picked_ytrim_none_po_kernel(
         keep = ctx.enter_context(tc.tile_pool(name="keep", bufs=1))
         psum = ctx.enter_context(tc.psum_pool(name="psum", bufs=1))
 
-        def sb(shape, dtype, name):
-            return keep.tile(shape, dtype, name=name, align_bytes=64)
+        def sb(shape, dtype, name, in_place_of=None):
+            return keep.tile(shape, dtype, name=name, tag=in_place_of or name, align_bytes=64)
 
-        banks = [psum.tile([P, S], F32, name="bank%d" % i) for i in range(8)]
-        spent = {}
+        banks = [psum.tile([P, BANK], F32, name="bank%d" % i) for i in range(8)]
 
-        offs_sb = sb([P, S // PER_COLUMN], U16, "offs_sb")
+        offs_sb = sb([P, S // ENTRIES], U16, "offs_sb")
         nc.sync.dma_start(offs_sb[:], offs)
 
         scale_table = sb([P, T], U8, "scale_table")
@@ -60,7 +61,7 @@ def tile_picked_ytrim_none_po_kernel(
             return [[raw[:, :, i * P : (i + 1) * P] for raw in raws] for i in range(count)]
 
         word_tables = [load_words(0)]
-        for q in range(4):
+        for q in range(QUADRANTS):
             nc.sync.dma_start(
                 scale_table[32 * q : 32 * q + 4 * PASSES, :].bitcast(I32),
                 x_scales[:, 4 * q : 4 * q + 4, :].bitcast(I32),
@@ -69,9 +70,9 @@ def tile_picked_ytrim_none_po_kernel(
         word_tables.append(load_words(1))
         pos_sb = []
         for i, pos in enumerate((pos1, pos2, pos3, pos4)):
-            tile = sb([P, V // PER_COLUMN], U16, "pos_sb%d" % i)
-            nc.sync.dma_start(tile[:], pos)
-            pos_sb.append(tile)
+            list_tile = sb([P, V // ENTRIES], U16, "pos_sb%d" % i)
+            nc.sync.dma_start(list_tile[:], pos)
+            pos_sb.append(list_tile)
         w1_raw = w1_raw + load_w1(1, 1) + load_w1(2, 2)
         w2_raw = sb([P, PACK, N], F32, "w2_raw")
         nc.sync.dma_start(w2_raw[:], w2.rearrange("(p j) c -> p j c", j=PACK))
@@ -84,29 +85,31 @@ def tile_picked_ytrim_none_po_kernel(
         nc.vector.tensor_copy(x_codes[0][:], word_tables[0][:].indirect(offs_sb[:]))
         nc.vector.tensor_copy(x_plane[:], scale_table[:].indirect(offs_sb[:]))
 
+        w1_grouped = []
+
         def quantise_w1(c):
             grouped = sb([P, PASSES, P * PACK], BF16, "w1_grouped%d" % c)
             for g in range(PASSES):
                 nc.scalar.activation(
-                    grouped[:, g, :].rearrange("p (a i j) -> p a j i", i=4, j=PACK),
-                    w1_raw[c][g].rearrange("p j (a i) -> p a j i", i=4),
+                    grouped[:, g, :].rearrange("p (a i j) -> p a j i", i=LINE, j=PACK),
+                    w1_raw[c][g].rearrange("p j (a i) -> p a j i", i=LINE),
                     COPY,
                 )
-            spent["w1_grouped%d" % c] = grouped[:].rearrange("p g n -> p (g n)")
+            w1_grouped.append(grouped[:].rearrange("p g n -> p (g n)"))
             codes = sb([P, PASSES * P], U32, "w1_codes%d" % c)
             plane = sb([P, PASSES * P], U8, "w1_plane%d" % c)
-            nc.vector.quantize_mx(codes[:].bitcast(FP8X4), plane[:], grouped[:].rearrange("p g n -> p (g n)"))
+            nc.vector.quantize_mx(codes[:].bitcast(FP8X4), plane[:], w1_grouped[c])
             return codes, plane
 
-        def first_product(c, codes, plane, pieces):
+        def first_product(c, operand, piece_banks, mover):
+            codes, plane = operand
             h = sb([P, S], F32, "h%d" % c)
-            width = S // pieces
-            for piece in range(pieces):
+            width = S // len(piece_banks)
+            for piece, bank in enumerate(piece_banks):
                 cols = slice(piece * width, (piece + 1) * width)
-                acc = banks[(c + piece + (c > 0)) % 2][:, 0:width]
                 for g in range(PASSES):
                     nc.tensor.matmul_mx(
-                        acc,
+                        bank[:, 0:width],
                         lhsT=codes[:, g * P : (g + 1) * P].bitcast(FP8X4),
                         lhsT_scale=plane[:, g * P : (g + 1) * P],
                         rhs=x_codes[g][:, cols].bitcast(FP8X4),
@@ -114,44 +117,46 @@ def tile_picked_ytrim_none_po_kernel(
                         start=(g == 0),
                         stop=(g == PASSES - 1),
                     )
-                nc.scalar.copy(h[:, cols], acc)
+                mover(h[:, cols], bank[:, 0:width])
             return h
 
-        first = quantise_w1(0)
+        first_operand = quantise_w1(0)
         for piece in range(2):
+            width = S // 2
             nc.vector.tensor_copy(
-                x_codes[1][:, piece * 256 : (piece + 1) * 256],
-                word_tables[1][:].indirect(offs_sb[:, piece * 16 : (piece + 1) * 16]),
+                x_codes[1][:, piece * width : (piece + 1) * width],
+                word_tables[1][:].indirect(offs_sb[:, piece * width // ENTRIES : (piece + 1) * width // ENTRIES]),
             )
-        h_tiles = [first_product(0, first[0], first[1], 2)]
+        h_tiles = [first_product(0, first_operand, banks[0:2], nc.vector.tensor_copy)]
+        for c in range(1, H // P):
+            h_tiles.append(first_product(c, quantise_w1(c), [banks[(c + 1) % 2]], nc.scalar.copy))
 
-        z_rows = [sb([P, 2, H // 2], BF16, "z_rows%d" % half) for half in range(HALVES)]
+        z_rows = [sb([P, 2, H // 2], BF16, "z_rows%d" % half) for half in range(V // P)]
 
-        def trim(unit, runs, reuse):
-            names = ("base", "e", "d", "f", "low", "high", "m1", "m2")
-            base, e, d, f, low, high, m1, m2 = [
-                spent[reuse[n]].bitcast(F32)[:, 0:V] if n in reuse else sb([P, V], F32, "%s_%d" % (n, unit))[:] for n in names
-            ]
-            spent["d"] = d
+        def trim(runs, base, gaps, pair, middle, totals):
             blocks = []
+            picks = []
             at = 0
             for c, v0, count in runs:
-                cols = slice(at, at + count)
-                picks = [h_tiles[c][:].indirect(t[:, v0 // PER_COLUMN : (v0 + count) // PER_COLUMN]) for t in pos_sb]
-                nc.vector.tensor_copy(base[:, cols], picks[0])
-                nc.vector.tensor_tensor(d[:, cols], picks[2], base[:, cols], ALU.subtract)
-                nc.vector.tensor_tensor(f[:, cols], picks[3], base[:, cols], ALU.subtract)
-                nc.vector.tensor_tensor(e[:, cols], picks[1], base[:, cols], ALU.subtract)
+                columns = slice(v0 // ENTRIES, (v0 + count) // ENTRIES)
+                picks.append((slice(at, at + count), [h_tiles[c][:].indirect(t[:, columns]) for t in pos_sb]))
                 for b in range(count // P):
-                    blocks.append((c, (v0 + b * P) // P, slice(at + b * P, at + (b + 1) * P)))
+                    blocks.append((c, v0 // P + b, slice(at + b * P, at + (b + 1) * P)))
                 at = at + count
-            nc.vector.tensor_tensor(low, d, f, ALU.min)
-            nc.vector.tensor_tensor(high, d, f, ALU.max)
-            nc.vector.scalar_tensor_tensor(m1, e, 0.0, low, ALU.min, ALU.max)
-            nc.vector.scalar_tensor_tensor(m2, e, 0.0, high, ALU.max, ALU.min)
-            for b, (c, half, cols) in enumerate(blocks):
-                total = banks[2 * (unit % 2) + b][:, 0:P]
-                terms = (base, base, m1, m2)
+            gap_b, gap_c, gap_d = gaps
+            low, high = pair
+            lower_middle, upper_middle = middle
+            for cols, pick in picks:
+                nc.vector.tensor_copy(base[:, cols], pick[0])
+            for gap, i in ((gap_c, 2), (gap_d, 3), (gap_b, 1)):
+                for cols, pick in picks:
+                    nc.vector.tensor_tensor(gap[:, cols], pick[i], base[:, cols], ALU.subtract)
+            nc.vector.tensor_tensor(low, gap_c, gap_d, ALU.min)
+            nc.vector.tensor_tensor(high, gap_c, gap_d, ALU.max)
+            nc.vector.scalar_tensor_tensor(lower_middle, gap_b, 0.0, low, ALU.min, ALU.max)
+            nc.vector.scalar_tensor_tensor(upper_middle, gap_b, 0.0, high, ALU.max, ALU.min)
+            terms = (base, base, lower_middle, upper_middle)
+            for total, (c, half, cols) in zip(totals, blocks):
                 for i, term in enumerate(terms):
                     nc.tensor.matmul(
                         total, term[:, cols], identity[:], start=(i == 0), stop=(i == len(terms) - 1), is_transpose=True
@@ -163,26 +168,50 @@ def tile_picked_ytrim_none_po_kernel(
                     scale=0.5,
                 )
 
+        def group_z(half, mover):
+            turned = banks[4 + half][:, 0 : 2 * P].rearrange("p (u v) -> p u v", u=2)
+            for u in range(2):
+                nc.tensor.transpose(turned[:, u, :], z_rows[half][:, u, :].bitcast(F32), identity[:])
+            grouped = sb([P, P * PACK], BF16, "z_grouped%d" % half)
+            mover(grouped[:].bitcast(F32).rearrange("p (v u) -> p v u", u=2), turned.rearrange("p u v -> p v u"))
+            return grouped
+
+        def work_tiles(name, count):
+            return [sb([P, V], F32, "%s%d" % (name, i))[:] for i in range(count)]
+
+        def sums_in(first, second):
+            return [banks[first][:, 0:P], banks[second][:, P : 2 * P]]
+
+        bases, work, middles = work_tiles("base", 4), work_tiles("work", 5), work_tiles("middle", 8)
+        spent = [grouped.bitcast(F32)[:, 0:V] for grouped in w1_grouped]
+        trim([(0, 0, V)], bases[0], [work[0], spent[1], work[2]], [spent[2], work[4]], middles[0:2], sums_in(0, 0))
+        trim([(1, 0, V)], bases[1], [work[0], spent[2], spent[3]], work[1:3], middles[2:4], sums_in(2, 3))
+
+        w2_grouped = sb([P, N * PACK], BF16, "w2_grouped")
+        dealt = w2_grouped[:].rearrange("p (t m j) -> p m j t", t=PACK, j=PACK)
+        source = w2_raw[:].rearrange("p j (m t) -> p m j t", t=PACK)
+        for piece in range(W2_PIECES):
+            part = slice(piece * P // W2_PIECES, (piece + 1) * P // W2_PIECES)
+            nc.scalar.copy(dealt[:, part], source[:, part])
+
+        trim([(2, 0, P), (3, 0, P)], bases[2], [work[0], work[2], work[1]], work[3:5], middles[4:6], sums_in(0, 1))
+        z_grouped = [group_z(0, nc.scalar.copy)]
+        trim([(2, P, P), (3, P, P)], bases[3], [work[0], work[4], work[3]], work[1:3], middles[6:8], sums_in(2, 3))
+        z_grouped.append(group_z(1, nc.vector.tensor_copy))
+
+        w2_codes = sb([P, N], U32, "w2_codes", "work2")
+        w2_plane = sb([P, N], U8, "w2_plane")
+        nc.vector.quantize_mx(w2_codes[:].bitcast(FP8X4), w2_plane[:], w2_grouped[:])
+
         out_codes = sb([P, V], U32, "out_codes")
         out_plane = sb([P, V], U8, "out_plane")
         out_rows = out_0.rearrange("(p t) v -> p t v", t=PACK)
         out_words = out_1[0].rearrange("p n t -> p (n t)").bitcast(I32)
 
-        def second_product(half, w2_codes, w2_plane, mover):
+        def second_product(half, z_codes, mover):
             cols = slice(half * P, (half + 1) * P)
-            turned = banks[4 + half][:, 0 : 2 * P].rearrange("p (u v) -> p u v", u=2)
-            for u in range(2):
-                nc.tensor.transpose(turned[:, u, :], z_rows[half][:, u, :].bitcast(F32), identity[:])
-            z_room = sb([P, P * 2 + P * PACK], BF16, "z_room%d" % half)
-            z_grouped = z_room[:, P * 2 :]
-            mover(
-                z_grouped.bitcast(F32).rearrange("p (v u) -> p v u", u=2),
-                turned.rearrange("p u v -> p v u"),
-            )
-            spent["z_room%d" % half] = z_room[:]
-            z_codes = sb([P, P], U32, "z_codes%d" % half)
             z_plane = sb([P, P], U8, "z_plane%d" % half)
-            nc.vector.quantize_mx(z_codes[:].bitcast(FP8X4), z_plane[:], z_grouped)
+            nc.vector.quantize_mx(z_codes[:].bitcast(FP8X4), z_plane[:], z_grouped[half][:])
             y_acc = banks[6 + half][:].rearrange("p (t v) -> p t v", t=PACK)
             for t in range(PACK):
                 nc.tensor.matmul_mx(
@@ -202,26 +231,8 @@ def tile_picked_ytrim_none_po_kernel(
             nc.vector.quantize_mx(out_codes[:, cols].bitcast(FP8X4), out_plane[:, cols], y_grouped[:])
             nc.sync.dma_start(out_words[:, cols], out_codes[:, cols].bitcast(I32))
 
-        for c in (1, 2, 3):
-            codes, plane = quantise_w1(c)
-            h_tiles.append(first_product(c, codes, plane, 1))
-        trim(0, [(0, 0, V)], {})
-        trim(1, [(1, 0, V)], {"f": "w1_grouped2", "e": "w1_grouped3", "d": "d"})
-
-        w2_grouped = sb([P, N * PACK], BF16, "w2_grouped")
-        dealt = w2_grouped[:].rearrange("p (t m j) -> p m j t", t=PACK, j=PACK)
-        source = w2_raw[:].rearrange("p j (m t) -> p m j t", t=PACK)
-        for piece in range(4):
-            nc.scalar.copy(dealt[:, 32 * piece : 32 * (piece + 1)], source[:, 32 * piece : 32 * (piece + 1)])
-        spent["w2_grouped"] = w2_grouped[:]
-        w2_codes = sb([P, N], U32, "w2_codes")
-        w2_plane = sb([P, N], U8, "w2_plane")
-        nc.vector.quantize_mx(w2_codes[:].bitcast(FP8X4), w2_plane[:], w2_grouped[:])
-
-        trim(2, [(2, 0, P), (3, 0, P)], {"d": "d"})
-        second_product(0, w2_codes, w2_plane, nc.scalar.copy)
-        trim(3, [(2, P, P), (3, P, P)], {"f": "z_room0", "base": "w2_grouped", "d": "d"})
-        second_product(1, w2_codes, w2_plane, nc.vector.tensor_copy)
-        for q in range(4):
+        second_product(0, sb([P, P], U32, "z_codes0", "work0"), nc.scalar.copy)
+        second_product(1, sb([P, P], U32, "z_codes1"), nc.vector.tensor_copy)
+        for q in range(QUADRANTS):
             queue = nc.sync if q % 2 == 0 else nc.scalar
             queue.dma_start(out_2[0][4 * q : 4 * q + 4, :].bitcast(I32), out_plane[32 * q : 32 * q + 4, :].bitcast(I32))

@@ -85,25 +85,27 @@ def tile_picked_ytrim_none_po_kernel(
         nc.vector.tensor_copy(x_codes[0][:], word_tables[0][:].indirect(offs_sb[:]))
         nc.vector.tensor_copy(x_plane[:], scale_table[:].indirect(offs_sb[:]))
 
-        w1_grouped = []
+        arenas = []
 
         def quantise_w1(c):
-            grouped = sb([P, PASSES, P * PACK], BF16, "w1_grouped%d" % c)
+            arena = sb([P, 3 * V], F32, "w1_arena%d" % c)
+            arenas.append([arena[:, i * V : (i + 1) * V] for i in range(3)])
+            flat = arena[:, V // 2 : V // 2 + 2 * V].bitcast(BF16)
+            grouped = flat.rearrange("p (g n) -> p g n", g=PASSES)
             for g in range(PASSES):
                 nc.scalar.activation(
                     grouped[:, g, :].rearrange("p (a i j) -> p a j i", i=LINE, j=PACK),
                     w1_raw[c][g].rearrange("p j (a i) -> p a j i", i=LINE),
                     COPY,
                 )
-            w1_grouped.append(grouped[:].rearrange("p g n -> p (g n)"))
-            codes = sb([P, PASSES * P], U32, "w1_codes%d" % c)
+            codes = sb([P, PASSES * P], U32, "w1_codes%d" % c, "w1_arena1" if c == 3 else None)
             plane = sb([P, PASSES * P], U8, "w1_plane%d" % c)
-            nc.vector.quantize_mx(codes[:].bitcast(FP8X4), plane[:], w1_grouped[c])
+            nc.vector.quantize_mx(codes[:].bitcast(FP8X4), plane[:], flat)
             return codes, plane
 
         def first_product(c, operand, piece_banks, mover):
             codes, plane = operand
-            h = sb([P, S], F32, "h%d" % c)
+            h = sb([P, S], F32, "h%d" % c, "w1_raw2_1" if c == 1 else None)
             width = S // len(piece_banks)
             for piece, bank in enumerate(piece_banks):
                 cols = slice(piece * width, (piece + 1) * width)
@@ -128,78 +130,113 @@ def tile_picked_ytrim_none_po_kernel(
                 word_tables[1][:].indirect(offs_sb[:, piece * width // ENTRIES : (piece + 1) * width // ENTRIES]),
             )
         h_tiles = [first_product(0, first_operand, banks[0:2], nc.vector.tensor_copy)]
-        for c in range(1, H // P):
-            h_tiles.append(first_product(c, quantise_w1(c), [banks[(c + 1) % 2]], nc.scalar.copy))
+        for c in range(1, H // P - 1):
+            h_tiles.append(first_product(c, quantise_w1(c), [banks[(c + 1) % 4]], nc.scalar.copy))
 
         z_rows = [sb([P, 2, H // 2], BF16, "z_rows%d" % half) for half in range(V // P)]
 
-        def trim(runs, base, gaps, pair, middle, totals):
-            blocks = []
-            picks = []
-            at = 0
-            for c, v0, count in runs:
-                columns = slice(v0 // ENTRIES, (v0 + count) // ENTRIES)
-                picks.append((slice(at, at + count), [h_tiles[c][:].indirect(t[:, columns]) for t in pos_sb]))
-                for b in range(count // P):
-                    blocks.append((c, v0 // P + b, slice(at + b * P, at + (b + 1) * P)))
-                at = at + count
-            gap_b, gap_c, gap_d = gaps
-            low, high = pair
-            lower_middle, upper_middle = middle
-            for cols, pick in picks:
-                nc.vector.tensor_copy(base[:, cols], pick[0])
-            for gap, i in ((gap_c, 2), (gap_d, 3), (gap_b, 1)):
-                for cols, pick in picks:
-                    nc.vector.tensor_tensor(gap[:, cols], pick[i], base[:, cols], ALU.subtract)
-            nc.vector.tensor_tensor(low, gap_c, gap_d, ALU.min)
-            nc.vector.tensor_tensor(high, gap_c, gap_d, ALU.max)
-            nc.vector.scalar_tensor_tensor(lower_middle, gap_b, 0.0, low, ALU.min, ALU.max)
-            nc.vector.scalar_tensor_tensor(upper_middle, gap_b, 0.0, high, ALU.max, ALU.min)
-            terms = (base, base, lower_middle, upper_middle)
-            for total, (c, half, cols) in zip(totals, blocks):
-                for i, term in enumerate(terms):
-                    nc.tensor.matmul(
-                        total, term[:, cols], identity[:], start=(i == 0), stop=(i == len(terms) - 1), is_transpose=True
-                    )
-                nc.scalar.activation(
-                    z_rows[half][:, :, 64 * c : 64 * (c + 1)].rearrange("v u (q e) -> v u q e", e=2),
-                    total.rearrange("v (q u e) -> v u q e", u=2, e=2),
-                    COPY,
-                    scale=0.5,
-                )
+        def pick(i, c, v0, count):
+            return h_tiles[c][:].indirect(pos_sb[i][:, v0 // ENTRIES : (v0 + count) // ENTRIES])
 
-        def group_z(half, mover):
-            turned = banks[4 + half][:, 0 : 2 * P].rearrange("p (u v) -> p u v", u=2)
+        def fetch_base(base, c, v0, count):
+            nc.vector.tensor_copy(base, pick(0, c, v0, count))
+
+        def fetch_gap(gap, i, base, c, v0, count):
+            nc.vector.tensor_tensor(gap, pick(i, c, v0, count), base, ALU.subtract)
+
+        def lesser(low, gap_c, gap_d):
+            nc.vector.tensor_tensor(low, gap_c, gap_d, ALU.min)
+
+        def greater(high, gap_c, gap_d):
+            nc.vector.tensor_tensor(high, gap_c, gap_d, ALU.max)
+
+        def lower_middle(out, gap_b, low):
+            nc.vector.scalar_tensor_tensor(out, gap_b, 0.0, low, ALU.min, ALU.max)
+
+        def upper_middle(out, gap_b, high):
+            nc.vector.scalar_tensor_tensor(out, gap_b, 0.0, high, ALU.max, ALU.min)
+
+        def sum_up(total, c, half, base, lower, upper):
+            terms = (base, base, lower, upper)
+            for i, term in enumerate(terms):
+                nc.tensor.matmul(total, term, identity[:], start=(i == 0), stop=(i == len(terms) - 1), is_transpose=True)
+            nc.scalar.activation(
+                z_rows[half][:, :, 64 * c : 64 * (c + 1)].rearrange("v u (q e) -> v u q e", e=2),
+                total.rearrange("v (q u e) -> v u q e", u=2, e=2),
+                COPY,
+                scale=0.5,
+            )
+
+        def group_z(half, bank, mover):
+            turned = bank[:, 0 : 2 * P].rearrange("p (u v) -> p u v", u=2)
             for u in range(2):
                 nc.tensor.transpose(turned[:, u, :], z_rows[half][:, u, :].bitcast(F32), identity[:])
             grouped = sb([P, P * PACK], BF16, "z_grouped%d" % half)
             mover(grouped[:].bitcast(F32).rearrange("p (v u) -> p v u", u=2), turned.rearrange("p u v -> p v u"))
             return grouped
 
-        def work_tiles(name, count):
-            return [sb([P, V], F32, "%s%d" % (name, i))[:] for i in range(count)]
+        def work(name, width=V):
+            return sb([P, width], F32, name)[:]
 
-        def sums_in(first, second):
-            return [banks[first][:, 0:P], banks[second][:, P : 2 * P]]
+        first, second = slice(0, P), slice(P, V)
 
-        bases, work, middles = work_tiles("base", 4), work_tiles("work", 5), work_tiles("middle", 8)
-        spent = [grouped.bitcast(F32)[:, 0:V] for grouped in w1_grouped]
-        trim([(0, 0, V)], bases[0], [work[0], spent[1], work[2]], [spent[2], work[4]], middles[0:2], sums_in(0, 0))
-        trim([(1, 0, V)], bases[1], [work[0], spent[2], spent[3]], work[1:3], middles[2:4], sums_in(2, 3))
+        def unit(c, base, gaps, pair, sum_banks, fetch_next):
+            gap_c, gap_d, gap_b = gaps
+            low, high = pair
+            for gap, i in ((gap_c, 2), (gap_d, 3), (gap_b, 1)):
+                fetch_gap(gap, i, base, c, 0, V)
+            lower, upper = work("lower%d" % c), work("upper%d" % c)
+            lesser(low, gap_c, gap_d)
+            greater(high, gap_c, gap_d)
+            lower_middle(lower, gap_b, low)
+            if fetch_next:
+                fetch_base(gap_c, c + 1, 0, V)
+            upper_middle(upper, gap_b, high)
+            for half, cols in enumerate((first, second)):
+                sum_up(sum_banks[half][:, cols], c, half, base[:, cols], lower[:, cols], upper[:, cols])
 
-        w2_grouped = sb([P, N * PACK], BF16, "w2_grouped")
+        base0 = work("base0")
+        fetch_base(base0, 0, 0, V)
+        unit(0, base0, arenas[1], arenas[2][0:2], [banks[3]] * 2, False)
+        base1 = arenas[2][0]
+        fetch_base(base1, 1, 0, V)
+        h_tiles.append(first_product(3, quantise_w1(3), [banks[0]], nc.scalar.copy))
+        unit(1, base1, arenas[3], [work("low1"), work("high1")], [banks[0]] * 2, True)
+
+        w2_grouped = sb([P, N * PACK], BF16, "w2_grouped", "w1_plane3")
         dealt = w2_grouped[:].rearrange("p (t m j) -> p m j t", t=PACK, j=PACK)
         source = w2_raw[:].rearrange("p j (m t) -> p m j t", t=PACK)
         for piece in range(W2_PIECES):
             part = slice(piece * P // W2_PIECES, (piece + 1) * P // W2_PIECES)
             nc.scalar.copy(dealt[:, part], source[:, part])
 
-        trim([(2, 0, P), (3, 0, P)], bases[2], [work[0], work[2], work[1]], work[3:5], middles[4:6], sums_in(0, 1))
-        z_grouped = [group_z(0, nc.scalar.copy)]
-        trim([(2, P, P), (3, P, P)], bases[3], [work[0], work[4], work[3]], work[1:3], middles[6:8], sums_in(2, 3))
-        z_grouped.append(group_z(1, nc.vector.tensor_copy))
+        gaps2 = [work("gap2_%d" % i) for i in range(3)]
+        unit(2, arenas[3][0], gaps2, [work("low2"), work("high2")], banks[4:6], True)
 
-        w2_codes = sb([P, N], U32, "w2_codes", "work2")
+        base = gaps2[0]
+        gap_c, gap_d, gap_b = work("gap_c3"), work("gap_d3", P), work("gap_b3", P)
+        early = [work("early%d" % i, P) for i in range(4)]
+        late = [work("late%d" % i, P) for i in range(4)]
+
+        def compare(bank, half, cols, gap_c, gap_d, gap_b, tiles):
+            low, high, lower, upper = tiles
+            lesser(low, gap_c, gap_d)
+            greater(high, gap_c, gap_d)
+            lower_middle(lower, gap_b, low)
+            upper_middle(upper, gap_b, high)
+            sum_up(bank[:, 0:P], 3, half, base[:, cols], lower, upper)
+
+        fetch_gap(gap_c, 2, base, 3, 0, V)
+        fetch_gap(gap_d, 3, base[:, first], 3, 0, P)
+        fetch_gap(gap_b, 1, base[:, first], 3, 0, P)
+        compare(banks[6], 0, first, gap_c[:, first], gap_d, gap_b, early)
+        z_grouped = [group_z(0, banks[1], nc.scalar.copy)]
+        fetch_gap(gap_d, 3, base[:, second], 3, P, P)
+        fetch_gap(gap_c[:, first], 1, base[:, second], 3, P, P)
+        compare(banks[7], 1, second, gap_c[:, second], gap_d, gap_c[:, first], late)
+        z_grouped.append(group_z(1, banks[2], nc.vector.tensor_copy))
+
+        w2_codes = sb([P, N], U32, "w2_codes", "late0")
         w2_plane = sb([P, N], U8, "w2_plane")
         nc.vector.quantize_mx(w2_codes[:].bitcast(FP8X4), w2_plane[:], w2_grouped[:])
 
@@ -212,7 +249,7 @@ def tile_picked_ytrim_none_po_kernel(
             cols = slice(half * P, (half + 1) * P)
             z_plane = sb([P, P], U8, "z_plane%d" % half)
             nc.vector.quantize_mx(z_codes[:].bitcast(FP8X4), z_plane[:], z_grouped[half][:])
-            y_acc = banks[6 + half][:].rearrange("p (t v) -> p t v", t=PACK)
+            y_acc = banks[4 + half][:].rearrange("p (t v) -> p t v", t=PACK)
             for t in range(PACK):
                 nc.tensor.matmul_mx(
                     y_acc[:, t, :],
@@ -231,7 +268,7 @@ def tile_picked_ytrim_none_po_kernel(
             nc.vector.quantize_mx(out_codes[:, cols].bitcast(FP8X4), out_plane[:, cols], y_grouped[:])
             nc.sync.dma_start(out_words[:, cols], out_codes[:, cols].bitcast(I32))
 
-        second_product(0, sb([P, P], U32, "z_codes0", "work0"), nc.scalar.copy)
+        second_product(0, sb([P, P], U32, "z_codes0", "late1"), nc.scalar.copy)
         second_product(1, sb([P, P], U32, "z_codes1"), nc.vector.tensor_copy)
         for q in range(QUADRANTS):
             queue = nc.sync if q % 2 == 0 else nc.scalar

@@ -51,12 +51,16 @@ def tile_picked_ytrim_none_po_kernel(
             nc.sync.dma_start(table[:].bitcast(I32), x_words[g].rearrange("p n t -> p (n t)").bitcast(I32))
             return table
 
+        edges = {}
+
         def load_w1(first, count):
             raws = []
             for g in range(PASSES):
-                raw = sb([P, PACK, count * P], F32, "w1_raw%d_%d" % (first, g))
+                padded = sb([P, (PACK * count + 2) * P], F32, "w1_raw%d_%d" % (first, g))
+                edges[first, g] = (padded[:, 0:V], padded[:, PACK * count * P :])
+                raw = padded[:, P : (PACK * count + 1) * P].rearrange("p (j c) -> p j c", j=PACK)
                 rows = w1[g * K_PASS : (g + 1) * K_PASS, first * P : (first + count) * P]
-                nc.sync.dma_start(raw[:], rows.rearrange("(p j) c -> p j c", j=PACK))
+                nc.sync.dma_start(raw, rows.rearrange("(p j) c -> p j c", j=PACK))
                 raws.append(raw)
             return [[raw[:, :, i * P : (i + 1) * P] for raw in raws] for i in range(count)]
 
@@ -87,7 +91,7 @@ def tile_picked_ytrim_none_po_kernel(
 
         arenas = []
 
-        def quantise_w1(c):
+        def regroup_w1(c):
             arena = sb([P, 3 * V], F32, "w1_arena%d" % c)
             arenas.append([arena[:, i * V : (i + 1) * V] for i in range(3)])
             flat = arena[:, V // 2 : V // 2 + 2 * V].bitcast(BF16)
@@ -98,14 +102,17 @@ def tile_picked_ytrim_none_po_kernel(
                     w1_raw[c][g].rearrange("p j (a i) -> p a j i", i=LINE),
                     COPY,
                 )
-            codes = sb([P, PASSES * P], U32, "w1_codes%d" % c, "w1_arena1" if c == 3 else None)
+            return flat
+
+        def quantise_w1(c, flat, in_place_of=None):
+            codes = sb([P, PASSES * P], U32, "w1_codes%d" % c, in_place_of)
             plane = sb([P, PASSES * P], U8, "w1_plane%d" % c)
             nc.vector.quantize_mx(codes[:].bitcast(FP8X4), plane[:], flat)
             return codes, plane
 
         def first_product(c, operand, piece_banks, mover):
             codes, plane = operand
-            h = sb([P, S], F32, "h%d" % c, "w1_raw2_1" if c == 1 else None)
+            h = sb([P, S], F32, "h%d" % c)
             width = S // len(piece_banks)
             for piece, bank in enumerate(piece_banks):
                 cols = slice(piece * width, (piece + 1) * width)
@@ -122,7 +129,7 @@ def tile_picked_ytrim_none_po_kernel(
                 mover(h[:, cols], bank[:, 0:width])
             return h
 
-        first_operand = quantise_w1(0)
+        first_operand = quantise_w1(0, regroup_w1(0))
         for piece in range(2):
             width = S // 2
             nc.vector.tensor_copy(
@@ -130,8 +137,8 @@ def tile_picked_ytrim_none_po_kernel(
                 word_tables[1][:].indirect(offs_sb[:, piece * width // ENTRIES : (piece + 1) * width // ENTRIES]),
             )
         h_tiles = [first_product(0, first_operand, banks[0:2], nc.vector.tensor_copy)]
-        for c in range(1, H // P - 1):
-            h_tiles.append(first_product(c, quantise_w1(c), [banks[(c + 1) % 4]], nc.scalar.copy))
+        h_tiles.append(first_product(1, quantise_w1(1, regroup_w1(1)), [banks[2]], nc.scalar.copy))
+        late_w1 = [regroup_w1(2), regroup_w1(3)]
 
         z_rows = [sb([P, 2, H // 2], BF16, "z_rows%d" % half) for half in range(V // P)]
 
@@ -180,11 +187,9 @@ def tile_picked_ytrim_none_po_kernel(
 
         first, second = slice(0, P), slice(P, V)
 
-        def unit(c, base, gaps, pair, sum_banks, fetch_next):
+        def compare_all(c, gaps, pair, fetch_next):
             gap_c, gap_d, gap_b = gaps
             low, high = pair
-            for gap, i in ((gap_c, 2), (gap_d, 3), (gap_b, 1)):
-                fetch_gap(gap, i, base, c, 0, V)
             lower, upper = work("lower%d" % c), work("upper%d" % c)
             lesser(low, gap_c, gap_d)
             greater(high, gap_c, gap_d)
@@ -192,16 +197,31 @@ def tile_picked_ytrim_none_po_kernel(
             if fetch_next:
                 fetch_base(gap_c, c + 1, 0, V)
             upper_middle(upper, gap_b, high)
-            for half, cols in enumerate((first, second)):
-                sum_up(sum_banks[half][:, cols], c, half, base[:, cols], lower[:, cols], upper[:, cols])
+            return lower, upper
 
-        base0 = work("base0")
+        def sum_all(c, base, middles, sum_banks):
+            for half, cols in enumerate((first, second)):
+                sum_up(sum_banks[half][:, cols], c, half, base[:, cols], middles[0][:, cols], middles[1][:, cols])
+
+        def fetch_gaps(c, base, gaps):
+            for gap, i in zip(gaps, (2, 3, 1)):
+                fetch_gap(gap, i, base, c, 0, V)
+
+        base0, base1 = work("base0"), work("low0")
         fetch_base(base0, 0, 0, V)
-        unit(0, base0, arenas[1], arenas[2][0:2], [banks[3]] * 2, False)
-        base1 = arenas[2][0]
+        gaps0 = [edges[1, 1][0], arenas[1][0], arenas[1][1]]
+        fetch_gaps(0, base0, gaps0)
+        middles0 = compare_all(0, gaps0, [base1, work("high0")], False)
         fetch_base(base1, 1, 0, V)
-        h_tiles.append(first_product(3, quantise_w1(3), [banks[0]], nc.scalar.copy))
-        unit(1, base1, arenas[3], [work("low1"), work("high1")], [banks[0]] * 2, True)
+        h_tiles.append(first_product(2, quantise_w1(2, late_w1[0], "w1_arena1"), [banks[3]], nc.scalar.copy))
+        gaps1 = [edges[2, 1][0], arenas[2][0], arenas[2][1]]
+        fetch_gap(gaps1[0], 2, base1, 1, 0, V)
+        fetch_gap(gaps1[1], 3, base1, 1, 0, V)
+        fetch_gap(gaps1[2], 1, base1, 1, 0, V)
+        h_tiles.append(first_product(3, quantise_w1(3, late_w1[1], "high0"), [banks[0]], nc.scalar.copy))
+        sum_all(0, base0, middles0, [banks[3]] * 2)
+        middles1 = compare_all(1, gaps1, [edges[2, 1][1], arenas[3][0]], True)
+        sum_all(1, base1, middles1, [banks[0]] * 2)
 
         w2_grouped = sb([P, N * PACK], BF16, "w2_grouped", "w1_plane3")
         dealt = w2_grouped[:].rearrange("p (t m j) -> p m j t", t=PACK, j=PACK)
@@ -211,7 +231,8 @@ def tile_picked_ytrim_none_po_kernel(
             nc.scalar.copy(dealt[:, part], source[:, part])
 
         gaps2 = [work("gap2_%d" % i) for i in range(3)]
-        unit(2, arenas[3][0], gaps2, [work("low2"), work("high2")], banks[4:6], True)
+        fetch_gaps(2, gaps1[0], gaps2)
+        sum_all(2, gaps1[0], compare_all(2, gaps2, [work("low2"), work("high2")], True), banks[4:6])
 
         base = gaps2[0]
         gap_c, gap_d, gap_b = work("gap_c3"), work("gap_d3", P), work("gap_b3", P)

@@ -23,6 +23,7 @@ PASSES = K // K_PASS
 QUADRANTS = 4
 ENTRIES = 16
 LINE = 4
+RUN = 16
 BANK = 512
 W2_PIECES = 4
 
@@ -56,13 +57,13 @@ def tile_picked_ytrim_none_po_kernel(
         def load_w1(first, count):
             raws = []
             for g in range(PASSES):
-                padded = sb([P, (PACK * count + 2) * P], F32, "w1_raw%d_%d" % (first, g))
-                edges[first, g] = (padded[:, 0:V], padded[:, PACK * count * P :])
-                raw = padded[:, P : (PACK * count + 1) * P].rearrange("p (j c) -> p j c", j=PACK)
+                padded = sb([P, PACK * count * P + 2 * (V - RUN)], F32, "w1_raw%d_%d" % (first, g))
+                edges[first, g] = (padded[:, 0:V], padded[:, V - RUN + PACK * count * P - RUN :])
+                raw = padded[:, V - RUN : V - RUN + PACK * count * P].rearrange("p (j c) -> p j c", j=PACK)
                 rows = w1[g * K_PASS : (g + 1) * K_PASS, first * P : (first + count) * P]
                 nc.sync.dma_start(raw, rows.rearrange("(p j) c -> p j c", j=PACK))
                 raws.append(raw)
-            return [[raw[:, :, i * P : (i + 1) * P] for raw in raws] for i in range(count)]
+            return raws
 
         word_tables = [load_words(0)]
         for q in range(QUADRANTS):
@@ -70,16 +71,21 @@ def tile_picked_ytrim_none_po_kernel(
                 scale_table[32 * q : 32 * q + 4 * PASSES, :].bitcast(I32),
                 x_scales[:, 4 * q : 4 * q + 4, :].bitcast(I32),
             )
-        w1_raw = load_w1(0, 1)
+        w1_raw = [load_w1(0, 1)]
         word_tables.append(load_words(1))
         pos_sb = []
         for i, pos in enumerate((pos1, pos2, pos3, pos4)):
             list_tile = sb([P, V // ENTRIES], U16, "pos_sb%d" % i)
             nc.sync.dma_start(list_tile[:], pos)
             pos_sb.append(list_tile)
-        w1_raw = w1_raw + load_w1(1, 1) + load_w1(2, 2)
+        w1_raw.append(load_w1(1, 1))
+        wide = [raw.rearrange("p j (b u r) -> p j b u r", u=2, r=RUN) for raw in load_w1(2, 2)]
+        w1_raw = [[raw.rearrange("p j (b r) -> p j b r", r=RUN) for raw in raws] for raws in w1_raw]
+        w1_raw.extend([[raw[:, :, :, u, :] for raw in wide] for u in range(2)])
         w2_raw = sb([P, PACK, N], F32, "w2_raw")
-        nc.sync.dma_start(w2_raw[:], w2.rearrange("(p j) c -> p j c", j=PACK))
+        w2_rows = w2.rearrange("(b u r e) c -> u b r (e c)", u=2, r=8, e=2)
+        for u in range(2):
+            nc.sync.dma_start(w2_raw[:, 2 * u : 2 * u + 2, :].rearrange("p e c -> p (e c)"), w2_rows[u])
 
         identity = sb([P, P], F32, "identity")
         make_identity(nc, identity[:])
@@ -97,10 +103,9 @@ def tile_picked_ytrim_none_po_kernel(
             flat = arena[:, V // 2 : V // 2 + 2 * V].bitcast(BF16)
             grouped = flat.rearrange("p (g n) -> p g n", g=PASSES)
             for g in range(PASSES):
-                nc.scalar.activation(
-                    grouped[:, g, :].rearrange("p (a i j) -> p a j i", i=LINE, j=PACK),
-                    w1_raw[c][g].rearrange("p j (a i) -> p a j i", i=LINE),
-                    COPY,
+                nc.scalar.copy(
+                    grouped[:, g, :].rearrange("p (b a i j) -> p b a j i", a=RUN // LINE, i=LINE, j=PACK),
+                    w1_raw[c][g].rearrange("p j b (a i) -> p b a j i", i=LINE),
                 )
             return flat
 
@@ -140,7 +145,8 @@ def tile_picked_ytrim_none_po_kernel(
         h_tiles.append(first_product(1, quantise_w1(1, regroup_w1(1)), [banks[2]], nc.scalar.copy))
         late_w1 = [regroup_w1(2), regroup_w1(3)]
 
-        z_rows = [sb([P, 2, H // 2], BF16, "z_rows%d" % half) for half in range(V // P)]
+        z_flat = [sb([P, H], BF16, "z_rows%d" % half)[:] for half in range(V // P)]
+        z_rows = [rows.rearrange("v (u n) -> v u n", u=2) for rows in z_flat]
 
         def pick(i, c, v0, count):
             return h_tiles[c][:].indirect(pos_sb[i][:, v0 // ENTRIES : (v0 + count) // ENTRIES])
@@ -167,17 +173,16 @@ def tile_picked_ytrim_none_po_kernel(
             terms = (base, base, lower, upper)
             for i, term in enumerate(terms):
                 nc.tensor.matmul(total, term, identity[:], start=(i == 0), stop=(i == len(terms) - 1), is_transpose=True)
-            nc.scalar.activation(
-                z_rows[half][:, :, 64 * c : 64 * (c + 1)].rearrange("v u (q e) -> v u q e", e=2),
-                total.rearrange("v (q u e) -> v u q e", u=2, e=2),
-                COPY,
-                scale=0.5,
-            )
+            if c < 2:
+                rows = z_rows[half][:, :, 64 * c : 64 * (c + 1)].rearrange("v u (b r) -> v u b r", r=RUN)
+                nc.scalar.activation(rows, total.rearrange("v (b u r) -> v u b r", u=2, r=RUN), COPY, scale=0.5)
+            else:
+                nc.scalar.activation(z_flat[half][:, (c - 2) * H // 2 + P : (c - 1) * H // 2], total, COPY, scale=0.5)
 
         def group_z(half, bank, mover):
             turned = bank[:, 0 : 2 * P].rearrange("p (u v) -> p u v", u=2)
             for u in range(2):
-                nc.tensor.transpose(turned[:, u, :], z_rows[half][:, u, :].bitcast(F32), identity[:])
+                nc.tensor.transpose(turned[:, u, :], z_flat[half][:, u * H // 2 : (u + 1) * H // 2].bitcast(F32), identity[:])
             grouped = sb([P, P * PACK], BF16, "z_grouped%d" % half)
             mover(grouped[:].bitcast(F32).rearrange("p (v u) -> p v u", u=2), turned.rearrange("p u v -> p v u"))
             return grouped
@@ -266,7 +271,7 @@ def tile_picked_ytrim_none_po_kernel(
         out_rows = out_0.rearrange("(p t) v -> p t v", t=PACK)
         out_words = out_1[0].rearrange("p n t -> p (n t)").bitcast(I32)
 
-        def second_product(half, z_codes, mover):
+        def second_product(half, z_codes, mover, pieces):
             cols = slice(half * P, (half + 1) * P)
             z_plane = sb([P, P], U8, "z_plane%d" % half)
             nc.vector.quantize_mx(z_codes[:].bitcast(FP8X4), z_plane[:], z_grouped[half][:])
@@ -284,13 +289,17 @@ def tile_picked_ytrim_none_po_kernel(
             y_grouped = sb([P, P * PACK], BF16, "y_grouped%d" % half)
             mover(y_grouped[:].rearrange("p (v t) -> p v t", t=PACK), y_acc.rearrange("p t v -> p v t"))
             y = sb([P, PACK, P], F32, "y%d" % half)
-            nc.scalar.copy(y[:], y_acc)
-            nc.scalar.dma_start(out_rows[:, :, cols], y[:])
+            step = PACK // pieces
+            for piece in range(pieces):
+                rows = slice(piece * step, (piece + 1) * step)
+                nc.scalar.copy(y[:, rows, :], y_acc[:, rows, :])
+                queue = nc.scalar if piece == pieces - 1 else nc.sync
+                queue.dma_start(out_rows[:, rows, cols], y[:, rows, :])
             nc.vector.quantize_mx(out_codes[:, cols].bitcast(FP8X4), out_plane[:, cols], y_grouped[:])
-            nc.sync.dma_start(out_words[:, cols], out_codes[:, cols].bitcast(I32))
 
-        second_product(0, sb([P, P], U32, "z_codes0", "late1"), nc.scalar.copy)
-        second_product(1, sb([P, P], U32, "z_codes1"), nc.vector.tensor_copy)
+        second_product(0, sb([P, P], U32, "z_codes0", "late1"), nc.scalar.copy, 1)
+        second_product(1, sb([P, P], U32, "z_codes1"), nc.vector.tensor_copy, 2)
+        nc.sync.dma_start(out_words, out_codes[:].bitcast(I32))
         for q in range(QUADRANTS):
-            queue = nc.sync if q % 2 == 0 else nc.scalar
+            queue = nc.scalar if q == QUADRANTS - 1 else nc.sync
             queue.dma_start(out_2[0][4 * q : 4 * q + 4, :].bitcast(I32), out_plane[32 * q : 32 * q + 4, :].bitcast(I32))

@@ -24,6 +24,7 @@ QUADRANTS = 4
 ENTRIES = 16
 LINE = 4
 RUN = 16
+U_WIDTH = H // 2
 BANK = 512
 W2_PIECES = 4
 
@@ -54,13 +55,14 @@ def tile_picked_ytrim_none_po_kernel(
 
         edges = {}
 
-        def load_w1(first, count):
+        def load_w1(chunk, count):
             raws = []
             for g in range(PASSES):
-                padded = sb([P, PACK * count * P + 2 * (V - RUN)], F32, "w1_raw%d_%d" % (first, g))
-                edges[first, g] = (padded[:, 0:V], padded[:, V - RUN + PACK * count * P - RUN :])
-                raw = padded[:, V - RUN : V - RUN + PACK * count * P].rearrange("p (j c) -> p j c", j=PACK)
-                rows = w1[g * K_PASS : (g + 1) * K_PASS, first * P : (first + count) * P]
+                loaded, spare = PACK * count * P, V - RUN
+                padded = sb([P, loaded + 2 * spare], F32, "w1_raw%d_%d" % (chunk, g))
+                edges[chunk, g] = (padded[:, 0:V], padded[:, spare + loaded - RUN :])
+                raw = padded[:, spare : spare + loaded].rearrange("p (j c) -> p j c", j=PACK)
+                rows = w1[g * K_PASS : (g + 1) * K_PASS, chunk * P : (chunk + count) * P]
                 nc.sync.dma_start(raw, rows.rearrange("(p j) c -> p j c", j=PACK))
                 raws.append(raw)
             return raws
@@ -95,12 +97,12 @@ def tile_picked_ytrim_none_po_kernel(
         nc.vector.tensor_copy(x_codes[0][:], word_tables[0][:].indirect(offs_sb[:]))
         nc.vector.tensor_copy(x_plane[:], scale_table[:].indirect(offs_sb[:]))
 
-        arenas = []
+        spent = []
 
         def regroup_w1(c):
-            arena = sb([P, 3 * V], F32, "w1_arena%d" % c)
-            arenas.append([arena[:, i * V : (i + 1) * V] for i in range(3)])
-            flat = arena[:, V // 2 : V // 2 + 2 * V].bitcast(BF16)
+            as_f32 = sb([P, 2 * V], F32, "w1_grouped%d" % c)
+            spent.append([as_f32[:, 0:V], as_f32[:, V : 2 * V]])
+            flat = as_f32[:].bitcast(BF16)
             grouped = flat.rearrange("p (g n) -> p g n", g=PASSES)
             for g in range(PASSES):
                 nc.scalar.copy(
@@ -134,15 +136,15 @@ def tile_picked_ytrim_none_po_kernel(
                 mover(h[:, cols], bank[:, 0:width])
             return h
 
-        first_operand = quantise_w1(0, regroup_w1(0))
+        operand0 = quantise_w1(0, regroup_w1(0))
         for piece in range(2):
             width = S // 2
             nc.vector.tensor_copy(
                 x_codes[1][:, piece * width : (piece + 1) * width],
                 word_tables[1][:].indirect(offs_sb[:, piece * width // ENTRIES : (piece + 1) * width // ENTRIES]),
             )
-        h_tiles = [first_product(0, first_operand, banks[0:2], nc.vector.tensor_copy)]
-        h_tiles.append(first_product(1, quantise_w1(1, regroup_w1(1)), [banks[2]], nc.scalar.copy))
+        h_tiles = [first_product(0, operand0, banks[0:2], nc.vector.tensor_copy)]
+        h_tiles.append(first_product(1, quantise_w1(1, regroup_w1(1)), [banks[2], banks[4]], nc.scalar.copy))
         late_w1 = [regroup_w1(2), regroup_w1(3)]
 
         z_flat = [sb([P, H], BF16, "z_rows%d" % half)[:] for half in range(V // P)]
@@ -151,8 +153,8 @@ def tile_picked_ytrim_none_po_kernel(
         def pick(i, c, v0, count):
             return h_tiles[c][:].indirect(pos_sb[i][:, v0 // ENTRIES : (v0 + count) // ENTRIES])
 
-        def fetch_base(base, c, v0, count):
-            nc.vector.tensor_copy(base, pick(0, c, v0, count))
+        def fetch_base(base, c):
+            nc.vector.tensor_copy(base, pick(0, c, 0, V))
 
         def fetch_gap(gap, i, base, c, v0, count):
             nc.vector.tensor_tensor(gap, pick(i, c, v0, count), base, ALU.subtract)
@@ -174,15 +176,17 @@ def tile_picked_ytrim_none_po_kernel(
             for i, term in enumerate(terms):
                 nc.tensor.matmul(total, term, identity[:], start=(i == 0), stop=(i == len(terms) - 1), is_transpose=True)
             if c < 2:
-                rows = z_rows[half][:, :, 64 * c : 64 * (c + 1)].rearrange("v u (b r) -> v u b r", r=RUN)
+                rows = z_rows[half][:, :, 4 * RUN * c : 4 * RUN * (c + 1)].rearrange("v u (b r) -> v u b r", r=RUN)
                 nc.scalar.activation(rows, total.rearrange("v (b u r) -> v u b r", u=2, r=RUN), COPY, scale=0.5)
             else:
-                nc.scalar.activation(z_flat[half][:, (c - 2) * H // 2 + P : (c - 1) * H // 2], total, COPY, scale=0.5)
+                rows = z_flat[half][:, (c - 2) * U_WIDTH + U_WIDTH // 2 : (c - 1) * U_WIDTH]
+                nc.scalar.activation(rows, total, COPY, scale=0.5)
 
         def group_z(half, bank, mover):
             turned = bank[:, 0 : 2 * P].rearrange("p (u v) -> p u v", u=2)
             for u in range(2):
-                nc.tensor.transpose(turned[:, u, :], z_flat[half][:, u * H // 2 : (u + 1) * H // 2].bitcast(F32), identity[:])
+                words = z_flat[half][:, u * U_WIDTH : (u + 1) * U_WIDTH].bitcast(F32)
+                nc.tensor.transpose(turned[:, u, :], words, identity[:])
             grouped = sb([P, P * PACK], BF16, "z_grouped%d" % half)
             mover(grouped[:].bitcast(F32).rearrange("p (v u) -> p v u", u=2), turned.rearrange("p u v -> p v u"))
             return grouped
@@ -200,7 +204,7 @@ def tile_picked_ytrim_none_po_kernel(
             greater(high, gap_c, gap_d)
             lower_middle(lower, gap_b, low)
             if fetch_next:
-                fetch_base(gap_c, c + 1, 0, V)
+                fetch_base(gap_c, c + 1)
             upper_middle(upper, gap_b, high)
             return lower, upper
 
@@ -213,19 +217,18 @@ def tile_picked_ytrim_none_po_kernel(
                 fetch_gap(gap, i, base, c, 0, V)
 
         base0, base1 = work("base0"), work("low0")
-        fetch_base(base0, 0, 0, V)
-        gaps0 = [edges[1, 1][0], arenas[1][0], arenas[1][1]]
+        fetch_base(base0, 0)
+        gaps0 = [edges[1, 1][0], spent[1][0], spent[1][1]]
         fetch_gaps(0, base0, gaps0)
         middles0 = compare_all(0, gaps0, [base1, work("high0")], False)
-        fetch_base(base1, 1, 0, V)
-        h_tiles.append(first_product(2, quantise_w1(2, late_w1[0], "w1_arena1"), [banks[3]], nc.scalar.copy))
-        gaps1 = [edges[2, 1][0], arenas[2][0], arenas[2][1]]
-        fetch_gap(gaps1[0], 2, base1, 1, 0, V)
-        fetch_gap(gaps1[1], 3, base1, 1, 0, V)
-        fetch_gap(gaps1[2], 1, base1, 1, 0, V)
+
+        fetch_base(base1, 1)
+        h_tiles.append(first_product(2, quantise_w1(2, late_w1[0], "w1_grouped1"), [banks[3]], nc.scalar.copy))
+        gaps1 = [edges[2, 1][0], spent[2][0], spent[2][1]]
+        fetch_gaps(1, base1, gaps1)
         h_tiles.append(first_product(3, quantise_w1(3, late_w1[1], "high0"), [banks[0]], nc.scalar.copy))
         sum_all(0, base0, middles0, [banks[3]] * 2)
-        middles1 = compare_all(1, gaps1, [edges[2, 1][1], arenas[3][0]], True)
+        middles1 = compare_all(1, gaps1, [edges[2, 1][1], spent[3][0]], True)
         sum_all(1, base1, middles1, [banks[0]] * 2)
 
         w2_grouped = sb([P, N * PACK], BF16, "w2_grouped", "w1_plane3")
@@ -235,31 +238,30 @@ def tile_picked_ytrim_none_po_kernel(
             part = slice(piece * P // W2_PIECES, (piece + 1) * P // W2_PIECES)
             nc.scalar.copy(dealt[:, part], source[:, part])
 
+        base2 = gaps1[0]
         gaps2 = [work("gap2_%d" % i) for i in range(3)]
-        fetch_gaps(2, gaps1[0], gaps2)
-        sum_all(2, gaps1[0], compare_all(2, gaps2, [work("low2"), work("high2")], True), banks[4:6])
+        fetch_gaps(2, base2, gaps2)
+        sum_all(2, base2, compare_all(2, gaps2, [work("low2"), work("high2")], True), banks[4:6])
 
-        base = gaps2[0]
-        gap_c, gap_d, gap_b = work("gap_c3"), work("gap_d3", P), work("gap_b3", P)
+        base3 = gaps2[0]
+        gap_c3, gap_d3, gap_b3 = work("gap_c3", P), work("gap_d3", P), work("gap_b3", P)
         early = [work("early%d" % i, P) for i in range(4)]
         late = [work("late%d" % i, P) for i in range(4)]
 
-        def compare(bank, half, cols, gap_c, gap_d, gap_b, tiles):
+        def finish_half(half, gap_b, tiles, bank):
+            cols = (first, second)[half]
             low, high, lower, upper = tiles
-            lesser(low, gap_c, gap_d)
-            greater(high, gap_c, gap_d)
+            for gap, i in ((gap_c3, 2), (gap_d3, 3), (gap_b, 1)):
+                fetch_gap(gap, i, base3[:, cols], 3, half * P, P)
+            lesser(low, gap_c3, gap_d3)
+            greater(high, gap_c3, gap_d3)
             lower_middle(lower, gap_b, low)
             upper_middle(upper, gap_b, high)
-            sum_up(bank[:, 0:P], 3, half, base[:, cols], lower, upper)
+            sum_up(bank[:, 0:P], 3, half, base3[:, cols], lower, upper)
 
-        fetch_gap(gap_c, 2, base, 3, 0, V)
-        fetch_gap(gap_d, 3, base[:, first], 3, 0, P)
-        fetch_gap(gap_b, 1, base[:, first], 3, 0, P)
-        compare(banks[6], 0, first, gap_c[:, first], gap_d, gap_b, early)
+        finish_half(0, gap_b3, early, banks[6])
         z_grouped = [group_z(0, banks[1], nc.scalar.copy)]
-        fetch_gap(gap_d, 3, base[:, second], 3, P, P)
-        fetch_gap(gap_c[:, first], 1, base[:, second], 3, P, P)
-        compare(banks[7], 1, second, gap_c[:, second], gap_d, gap_c[:, first], late)
+        finish_half(1, early[0], late, banks[7])
         z_grouped.append(group_z(1, banks[2], nc.vector.tensor_copy))
 
         w2_codes = sb([P, N], U32, "w2_codes", "late0")
@@ -271,14 +273,18 @@ def tile_picked_ytrim_none_po_kernel(
         out_rows = out_0.rearrange("(p t) v -> p t v", t=PACK)
         out_words = out_1[0].rearrange("p n t -> p (n t)").bitcast(I32)
 
-        def second_product(half, z_codes, mover, pieces):
-            cols = slice(half * P, (half + 1) * P)
-            z_plane = sb([P, P], U8, "z_plane%d" % half)
-            nc.vector.quantize_mx(z_codes[:].bitcast(FP8X4), z_plane[:], z_grouped[half][:])
-            y_acc = banks[4 + half][:].rearrange("p (t v) -> p t v", t=PACK)
-            for t in range(PACK):
+        def quantise_z(half, in_place_of=None):
+            codes = sb([P, P], U32, "z_codes%d" % half, in_place_of)
+            plane = sb([P, P], U8, "z_plane%d" % half)
+            nc.vector.quantize_mx(codes[:].bitcast(FP8X4), plane[:], z_grouped[half][:])
+            return codes, plane
+
+        def second_product(operand, bank, count):
+            z_codes, z_plane = operand
+            acc = bank[:].rearrange("p (t v) -> p t v", t=PACK)
+            for t in range(count):
                 nc.tensor.matmul_mx(
-                    y_acc[:, t, :],
+                    acc[:, t, :],
                     lhsT=w2_codes[:, t * P : (t + 1) * P].bitcast(FP8X4),
                     lhsT_scale=w2_plane[:, t * P : (t + 1) * P],
                     rhs=z_codes[:].bitcast(FP8X4),
@@ -286,19 +292,34 @@ def tile_picked_ytrim_none_po_kernel(
                     start=True,
                     stop=True,
                 )
-            y_grouped = sb([P, P * PACK], BF16, "y_grouped%d" % half)
-            mover(y_grouped[:].rearrange("p (v t) -> p v t", t=PACK), y_acc.rearrange("p t v -> p v t"))
-            y = sb([P, PACK, P], F32, "y%d" % half)
-            step = PACK // pieces
-            for piece in range(pieces):
-                rows = slice(piece * step, (piece + 1) * step)
-                nc.scalar.copy(y[:, rows, :], y_acc[:, rows, :])
-                queue = nc.scalar if piece == pieces - 1 else nc.sync
-                queue.dma_start(out_rows[:, rows, cols], y[:, rows, :])
-            nc.vector.quantize_mx(out_codes[:, cols].bitcast(FP8X4), out_plane[:, cols], y_grouped[:])
+            return acc
 
-        second_product(0, sb([P, P], U32, "z_codes0", "late1"), nc.scalar.copy, 1)
-        second_product(1, sb([P, P], U32, "z_codes1"), nc.vector.tensor_copy, 2)
+        def group_y(half, acc, mover):
+            grouped = sb([P, P * PACK], BF16, "y_grouped%d" % half)
+            mover(grouped[:].rearrange("p (v t) -> p v t", t=PACK), acc.rearrange("p t v -> p v t"))
+            return grouped
+
+        def store_y(half, y, acc, rows, queue):
+            nc.scalar.copy(y[:, rows, :], acc[:, rows, :])
+            queue.dma_start(out_rows[:, rows, (first, second)[half]], y[:, rows, :])
+
+        def quantise_y(half, grouped):
+            cols = (first, second)[half]
+            nc.vector.quantize_mx(out_codes[:, cols].bitcast(FP8X4), out_plane[:, cols], grouped[:])
+
+        acc = second_product(quantise_z(0, "late1"), banks[4], PACK)
+        grouped = group_y(0, acc, nc.scalar.copy)
+        store_y(0, sb([P, PACK, P], F32, "y0"), acc, slice(0, PACK), nc.sync)
+        quantise_y(0, grouped)
+
+        operand = quantise_z(1)
+        acc = second_product(operand, banks[5], PACK)
+        grouped = group_y(1, acc, nc.vector.tensor_copy)
+        y = sb([P, PACK, P], F32, "y1")
+        store_y(1, y, second_product(operand, banks[6], 2), slice(0, 2), nc.sync)
+        store_y(1, y, acc, slice(2, PACK), nc.scalar)
+        quantise_y(1, grouped)
+
         nc.sync.dma_start(out_words, out_codes[:].bitcast(I32))
         for q in range(QUADRANTS):
             queue = nc.scalar if q == QUADRANTS - 1 else nc.sync

@@ -120,9 +120,10 @@ def tile_picked_ytrim_none_po_kernel(
         def first_product(c, operand, piece_banks, mover):
             codes, plane = operand
             h = sb([P, S], F32, "h%d" % c)
-            width = S // len(piece_banks)
-            for piece, bank in enumerate(piece_banks):
-                cols = slice(piece * width, (piece + 1) * width)
+            start = 0
+            for bank, width in piece_banks:
+                cols = slice(start, start + width)
+                start = start + width
                 for g in range(PASSES):
                     nc.tensor.matmul_mx(
                         bank[:, 0:width],
@@ -143,8 +144,8 @@ def tile_picked_ytrim_none_po_kernel(
                 x_codes[1][:, piece * width : (piece + 1) * width],
                 word_tables[1][:].indirect(offs_sb[:, piece * width // ENTRIES : (piece + 1) * width // ENTRIES]),
             )
-        h_tiles = [first_product(0, operand0, banks[0:2], nc.vector.tensor_copy)]
-        h_tiles.append(first_product(1, quantise_w1(1, regroup_w1(1)), [banks[2], banks[4]], nc.scalar.copy))
+        h_tiles = [first_product(0, operand0, [(banks[0], 2 * P), (banks[1], P), (banks[7], P)], nc.vector.tensor_copy)]
+        h_tiles.append(first_product(1, quantise_w1(1, regroup_w1(1)), [(banks[2], 2 * P), (banks[4], 2 * P)], nc.scalar.copy))
         late_w1 = [regroup_w1(2), regroup_w1(3)]
 
         z_flat = [sb([P, H], BF16, "z_rows%d" % half)[:] for half in range(V // P)]
@@ -223,10 +224,10 @@ def tile_picked_ytrim_none_po_kernel(
         middles0 = compare_all(0, gaps0, [base1, work("high0")], False)
 
         fetch_base(base1, 1)
-        h_tiles.append(first_product(2, quantise_w1(2, late_w1[0], "w1_grouped1"), [banks[3]], nc.scalar.copy))
+        h_tiles.append(first_product(2, quantise_w1(2, late_w1[0], "w1_grouped1"), [(banks[3], S)], nc.scalar.copy))
         gaps1 = [edges[2, 1][0], spent[2][0], spent[2][1]]
         fetch_gaps(1, base1, gaps1)
-        h_tiles.append(first_product(3, quantise_w1(3, late_w1[1], "high0"), [banks[0]], nc.scalar.copy))
+        h_tiles.append(first_product(3, quantise_w1(3, late_w1[1], "high0"), [(banks[0], S)], nc.scalar.copy))
         sum_all(0, base0, middles0, [banks[3]] * 2)
         middles1 = compare_all(1, gaps1, [edges[2, 1][1], spent[3][0]], True)
         sum_all(1, base1, middles1, [banks[0]] * 2)
@@ -262,7 +263,7 @@ def tile_picked_ytrim_none_po_kernel(
         finish_half(0, gap_b3, early, banks[6])
         z_grouped = [group_z(0, banks[1], nc.scalar.copy)]
         finish_half(1, early[0], late, banks[7])
-        z_grouped.append(group_z(1, banks[2], nc.vector.tensor_copy))
+        z_grouped.append(group_z(1, banks[2], nc.scalar.copy))
 
         w2_codes = sb([P, N], U32, "w2_codes", "late0")
         w2_plane = sb([P, N], U8, "w2_plane")
@@ -308,9 +309,8 @@ def tile_picked_ytrim_none_po_kernel(
             nc.vector.quantize_mx(out_codes[:, cols].bitcast(FP8X4), out_plane[:, cols], grouped[:])
 
         acc = second_product(quantise_z(0, "late1"), banks[4], PACK)
-        grouped = group_y(0, acc, nc.scalar.copy)
         store_y(0, sb([P, PACK, P], F32, "y0"), acc, slice(0, PACK), nc.sync)
-        quantise_y(0, grouped)
+        quantise_y(0, group_y(0, acc, nc.scalar.copy))
 
         operand = quantise_z(1)
         acc = second_product(operand, banks[5], PACK)

@@ -38,7 +38,7 @@ def tile_picked_ytrim_none_po_kernel(
         psum = ctx.enter_context(tc.psum_pool(name="psum", bufs=1))
 
         def sb(shape, dtype, name, in_place_of=None):
-            return keep.tile(shape, dtype, name=name, tag=in_place_of or name, align_bytes=64)
+            return keep.tile(shape, dtype, name=name, tag=in_place_of or name, align_bytes=256)
 
         banks = [psum.tile([P, BANK], F32, name="bank%d" % i) for i in range(8)]
 
@@ -58,10 +58,10 @@ def tile_picked_ytrim_none_po_kernel(
         def load_w1(chunk, count):
             raws = []
             for g in range(PASSES):
-                loaded, spare = PACK * count * P, V - RUN
-                padded = sb([P, loaded + 2 * spare], F32, "w1_raw%d_%d" % (chunk, g))
-                edges[chunk, g] = (padded[:, 0:V], padded[:, spare + loaded - RUN :])
-                raw = padded[:, spare : spare + loaded].rearrange("p (j c) -> p j c", j=PACK)
+                loaded = PACK * count * P
+                padded = sb([P, loaded + 2 * V], F32, "w1_raw%d_%d" % (chunk, g))
+                edges[chunk, g] = (padded[:, RUN : RUN + V], padded[:, V + loaded - RUN : 2 * V + loaded - RUN])
+                raw = padded[:, V : V + loaded].rearrange("p (j c) -> p j c", j=PACK)
                 rows = w1[g * K_PASS : (g + 1) * K_PASS, chunk * P : (chunk + count) * P]
                 nc.sync.dma_start(raw, rows.rearrange("(p j) c -> p j c", j=PACK))
                 raws.append(raw)
@@ -117,11 +117,11 @@ def tile_picked_ytrim_none_po_kernel(
             nc.vector.quantize_mx(codes[:].bitcast(FP8X4), plane[:], flat)
             return codes, plane
 
-        def first_product(c, operand, piece_banks, mover):
+        def first_product(c, operand, pieces, mover):
             codes, plane = operand
             h = sb([P, S], F32, "h%d" % c)
             start = 0
-            for bank, width in piece_banks:
+            for bank, width in pieces:
                 cols = slice(start, start + width)
                 start = start + width
                 for g in range(PASSES):
@@ -144,8 +144,10 @@ def tile_picked_ytrim_none_po_kernel(
                 x_codes[1][:, piece * width : (piece + 1) * width],
                 word_tables[1][:].indirect(offs_sb[:, piece * width // ENTRIES : (piece + 1) * width // ENTRIES]),
             )
-        h_tiles = [first_product(0, operand0, [(banks[0], 2 * P), (banks[1], P), (banks[7], P)], nc.vector.tensor_copy)]
-        h_tiles.append(first_product(1, quantise_w1(1, regroup_w1(1)), [(banks[2], 2 * P), (banks[4], 2 * P)], nc.scalar.copy))
+        pieces0 = [(banks[0], S // 2), (banks[1], S // 4), (banks[7], S // 4)]
+        h_tiles = [first_product(0, operand0, pieces0, nc.vector.tensor_copy)]
+        pieces1 = [(banks[2], S // 2), (banks[4], S // 2)]
+        h_tiles.append(first_product(1, quantise_w1(1, regroup_w1(1)), pieces1, nc.scalar.copy))
         late_w1 = [regroup_w1(2), regroup_w1(3)]
 
         z_flat = [sb([P, H], BF16, "z_rows%d" % half)[:] for half in range(V // P)]
@@ -183,13 +185,13 @@ def tile_picked_ytrim_none_po_kernel(
                 rows = z_flat[half][:, (c - 2) * U_WIDTH + U_WIDTH // 2 : (c - 1) * U_WIDTH]
                 nc.scalar.activation(rows, total, COPY, scale=0.5)
 
-        def group_z(half, bank, mover):
+        def group_z(half, bank):
             turned = bank[:, 0 : 2 * P].rearrange("p (u v) -> p u v", u=2)
             for u in range(2):
                 words = z_flat[half][:, u * U_WIDTH : (u + 1) * U_WIDTH].bitcast(F32)
                 nc.tensor.transpose(turned[:, u, :], words, identity[:])
             grouped = sb([P, P * PACK], BF16, "z_grouped%d" % half)
-            mover(grouped[:].bitcast(F32).rearrange("p (v u) -> p v u", u=2), turned.rearrange("p u v -> p v u"))
+            nc.scalar.copy(grouped[:].bitcast(F32).rearrange("p (v u) -> p v u", u=2), turned.rearrange("p u v -> p v u"))
             return grouped
 
         def work(name, width=V):
@@ -224,7 +226,8 @@ def tile_picked_ytrim_none_po_kernel(
         middles0 = compare_all(0, gaps0, [base1, work("high0")], False)
 
         fetch_base(base1, 1)
-        h_tiles.append(first_product(2, quantise_w1(2, late_w1[0], "w1_grouped1"), [(banks[3], S)], nc.scalar.copy))
+        operand2 = quantise_w1(2, late_w1[0], "w1_grouped1")
+        h_tiles.append(first_product(2, operand2, [(banks[3], S)], nc.scalar.copy))
         gaps1 = [edges[2, 1][0], spent[2][0], spent[2][1]]
         fetch_gaps(1, base1, gaps1)
         h_tiles.append(first_product(3, quantise_w1(3, late_w1[1], "high0"), [(banks[0], S)], nc.scalar.copy))
@@ -261,9 +264,9 @@ def tile_picked_ytrim_none_po_kernel(
             sum_up(bank[:, 0:P], 3, half, base3[:, cols], lower, upper)
 
         finish_half(0, gap_b3, early, banks[6])
-        z_grouped = [group_z(0, banks[1], nc.scalar.copy)]
+        z_grouped = [group_z(0, banks[1])]
         finish_half(1, early[0], late, banks[7])
-        z_grouped.append(group_z(1, banks[2], nc.scalar.copy))
+        z_grouped.append(group_z(1, banks[2]))
 
         w2_codes = sb([P, N], U32, "w2_codes", "late0")
         w2_plane = sb([P, N], U8, "w2_plane")

@@ -23,6 +23,7 @@ PASSES = K // K_PASS
 QUADRANTS = 4
 ENTRIES = 16
 LINE = 4
+SPREAD = 8
 RUN = 16
 U_WIDTH = H // 2
 BANK = 512
@@ -45,8 +46,14 @@ def tile_picked_ytrim_none_po_kernel(
         offs_sb = sb([P, S // ENTRIES], U16, "offs_sb")
         nc.sync.dma_start(offs_sb[:], offs)
 
-        scale_table = sb([P, T], U8, "scale_table")
-        nc.vector.memset(scale_table[:].bitcast(I32), 0)
+        scale_tables = []
+        for g in range(PASSES):
+            table = sb([P, T], U8, "scale_table%d" % g)
+            nc.vector.memset(table[:].bitcast(I32), 0)
+            scale_tables.append(table)
+
+        x_plane = sb([P, PASSES * S], U8, "x_plane")
+        nc.vector.memset(x_plane[:].bitcast(I32), 0)
 
         def load_words(g):
             table = sb([P, T], U32, "word_table%d" % g)
@@ -55,11 +62,11 @@ def tile_picked_ytrim_none_po_kernel(
 
         edges = {}
 
-        def load_w1(chunk, count):
+        def load_w1(chunk, count, in_place_of=(None, None), passes=range(PASSES)):
             raws = []
-            for g in range(PASSES):
+            for g in passes:
                 loaded = PACK * count * P
-                padded = sb([P, loaded + 2 * V], F32, "w1_raw%d_%d" % (chunk, g))
+                padded = sb([P, loaded + 2 * V], F32, "w1_raw%d_%d" % (chunk, g), in_place_of[g])
                 edges[chunk, g] = (padded[:, RUN : RUN + V], padded[:, V + loaded - RUN : 2 * V + loaded - RUN])
                 raw = padded[:, V : V + loaded].rearrange("p (j c) -> p j c", j=PACK)
                 rows = w1[g * K_PASS : (g + 1) * K_PASS, chunk * P : (chunk + count) * P]
@@ -67,35 +74,31 @@ def tile_picked_ytrim_none_po_kernel(
                 raws.append(raw)
             return raws
 
-        word_tables = [load_words(0)]
-        for q in range(QUADRANTS):
-            nc.sync.dma_start(
-                scale_table[32 * q : 32 * q + 4 * PASSES, :].bitcast(I32),
-                x_scales[:, 4 * q : 4 * q + 4, :].bitcast(I32),
-            )
-        w1_raw = [load_w1(0, 1)]
-        word_tables.append(load_words(1))
-        pos_sb = []
-        for i, pos in enumerate((pos1, pos2, pos3, pos4)):
+        def load_list(i, pos):
             list_tile = sb([P, V // ENTRIES], U16, "pos_sb%d" % i)
             nc.sync.dma_start(list_tile[:], pos)
-            pos_sb.append(list_tile)
-        w1_raw.append(load_w1(1, 1))
-        wide = [raw.rearrange("p j (b u r) -> p j b u r", u=2, r=RUN) for raw in load_w1(2, 2)]
-        w1_raw = [[raw.rearrange("p j (b r) -> p j b r", r=RUN) for raw in raws] for raws in w1_raw]
-        w1_raw.extend([[raw[:, :, :, u, :] for raw in wide] for u in range(2)])
-        w2_raw = sb([P, PACK, N], F32, "w2_raw")
-        w2_rows = w2.rearrange("(b u r e) c -> u b r (e c)", u=2, r=8, e=2)
-        for u in range(2):
-            nc.sync.dma_start(w2_raw[:, 2 * u : 2 * u + 2, :].rearrange("p e c -> p (e c)"), w2_rows[u])
+            return list_tile
+
+        def by_runs(raws):
+            return [raw.rearrange("p j (b r) -> p j b r", r=RUN) for raw in raws]
+
+        first_raws = load_w1(0, 1, passes=[0])
+        for g in range(PASSES):
+            nc.sync.dma_start(scale_tables[g][0:P:SPREAD, :].bitcast(I32), x_scales[g].bitcast(I32))
+        word_tables = [load_words(0)]
+        w1_raw = [by_runs(first_raws + load_w1(0, 1, passes=[1]))]
+        word_tables.append(load_words(1))
 
         identity = sb([P, P], F32, "identity")
         make_identity(nc, identity[:])
 
         x_codes = [sb([P, S], U32, "x_codes%d" % g) for g in range(PASSES)]
-        x_plane = sb([P, S], U8, "x_plane")
+        x_spread = sb([P, PASSES * S], U8, "x_spread")
+        for g in range(PASSES):
+            nc.vector.tensor_copy(x_spread[:, g * S : (g + 1) * S], scale_tables[g][:].indirect(offs_sb[:]))
+        for r in range(4):
+            nc.scalar.dma_start(x_plane[r:P:32, :].bitcast(I32), x_spread[SPREAD * r : P : 32, :].bitcast(I32))
         nc.vector.tensor_copy(x_codes[0][:], word_tables[0][:].indirect(offs_sb[:]))
-        nc.vector.tensor_copy(x_plane[:], scale_table[:].indirect(offs_sb[:]))
 
         spent = []
 
@@ -130,7 +133,7 @@ def tile_picked_ytrim_none_po_kernel(
                         lhsT=codes[:, g * P : (g + 1) * P].bitcast(FP8X4),
                         lhsT_scale=plane[:, g * P : (g + 1) * P],
                         rhs=x_codes[g][:, cols].bitcast(FP8X4),
-                        rhs_scale=x_plane[4 * g : P, cols],
+                        rhs_scale=x_plane[:, g * S + cols.start : g * S + cols.stop],
                         start=(g == 0),
                         stop=(g == PASSES - 1),
                     )
@@ -138,14 +141,26 @@ def tile_picked_ytrim_none_po_kernel(
             return h
 
         operand0 = quantise_w1(0, regroup_w1(0))
+
+        w1_raw.append(by_runs(load_w1(1, 1, ("word_table0", "w1_raw0_1"))))
+        lists = (pos1, pos2, pos3, pos4)
+        loaded_lists = {i: load_list(i, lists[i]) for i in (0, 2, 3, 1)}
+        pos_sb = [loaded_lists[i] for i in range(4)]
         for piece in range(2):
             width = S // 2
             nc.vector.tensor_copy(
                 x_codes[1][:, piece * width : (piece + 1) * width],
                 word_tables[1][:].indirect(offs_sb[:, piece * width // ENTRIES : (piece + 1) * width // ENTRIES]),
             )
+        wide = load_w1(2, 2, ("w1_grouped0", "word_table1"))
+        wide = [raw.rearrange("p j (b u r) -> p j b u r", u=2, r=RUN) for raw in wide]
+        w1_raw.extend([[raw[:, :, :, u, :] for raw in wide] for u in range(2)])
         pieces0 = [(banks[0], S // 2), (banks[1], S // 4), (banks[7], S // 4)]
         h_tiles = [first_product(0, operand0, pieces0, nc.vector.tensor_copy)]
+        w2_raw = sb([P, PACK, N], F32, "w2_raw", "w1_codes0")
+        w2_rows = w2.rearrange("(b u r e) c -> u b r (e c)", u=2, r=8, e=2)
+        for u in range(2):
+            nc.sync.dma_start(w2_raw[:, 2 * u : 2 * u + 2, :].rearrange("p e c -> p (e c)"), w2_rows[u])
         pieces1 = [(banks[2], S // 2), (banks[4], S // 2)]
         h_tiles.append(first_product(1, quantise_w1(1, regroup_w1(1)), pieces1, nc.scalar.copy))
         late_w1 = [regroup_w1(2), regroup_w1(3)]

@@ -43,8 +43,6 @@ def tile_picked_ytrim_none_po_kernel(
 
         banks = [psum.tile([P, BANK], F32, name="bank%d" % i) for i in range(8)]
 
-        offs_sb = sb([P, S // ENTRIES], U16, "offs_sb")
-        nc.sync.dma_start(offs_sb[:], offs)
 
         scale_tables = []
         for g in range(PASSES):
@@ -83,6 +81,8 @@ def tile_picked_ytrim_none_po_kernel(
             return [raw.rearrange("p j (b r) -> p j b r", r=RUN) for raw in raws]
 
         first_raws = load_w1(0, 1, passes=[0])
+        offs_sb = sb([P, S // ENTRIES], U16, "offs_sb")
+        nc.sync.dma_start(offs_sb[:], offs)
         for g in range(PASSES):
             nc.sync.dma_start(scale_tables[g][0:P:SPREAD, :].bitcast(I32), x_scales[g].bitcast(I32))
         word_tables = [load_words(0)]
@@ -120,24 +120,25 @@ def tile_picked_ytrim_none_po_kernel(
             nc.vector.quantize_mx(codes[:].bitcast(FP8X4), plane[:], flat)
             return codes, plane
 
-        def first_product(c, operand, pieces, mover):
+        def first_product(c, operand, pieces, mover, by_pass=False):
             codes, plane = operand
             h = sb([P, S], F32, "h%d" % c)
-            start = 0
-            for bank, width in pieces:
-                cols = slice(start, start + width)
-                start = start + width
-                for g in range(PASSES):
-                    nc.tensor.matmul_mx(
-                        bank[:, 0:width],
-                        lhsT=codes[:, g * P : (g + 1) * P].bitcast(FP8X4),
-                        lhsT_scale=plane[:, g * P : (g + 1) * P],
-                        rhs=x_codes[g][:, cols].bitcast(FP8X4),
-                        rhs_scale=x_plane[:, g * S + cols.start : g * S + cols.stop],
-                        start=(g == 0),
-                        stop=(g == PASSES - 1),
-                    )
-                mover(h[:, cols], bank[:, 0:width])
+            starts = [sum(width for bank, width in pieces[:i]) for i in range(len(pieces))]
+            steps = [(i, g) for i in range(len(pieces)) for g in range(PASSES)]
+            for i, g in sorted(steps, key=lambda step: step[1]) if by_pass else steps:
+                bank, width = pieces[i]
+                cols = slice(starts[i], starts[i] + width)
+                nc.tensor.matmul_mx(
+                    bank[:, 0:width],
+                    lhsT=codes[:, g * P : (g + 1) * P].bitcast(FP8X4),
+                    lhsT_scale=plane[:, g * P : (g + 1) * P],
+                    rhs=x_codes[g][:, cols].bitcast(FP8X4),
+                    rhs_scale=x_plane[:, g * S + cols.start : g * S + cols.stop],
+                    start=(g == 0),
+                    stop=(g == PASSES - 1),
+                )
+                if g == PASSES - 1:
+                    mover(h[:, cols], bank[:, 0:width])
             return h
 
         operand0 = quantise_w1(0, regroup_w1(0))
@@ -156,7 +157,7 @@ def tile_picked_ytrim_none_po_kernel(
         wide = [raw.rearrange("p j (b u r) -> p j b u r", u=2, r=RUN) for raw in wide]
         w1_raw.extend([[raw[:, :, :, u, :] for raw in wide] for u in range(2)])
         pieces0 = [(banks[0], S // 2), (banks[1], S // 4), (banks[7], S // 4)]
-        h_tiles = [first_product(0, operand0, pieces0, nc.vector.tensor_copy)]
+        h_tiles = [first_product(0, operand0, pieces0, nc.vector.tensor_copy, by_pass=True)]
         w2_raw = sb([P, PACK, N], F32, "w2_raw", "w1_codes0")
         w2_rows = w2.rearrange("(b u r e) c -> u b r (e c)", u=2, r=8, e=2)
         for u in range(2):
@@ -340,5 +341,5 @@ def tile_picked_ytrim_none_po_kernel(
 
         nc.sync.dma_start(out_words, out_codes[:].bitcast(I32))
         for q in range(QUADRANTS):
-            queue = nc.scalar if q == QUADRANTS - 1 else nc.sync
+            queue = nc.scalar if q >= QUADRANTS // 2 else nc.sync
             queue.dma_start(out_2[0][4 * q : 4 * q + 4, :].bitcast(I32), out_plane[32 * q : 32 * q + 4, :].bitcast(I32))

@@ -190,8 +190,7 @@ def tile_picked_ytrim_none_po_kernel(
         def upper_middle(out, gap_b, high):
             nc.vector.scalar_tensor_tensor(out, gap_b, 0.0, high, ALU.max, ALU.min)
 
-        def sum_up(total, c, half, base, lower, upper):
-            terms = (base, base, lower, upper)
+        def sum_up(total, c, half, terms):
             for i, term in enumerate(terms):
                 nc.tensor.matmul(total, term, identity[:], start=(i == 0), stop=(i == len(terms) - 1), is_transpose=True)
             if c < 2:
@@ -227,9 +226,13 @@ def tile_picked_ytrim_none_po_kernel(
             upper_middle(upper, gap_b, high)
             return lower, upper
 
-        def sum_all(c, base, middles, sum_banks):
+        def sum_all(c, terms, sum_banks):
             for half, cols in enumerate((first, second)):
-                sum_up(sum_banks[half][:, cols], c, half, base[:, cols], middles[0][:, cols], middles[1][:, cols])
+                sum_up(sum_banks[half][:, cols], c, half, [term[:, cols] for term in terms])
+
+        def doubled(base, out):
+            nc.gpsimd.tensor_tensor(out, base, base, ALU.add)
+            return out
 
         def fetch_gaps(c, base, gaps):
             for gap, i in zip(gaps, (2, 3, 1)):
@@ -247,9 +250,9 @@ def tile_picked_ytrim_none_po_kernel(
         gaps1 = [edges[2, 1][0], spent[2][0], spent[2][1]]
         fetch_gaps(1, base1, gaps1)
         h_tiles.append(first_product(3, quantise_w1(3, late_w1[1], "high0"), [(banks[0], S)], nc.scalar.copy))
-        sum_all(0, base0, middles0, [banks[3]] * 2)
+        sum_all(0, (base0, base0) + middles0, [banks[3]] * 2)
         middles1 = compare_all(1, gaps1, [edges[2, 1][1], spent[3][0]], True)
-        sum_all(1, base1, middles1, [banks[0]] * 2)
+        sum_all(1, (doubled(base1, gaps1[1]),) + middles1, [banks[0]] * 2)
 
         w2_grouped = sb([P, N * PACK], BF16, "w2_grouped", "w1_plane3")
         dealt = w2_grouped[:].rearrange("p (t m j) -> p m j t", t=PACK, j=PACK)
@@ -261,7 +264,8 @@ def tile_picked_ytrim_none_po_kernel(
         base2 = gaps1[0]
         gaps2 = [work("gap2_%d" % i) for i in range(3)]
         fetch_gaps(2, base2, gaps2)
-        sum_all(2, base2, compare_all(2, gaps2, [work("low2"), work("high2")], True), banks[4:6])
+        middles2 = compare_all(2, gaps2, [work("low2"), work("high2")], True)
+        sum_all(2, (doubled(base2, gaps2[1]),) + middles2, banks[4:6])
 
         base3 = gaps2[0]
         gap_c3, gap_d3, gap_b3 = work("gap_c3", P), work("gap_d3", P), work("gap_b3", P)
@@ -277,7 +281,7 @@ def tile_picked_ytrim_none_po_kernel(
             greater(high, gap_c3, gap_d3)
             lower_middle(lower, gap_b, low)
             upper_middle(upper, gap_b, high)
-            sum_up(bank[:, 0:P], 3, half, base3[:, cols], lower, upper)
+            sum_up(bank[:, 0:P], 3, half, (base3[:, cols], base3[:, cols], lower, upper))
 
         finish_half(0, gap_b3, early, banks[6])
         z_grouped = [group_z(0, banks[1])]

@@ -15,6 +15,8 @@ U8 = mybir.dt.uint8
 FP8X4 = mybir.dt.float8_e4m3fn_x4
 ALU = mybir.AluOpType
 COPY = mybir.ActivationFunctionType.Copy
+RELU = mybir.ActivationFunctionType.Relu
+ABS = mybir.ActivationFunctionType.Abs
 
 P = 128
 PACK = 4
@@ -100,29 +102,25 @@ def tile_picked_ytrim_none_po_kernel(
             nc.scalar.dma_start(x_plane[r:P:32, :].bitcast(I32), x_spread[SPREAD * r : P : 32, :].bitcast(I32))
         nc.vector.tensor_copy(x_codes[0][:], word_tables[0][:].indirect(offs_sb[:]))
 
-        spent = []
+        def regroup_w1(c, g, out):
+            nc.scalar.copy(
+                out.bitcast(BF16).rearrange("p (b a i j) -> p b a j i", a=RUN // LINE, i=LINE, j=PACK),
+                w1_raw[c][g].rearrange("p j b (a i) -> p b a j i", i=LINE),
+            )
 
-        def regroup_w1(c):
-            as_f32 = sb([P, 2 * V], F32, "w1_grouped%d" % c)
-            spent.append([as_f32[:, 0:V], as_f32[:, V : 2 * V]])
-            flat = as_f32[:].bitcast(BF16)
-            grouped = flat.rearrange("p (g n) -> p g n", g=PASSES)
-            for g in range(PASSES):
-                nc.scalar.copy(
-                    grouped[:, g, :].rearrange("p (b a i j) -> p b a j i", a=RUN // LINE, i=LINE, j=PACK),
-                    w1_raw[c][g].rearrange("p j b (a i) -> p b a j i", i=LINE),
-                )
-            return flat
+        def quantise_w1(name, grouped, in_place_of=None):
+            width = grouped.shape[1] // 2
+            codes = sb([P, width], U32, "w1_codes" + name, in_place_of)
+            plane = sb([P, width], U8, "w1_plane" + name)
+            nc.vector.quantize_mx(codes[:].bitcast(FP8X4), plane[:], grouped.bitcast(BF16))
+            return [(codes[:, n : n + P], plane[:, n : n + P]) for n in range(0, width, P)]
 
-        def quantise_w1(c, flat, in_place_of=None):
-            codes = sb([P, PASSES * P], U32, "w1_codes%d" % c, in_place_of)
-            plane = sb([P, PASSES * P], U8, "w1_plane%d" % c)
-            nc.vector.quantize_mx(codes[:].bitcast(FP8X4), plane[:], flat)
-            return codes, plane
+        def both_passes(c):
+            tile = sb([P, PASSES * V], F32, "w1_grouped%d" % c)
+            return tile[:], [tile[:, g * V : (g + 1) * V] for g in range(PASSES)]
 
-        def first_product(c, operand, pieces, mover, by_pass=False):
-            codes, plane = operand
-            h = sb([P, S], F32, "h%d" % c)
+        def first_product(c, operand, pieces, mover, by_pass=False, in_place_of=None):
+            h = sb([P, S], F32, "h%d" % c, in_place_of)
             starts = [sum(width for bank, width in pieces[:i]) for i in range(len(pieces))]
             steps = [(i, g) for i in range(len(pieces)) for g in range(PASSES)]
             for i, g in sorted(steps, key=lambda step: step[1]) if by_pass else steps:
@@ -130,8 +128,8 @@ def tile_picked_ytrim_none_po_kernel(
                 cols = slice(starts[i], starts[i] + width)
                 nc.tensor.matmul_mx(
                     bank[:, 0:width],
-                    lhsT=codes[:, g * P : (g + 1) * P].bitcast(FP8X4),
-                    lhsT_scale=plane[:, g * P : (g + 1) * P],
+                    lhsT=operand[g][0].bitcast(FP8X4),
+                    lhsT_scale=operand[g][1],
                     rhs=x_codes[g][:, cols].bitcast(FP8X4),
                     rhs_scale=x_plane[:, g * S + cols.start : g * S + cols.stop],
                     start=(g == 0),
@@ -141,7 +139,10 @@ def tile_picked_ytrim_none_po_kernel(
                     mover(h[:, cols], bank[:, 0:width])
             return h
 
-        operand0 = quantise_w1(0, regroup_w1(0))
+        grouped0, spent0 = both_passes(0)
+        for g in range(PASSES):
+            regroup_w1(0, g, spent0[g])
+        operand0 = quantise_w1("0", grouped0)
 
         w1_raw.append(by_runs(load_w1(1, 1, ("word_table0", "w1_raw0_1"))))
         lists = (pos1, pos2, pos3, pos4)
@@ -163,8 +164,11 @@ def tile_picked_ytrim_none_po_kernel(
         for u in range(2):
             nc.sync.dma_start(w2_raw[:, 2 * u : 2 * u + 2, :].rearrange("p e c -> p (e c)"), w2_rows[u])
         pieces1 = [(banks[2], S // 2), (banks[4], S // 2)]
-        h_tiles.append(first_product(1, quantise_w1(1, regroup_w1(1)), pieces1, nc.scalar.copy))
-        late_w1 = [regroup_w1(2), regroup_w1(3)]
+        spent1 = [sb([P, V], F32, "w1_grouped1_%d" % g)[:] for g in range(PASSES)]
+        for g in range(PASSES):
+            regroup_w1(1, g, spent1[g])
+        operand1 = quantise_w1("1_0", spent1[0], "w1_plane0")
+        (grouped2, spent2), (grouped3, spent3) = both_passes(2), both_passes(3)
 
         z_flat = [sb([P, H], BF16, "z_rows%d" % half)[:] for half in range(V // P)]
         z_rows = [rows.rearrange("v (u n) -> v u n", u=2) for rows in z_flat]
@@ -214,77 +218,120 @@ def tile_picked_ytrim_none_po_kernel(
 
         first, second = slice(0, P), slice(P, V)
 
-        def compare_all(c, gaps, pair, fetch_next):
-            gap_c, gap_d, gap_b = gaps
-            low, high = pair
-            lower, upper = work("lower%d" % c), work("upper%d" % c)
-            lesser(low, gap_c, gap_d)
-            greater(high, gap_c, gap_d)
-            lower_middle(lower, gap_b, low)
-            if fetch_next:
-                fetch_base(gap_c, c + 1)
-            upper_middle(upper, gap_b, high)
-            return lower, upper
-
         def sum_all(c, terms, sum_banks):
             for half, cols in enumerate((first, second)):
                 sum_up(sum_banks[half][:, cols], c, half, [term[:, cols] for term in terms])
 
-        def doubled(base, out):
-            nc.gpsimd.tensor_tensor(out, base, base, ALU.add)
-            return out
+        def flanked(name):
+            tile = work(name, 2 * V)
+            return tile[:, V // 2 : V // 2 + V], tile[:, 0:V], tile[:, V : 2 * V]
 
-        def fetch_gaps(c, base, gaps):
-            for gap, i in zip(gaps, (2, 3, 1)):
-                fetch_gap(gap, i, base, c, 0, V)
+        def shortfall(out, gap_b):
+            nc.scalar.activation(out, gap_b, RELU, scale=-1.0)
 
-        base0, base1 = work("base0"), work("low0")
+        def spread(out, gap_b):
+            nc.scalar.activation(out, gap_b, ABS)
+
+        def least(out, base, short):
+            nc.gpsimd.tensor_tensor(out, base, short, ALU.subtract)
+
+        halves2 = [(banks[3], S // 2), (banks[5], S // 2)]
+        halves3 = [(banks[0], S // 2), (banks[6], S // 2)]
+
+        base0 = work("base0")
         fetch_base(base0, 0)
-        gaps0 = [edges[1, 1][0], spent[1][0], spent[1][1]]
-        fetch_gaps(0, base0, gaps0)
-        middles0 = compare_all(0, gaps0, [base1, work("high0")], False)
+        operand1 = operand1 + quantise_w1("1_1", spent1[1], "w1_grouped1_0")
+        regroup_w1(2, 0, spent2[0])
+        regroup_w1(3, 0, spent3[0])
+        regroup_w1(2, 1, spent2[1])
+        h_tiles.append(first_product(1, operand1, pieces1, nc.scalar.copy, by_pass=True, in_place_of="w1_grouped0"))
+        regroup_w1(3, 1, spent3[1])
+        gap_c0, gap_d0, gap_b0 = edges[1, 1][0], spent1[1], edges[1, 1][1]
+        fetch_gap(gap_c0, 2, base0, 0, 0, V)
+        fetch_gap(gap_d0, 3, base0, 0, 0, V)
+        fetch_gap(gap_b0, 1, base0, 0, 0, V)
 
+        operand2 = quantise_w1("2", grouped2)
+        base1, low0, high0 = edges[2, 1][0], spent2[0], spent2[1]
+        gap_b1, upper0, gap_c1 = flanked("gap_b1")
+        lower0, short1, least1 = work("lower0"), work("short1"), work("least1")
         fetch_base(base1, 1)
-        operand2 = quantise_w1(2, late_w1[0], "w1_grouped1")
-        h_tiles.append(first_product(2, operand2, [(banks[3], S)], nc.scalar.copy))
-        gaps1 = [edges[2, 1][0], spent[2][0], spent[2][1]]
-        fetch_gaps(1, base1, gaps1)
-        h_tiles.append(first_product(3, quantise_w1(3, late_w1[1], "high0"), [(banks[0], S)], nc.scalar.copy))
-        sum_all(0, (base0, base0) + middles0, [banks[3]] * 2)
-        middles1 = compare_all(1, gaps1, [edges[2, 1][1], spent[3][0]], True)
-        sum_all(1, (doubled(base1, gaps1[1]),) + middles1, [banks[0]] * 2)
+        lesser(low0, gap_c0, gap_d0)
+        fetch_gap(gap_b1, 1, base1, 1, 0, V)
+        greater(high0, gap_c0, gap_d0)
+        lower_middle(lower0, gap_b0, low0)
+        shortfall(short1, gap_b1)
+        h_tiles.append(first_product(2, operand2, halves2, nc.scalar.copy))
+        spread1 = sb([P, V], F32, "spread1", "w1_codes2")[:]
+        spread(spread1, gap_b1)
 
-        w2_grouped = sb([P, N * PACK], BF16, "w2_grouped", "w1_plane3")
+        operand3 = quantise_w1("3", grouped3)
+        base2 = edges[2, 1][1]
+        gap_b2, high1, low1 = flanked("gap_b2")
+        short2, least2 = work("short2"), work("least2")
+        gap_d1 = gap_b0
+        fetch_base(base2, 2)
+        least(least1, base1, short1)
+        upper_middle(upper0, gap_b0, high0)
+        fetch_gap(gap_b2, 1, base2, 2, 0, V)
+        shortfall(short2, gap_b2)
+        h_tiles.append(first_product(3, operand3, halves3, nc.scalar.copy))
+        spread2 = sb([P, V], F32, "spread2", "w1_codes3")[:]
+        spread(spread2, gap_b2)
+        fetch_gap(gap_c1, 2, least1, 1, 0, V)
+        fetch_gap(gap_d1, 3, least1, 1, 0, V)
+        sum_all(0, (base0, base0, lower0, upper0), [banks[0]] * 2)
+
+        base3 = spent3[0]
+        lower1, upper1 = work("lower1"), work("upper1")
+        fetch_base(base3, 3)
+        least(least2, base2, short2)
+        greater(high1, gap_c1, gap_d1)
+        lesser(low1, gap_c1, gap_d1)
+        lesser(upper1, spread1, high1)
+        nc.scalar.activation(lower1, low1, RELU)
+        sum_all(1, (least1, least1, lower1, upper1), [banks[3]] * 2)
+
+        w2_grouped = sb([P, N * PACK], BF16, "w2_grouped", "w1_grouped0")
         dealt = w2_grouped[:].rearrange("p (t m j) -> p m j t", t=PACK, j=PACK)
         source = w2_raw[:].rearrange("p j (m t) -> p m j t", t=PACK)
         for piece in range(W2_PIECES):
             part = slice(piece * P // W2_PIECES, (piece + 1) * P // W2_PIECES)
             nc.scalar.copy(dealt[:, part], source[:, part])
 
-        base2 = gaps1[0]
-        gaps2 = [work("gap2_%d" % i) for i in range(3)]
-        fetch_gaps(2, base2, gaps2)
-        middles2 = compare_all(2, gaps2, [work("low2"), work("high2")], True)
-        sum_all(2, (doubled(base2, gaps2[1]),) + middles2, banks[4:6])
-
-        base3 = gaps2[0]
-        gap_c3, gap_d3, gap_b3 = work("gap_c3", P), work("gap_d3", P), work("gap_b3", P)
+        gap_c2, gap_d2 = work("gap_c2"), work("gap_d2")
+        high2, low2, lower2, upper2 = work("high2"), work("low2"), work("lower2"), work("upper2")
+        gap_c3, gap_d3, gap_b3 = short2[:, first], base2[:, first], gap_c2[:, first]
         early = [work("early%d" % i, P) for i in range(4)]
         late = [work("late%d" % i, P) for i in range(4)]
+
+        def fetch_last(gap, i, half):
+            fetch_gap(gap, i, base3[:, (first, second)[half]], 3, half * P, P)
 
         def finish_half(half, gap_b, tiles, bank):
             cols = (first, second)[half]
             low, high, lower, upper = tiles
-            for gap, i in ((gap_c3, 2), (gap_d3, 3), (gap_b, 1)):
-                fetch_gap(gap, i, base3[:, cols], 3, half * P, P)
             lesser(low, gap_c3, gap_d3)
             greater(high, gap_c3, gap_d3)
             lower_middle(lower, gap_b, low)
             upper_middle(upper, gap_b, high)
             sum_up(bank[:, 0:P], 3, half, (base3[:, cols], base3[:, cols], lower, upper))
 
+        fetch_gap(gap_c2, 2, least2, 2, 0, V)
+        fetch_gap(gap_d2, 3, least2, 2, 0, V)
+        fetch_last(gap_c3, 2, 0)
+        greater(high2, gap_c2, gap_d2)
+        lesser(low2, gap_c2, gap_d2)
+        fetch_last(gap_d3, 3, 0)
+        lesser(upper2, spread2, high2)
+        nc.scalar.activation(lower2, low2, RELU)
+        sum_all(2, (least2, least2, lower2, upper2), banks[4:6])
+        fetch_last(gap_b3, 1, 0)
+
         finish_half(0, gap_b3, early, banks[6])
         z_grouped = [group_z(0, banks[1])]
+        for gap, i in ((gap_c3, 2), (gap_d3, 3), (early[0], 1)):
+            fetch_last(gap, i, 1)
         finish_half(1, early[0], late, banks[7])
         z_grouped.append(group_z(1, banks[2]))
 

@@ -60,15 +60,19 @@ def tile_picked_ytrim_none_po_kernel(
             nc.sync.dma_start(table[:].bitcast(I32), x_words[g].rearrange("p n t -> p (n t)").bitcast(I32))
             return table
 
-        edges = {}
+        edges, wide_edges, second_edges = {}, {}, {}
 
         def load_w1(chunk, count, in_place_of=(None, None), passes=range(PASSES)):
             raws = []
             for g in passes:
-                loaded = PACK * count * P
-                padded = sb([P, loaded + 2 * V], F32, "w1_raw%d_%d" % (chunk, g), in_place_of[g])
-                edges[chunk, g] = (padded[:, RUN : RUN + V], padded[:, V + loaded - RUN : 2 * V + loaded - RUN])
-                raw = padded[:, V : V + loaded].rearrange("p (j c) -> p j c", j=PACK)
+                width = count * P
+                pitch = width + (2 * V if (chunk, g) == (2, 1) else 0)
+                end = 2 * V + (PACK - 1) * pitch + width
+                padded = sb([P, 2 * V + PACK * pitch + V], F32, "w1_raw%d_%d" % (chunk, g), in_place_of[g])
+                edges[chunk, g] = (padded[:, V + RUN : 2 * V + RUN], padded[:, end - RUN : end - RUN + V])
+                wide_edges[chunk, g] = padded[:, V // 2 + RUN : V // 2 + RUN + 2 * V]
+                second_edges[chunk, g] = padded[:, pitch + RUN : pitch + RUN + 2 * V]
+                raw = padded[:, 2 * V : 2 * V + PACK * pitch].rearrange("p (j c) -> p j c", j=PACK)[:, :, 0:width]
                 rows = w1[g * K_PASS : (g + 1) * K_PASS, chunk * P : (chunk + count) * P]
                 nc.sync.dma_start(raw, rows.rearrange("(p j) c -> p j c", j=PACK))
                 raws.append(raw)
@@ -102,10 +106,10 @@ def tile_picked_ytrim_none_po_kernel(
             nc.scalar.dma_start(x_plane[r:P:32, :].bitcast(I32), x_spread[SPREAD * r : P : 32, :].bitcast(I32))
         nc.vector.tensor_copy(x_codes[0][:], word_tables[0][:].indirect(offs_sb[:]))
 
-        def regroup_w1(c, g, out):
+        def regroup_w1(c, g, out, runs=slice(0, P // RUN)):
             nc.scalar.copy(
-                out.bitcast(BF16).rearrange("p (b a i j) -> p b a j i", a=RUN // LINE, i=LINE, j=PACK),
-                w1_raw[c][g].rearrange("p j b (a i) -> p b a j i", i=LINE),
+                out.bitcast(BF16).rearrange("p (b a i j) -> p b a j i", a=RUN // LINE, i=LINE, j=PACK)[:, runs],
+                w1_raw[c][g].rearrange("p j b (a i) -> p b a j i", i=LINE)[:, runs],
             )
 
         def quantise_w1(name, grouped, in_place_of=None):
@@ -114,6 +118,9 @@ def tile_picked_ytrim_none_po_kernel(
             plane = sb([P, width], U8, "w1_plane" + name)
             nc.vector.quantize_mx(codes[:].bitcast(FP8X4), plane[:], grouped.bitcast(BF16))
             return [(codes[:, n : n + P], plane[:, n : n + P]) for n in range(0, width, P)]
+
+        def work_tile(name, width):
+            return sb([P, width], F32, name)[:]
 
         def both_passes(c):
             tile = sb([P, PASSES * V], F32, "w1_grouped%d" % c)
@@ -168,7 +175,8 @@ def tile_picked_ytrim_none_po_kernel(
         for g in range(PASSES):
             regroup_w1(1, g, spent1[g])
         operand1 = quantise_w1("1_0", spent1[0], "w1_plane0")
-        (grouped2, spent2), (grouped3, spent3) = both_passes(2), both_passes(3)
+        grouped_early = work_tile("w1_grouped_early", 2 * V)
+        spent3 = [grouped_early[:, V : 2 * V], second_edges[2, 1][:, V : 2 * V]]
 
         z_flat = [sb([P, H], BF16, "z_rows%d" % half)[:] for half in range(V // P)]
         z_rows = [rows.rearrange("v (u n) -> v u n", u=2) for rows in z_flat]
@@ -222,8 +230,7 @@ def tile_picked_ytrim_none_po_kernel(
             for half, cols in enumerate((first, second)):
                 sum_up(sum_banks[half][:, cols], c, half, [term[:, cols] for term in terms])
 
-        def flanked(name):
-            tile = work(name, 2 * V)
+        def flanked(tile):
             return tile[:, V // 2 : V // 2 + V], tile[:, 0:V], tile[:, V : 2 * V]
 
         def shortfall(out, gap_b):
@@ -236,38 +243,41 @@ def tile_picked_ytrim_none_po_kernel(
             nc.gpsimd.tensor_tensor(out, base, short, ALU.subtract)
 
         halves2 = [(banks[3], S // 2), (banks[5], S // 2)]
-        halves3 = [(banks[0], S // 2), (banks[6], S // 2)]
+        halves3 = halves2
 
         base0 = work("base0")
         fetch_base(base0, 0)
         operand1 = operand1 + quantise_w1("1_1", spent1[1], "w1_grouped1_0")
-        regroup_w1(2, 0, spent2[0])
+        grouped2_0 = grouped_early[:, 0:V]
+        grouped2_1, low0, high0 = flanked(work("w1_grouped2_1", 2 * V))
+        regroup_w1(2, 0, grouped2_0)
         regroup_w1(3, 0, spent3[0])
-        regroup_w1(2, 1, spent2[1])
-        h_tiles.append(first_product(1, operand1, pieces1, nc.scalar.copy, by_pass=True, in_place_of="w1_grouped0"))
-        regroup_w1(3, 1, spent3[1])
         gap_c0, gap_d0, gap_b0 = edges[1, 1][0], spent1[1], edges[1, 1][1]
         fetch_gap(gap_c0, 2, base0, 0, 0, V)
         fetch_gap(gap_d0, 3, base0, 0, 0, V)
         fetch_gap(gap_b0, 1, base0, 0, 0, V)
+        early2, early3 = quantise_w1("_early", grouped_early)
+        h_tiles.append(first_product(1, operand1, pieces1, nc.scalar.copy, by_pass=True, in_place_of="w1_grouped0"))
+        regroup_w1(2, 1, grouped2_1, slice(7, 8))
+        regroup_w1(2, 1, grouped2_1, slice(0, 7))
+        regroup_w1(3, 1, spent3[1])
 
-        operand2 = quantise_w1("2", grouped2)
-        base1, low0, high0 = edges[2, 1][0], spent2[0], spent2[1]
-        gap_b1, upper0, gap_c1 = flanked("gap_b1")
-        lower0, short1, least1 = work("lower0"), work("short1"), work("least1")
+        gap_b1, upper0, gap_c1 = flanked(wide_edges[2, 1])
+        base1, lower0, short1, least1 = work("base1"), edges[2, 1][1], work("short1"), low0
         fetch_base(base1, 1)
-        lesser(low0, gap_c0, gap_d0)
+        operand2 = [early2] + quantise_w1("2_1", grouped2_1)
         fetch_gap(gap_b1, 1, base1, 1, 0, V)
+        lesser(low0, gap_c0, gap_d0)
         greater(high0, gap_c0, gap_d0)
         lower_middle(lower0, gap_b0, low0)
         shortfall(short1, gap_b1)
-        h_tiles.append(first_product(2, operand2, halves2, nc.scalar.copy))
-        spread1 = sb([P, V], F32, "spread1", "w1_codes2")[:]
+        h_tiles.append(first_product(2, operand2, halves2, nc.scalar.copy, by_pass=True))
+        spread1 = sb([P, V], F32, "spread1", "w1_codes2_1")[:]
         spread(spread1, gap_b1)
 
-        operand3 = quantise_w1("3", grouped3)
-        base2 = edges[2, 1][1]
-        gap_b2, high1, low1 = flanked("gap_b2")
+        operand3 = [early3] + quantise_w1("3_1", spent3[1])
+        base2 = work("base2")
+        gap_b2, high1, low1 = flanked(work("gap_b2", 2 * V))
         short2, least2 = work("short2"), work("least2")
         gap_d1 = gap_b0
         fetch_base(base2, 2)
@@ -276,13 +286,13 @@ def tile_picked_ytrim_none_po_kernel(
         fetch_gap(gap_b2, 1, base2, 2, 0, V)
         shortfall(short2, gap_b2)
         h_tiles.append(first_product(3, operand3, halves3, nc.scalar.copy))
-        spread2 = sb([P, V], F32, "spread2", "w1_codes3")[:]
+        spread2 = sb([P, V], F32, "spread2", "w1_codes3_1")[:]
         spread(spread2, gap_b2)
         fetch_gap(gap_c1, 2, least1, 1, 0, V)
         fetch_gap(gap_d1, 3, least1, 1, 0, V)
-        sum_all(0, (base0, base0, lower0, upper0), [banks[0]] * 2)
+        sum_all(0, (base0, base0, lower0, upper0), [banks[3]] * 2)
 
-        base3 = spent3[0]
+        base3 = spent3[1]
         lower1, upper1 = work("lower1"), work("upper1")
         fetch_base(base3, 3)
         least(least2, base2, short2)
@@ -290,7 +300,7 @@ def tile_picked_ytrim_none_po_kernel(
         lesser(low1, gap_c1, gap_d1)
         lesser(upper1, spread1, high1)
         nc.scalar.activation(lower1, low1, RELU)
-        sum_all(1, (least1, least1, lower1, upper1), [banks[3]] * 2)
+        sum_all(1, (least1, least1, lower1, upper1), [banks[0]] * 2)
 
         w2_grouped = sb([P, N * PACK], BF16, "w2_grouped", "w1_grouped0")
         dealt = w2_grouped[:].rearrange("p (t m j) -> p m j t", t=PACK, j=PACK)
@@ -332,14 +342,13 @@ def tile_picked_ytrim_none_po_kernel(
         z_grouped = [group_z(0, banks[1])]
         for gap, i in ((gap_c3, 2), (gap_d3, 3), (early[0], 1)):
             fetch_last(gap, i, 1)
-        finish_half(1, early[0], late, banks[7])
+        finish_half(1, early[0], late, banks[6])
         z_grouped.append(group_z(1, banks[2]))
 
         w2_codes = sb([P, N], U32, "w2_codes", "late0")
         w2_plane = sb([P, N], U8, "w2_plane")
         nc.vector.quantize_mx(w2_codes[:].bitcast(FP8X4), w2_plane[:], w2_grouped[:])
 
-        out_codes = sb([P, V], U32, "out_codes")
         out_plane = sb([P, V], U8, "out_plane")
         out_rows = out_0.rearrange("(p t) v -> p t v", t=PACK)
         out_words = out_1[0].rearrange("p n t -> p (n t)").bitcast(I32)
@@ -370,24 +379,26 @@ def tile_picked_ytrim_none_po_kernel(
             mover(grouped[:].rearrange("p (v t) -> p v t", t=PACK), acc.rearrange("p t v -> p v t"))
             return grouped
 
-        def store_y(half, y, acc, rows, queue):
-            nc.scalar.copy(y[:, rows, :], acc[:, rows, :])
+        def store_y(half, y, acc, rows, queue, mover=nc.scalar.copy):
+            mover(y[:, rows, :], acc[:, rows, :])
             queue.dma_start(out_rows[:, rows, (first, second)[half]], y[:, rows, :])
 
         def quantise_y(half, grouped):
             cols = (first, second)[half]
             nc.vector.quantize_mx(out_codes[:, cols].bitcast(FP8X4), out_plane[:, cols], grouped[:])
 
-        acc = second_product(quantise_z(0, "late1"), banks[4], PACK)
+        acc = second_product(quantise_z(0, "late1"), banks[6], PACK)
         store_y(0, sb([P, PACK, P], F32, "y0"), acc, slice(0, PACK), nc.sync)
-        quantise_y(0, group_y(0, acc, nc.scalar.copy))
+        grouped_first = group_y(0, acc, nc.vector.tensor_copy)
 
         operand = quantise_z(1)
         acc = second_product(operand, banks[5], PACK)
-        grouped = group_y(1, acc, nc.vector.tensor_copy)
+        grouped = group_y(1, acc, nc.scalar.copy)
         y = sb([P, PACK, P], F32, "y1")
-        store_y(1, y, second_product(operand, banks[6], 2), slice(0, 2), nc.sync)
+        store_y(1, y, second_product(operand, banks[7], 2), slice(0, 2), nc.sync, nc.vector.tensor_copy)
         store_y(1, y, acc, slice(2, PACK), nc.scalar)
+        out_codes = sb([P, V], U32, "out_codes", "z_codes1")
+        quantise_y(0, grouped_first)
         quantise_y(1, grouped)
 
         nc.sync.dma_start(out_words, out_codes[:].bitcast(I32))

@@ -349,6 +349,7 @@ def tile_picked_ytrim_none_po_kernel(
         w2_plane = sb([P, N], U8, "w2_plane")
         nc.vector.quantize_mx(w2_codes[:].bitcast(FP8X4), w2_plane[:], w2_grouped[:])
 
+        out_codes = sb([P, V], U32, "out_codes")
         out_plane = sb([P, V], U8, "out_plane")
         out_rows = out_0.rearrange("(p t) v -> p t v", t=PACK)
         out_words = out_1[0].rearrange("p n t -> p (n t)").bitcast(I32)
@@ -379,8 +380,8 @@ def tile_picked_ytrim_none_po_kernel(
             mover(grouped[:].rearrange("p (v t) -> p v t", t=PACK), acc.rearrange("p t v -> p v t"))
             return grouped
 
-        def store_y(half, y, acc, rows, queue, mover=nc.scalar.copy):
-            mover(y[:, rows, :], acc[:, rows, :])
+        def store_y(half, y, acc, rows, queue):
+            nc.scalar.copy(y[:, rows, :], acc[:, rows, :])
             queue.dma_start(out_rows[:, rows, (first, second)[half]], y[:, rows, :])
 
         def quantise_y(half, grouped):
@@ -389,16 +390,14 @@ def tile_picked_ytrim_none_po_kernel(
 
         acc = second_product(quantise_z(0, "late1"), banks[6], PACK)
         store_y(0, sb([P, PACK, P], F32, "y0"), acc, slice(0, PACK), nc.sync)
-        grouped_first = group_y(0, acc, nc.vector.tensor_copy)
+        quantise_y(0, group_y(0, acc, nc.scalar.copy))
 
         operand = quantise_z(1)
         acc = second_product(operand, banks[5], PACK)
-        grouped = group_y(1, acc, nc.scalar.copy)
+        grouped = group_y(1, acc, nc.vector.tensor_copy)
         y = sb([P, PACK, P], F32, "y1")
-        store_y(1, y, second_product(operand, banks[7], 2), slice(0, 2), nc.sync, nc.vector.tensor_copy)
+        store_y(1, y, second_product(operand, banks[7], 2), slice(0, 2), nc.sync)
         store_y(1, y, acc, slice(2, PACK), nc.scalar)
-        out_codes = sb([P, V], U32, "out_codes", "z_codes1")
-        quantise_y(0, grouped_first)
         quantise_y(1, grouped)
 
         nc.sync.dma_start(out_words, out_codes[:].bitcast(I32))

@@ -1,7 +1,6 @@
 from contextlib import ExitStack
 
 import concourse.mybir as mybir
-from concourse.masks import make_identity
 
 K, T, S, V, H, N = 1024, 2048, 512, 256, 512, 512
 FLOPS = 2 * K * H * S + 2 * H * N * V
@@ -15,8 +14,6 @@ U8 = mybir.dt.uint8
 FP8X4 = mybir.dt.float8_e4m3fn_x4
 ALU = mybir.AluOpType
 COPY = mybir.ActivationFunctionType.Copy
-RELU = mybir.ActivationFunctionType.Relu
-ABS = mybir.ActivationFunctionType.Abs
 
 P = 128
 PACK = 4
@@ -25,11 +22,8 @@ PASSES = K // K_PASS
 QUADRANTS = 4
 ENTRIES = 16
 LINE = 4
-SPREAD = 8
-RUN = 16
-U_WIDTH = H // 2
 BANK = 512
-W2_PIECES = 4
+HALF = V // 2
 
 
 def tile_picked_ytrim_none_po_kernel(
@@ -45,319 +39,174 @@ def tile_picked_ytrim_none_po_kernel(
 
         banks = [psum.tile([P, BANK], F32, name="bank%d" % i) for i in range(8)]
 
+        scale_table = sb([P, T], U8, "scale_table")
+        nc.vector.memset(scale_table[:].bitcast(I32), 0)
 
-        scale_tables = []
-        for g in range(PASSES):
-            table = sb([P, T], U8, "scale_table%d" % g)
-            nc.vector.memset(table[:].bitcast(I32), 0)
-            scale_tables.append(table)
-
-        x_plane = sb([P, PASSES * S], U8, "x_plane")
-        nc.vector.memset(x_plane[:].bitcast(I32), 0)
+        def load_rows(w, g, c0, width, name):
+            raw = sb([P, PACK, width], F32, name)
+            nc.sync.dma_start(raw[:], w[g * K_PASS : (g + 1) * K_PASS, c0 : c0 + width].rearrange("(p j) c -> p j c", j=PACK))
+            return raw
 
         def load_words(g):
             table = sb([P, T], U32, "word_table%d" % g)
             nc.sync.dma_start(table[:].bitcast(I32), x_words[g].rearrange("p n t -> p (n t)").bitcast(I32))
             return table
 
-        edges, wide_edges, second_edges = {}, {}, {}
+        def load_scales(g):
+            for q in range(QUADRANTS):
+                rows = scale_table[32 * q + 4 * g : 32 * q + 4 * g + 4, :]
+                nc.sync.dma_start(rows.bitcast(I32), x_scales[g][4 * q : 4 * q + 4, :].bitcast(I32))
 
-        def load_w1(chunk, count, in_place_of=(None, None), passes=range(PASSES)):
-            raws = []
-            for g in passes:
-                width = count * P
-                pitch = width + (2 * V if (chunk, g) == (2, 1) else 0)
-                end = 2 * V + (PACK - 1) * pitch + width
-                padded = sb([P, 2 * V + PACK * pitch + V], F32, "w1_raw%d_%d" % (chunk, g), in_place_of[g])
-                edges[chunk, g] = (padded[:, V + RUN : 2 * V + RUN], padded[:, end - RUN : end - RUN + V])
-                wide_edges[chunk, g] = padded[:, V // 2 + RUN : V // 2 + RUN + 2 * V]
-                second_edges[chunk, g] = padded[:, pitch + RUN : pitch + RUN + 2 * V]
-                raw = padded[:, 2 * V : 2 * V + PACK * pitch].rearrange("p (j c) -> p j c", j=PACK)[:, :, 0:width]
-                rows = w1[g * K_PASS : (g + 1) * K_PASS, chunk * P : (chunk + count) * P]
-                nc.sync.dma_start(raw, rows.rearrange("(p j) c -> p j c", j=PACK))
-                raws.append(raw)
-            return raws
-
-        def load_list(i, pos):
-            list_tile = sb([P, V // ENTRIES], U16, "pos_sb%d" % i)
+        def load_list(name, pos, entries):
+            list_tile = sb([P, entries // ENTRIES], U16, name)
             nc.sync.dma_start(list_tile[:], pos)
             return list_tile
 
-        def by_runs(raws):
-            return [raw.rearrange("p j (b r) -> p j b r", r=RUN) for raw in raws]
-
-        first_raws = load_w1(0, 1, passes=[0])
-        offs_sb = sb([P, S // ENTRIES], U16, "offs_sb")
-        nc.sync.dma_start(offs_sb[:], offs)
-        for g in range(PASSES):
-            nc.sync.dma_start(scale_tables[g][0:P:SPREAD, :].bitcast(I32), x_scales[g].bitcast(I32))
+        w1_first = load_rows(w1, 0, 0, H, "w1_raw0")
+        offs_sb = load_list("offs_sb", offs, S)
+        load_scales(0)
         word_tables = [load_words(0)]
-        w1_raw = [by_runs(first_raws + load_w1(0, 1, passes=[1]))]
+        w1_left = load_rows(w1, 1, 0, H // 2, "w1_raw1_left")
+        load_scales(1)
         word_tables.append(load_words(1))
+        w1_right = load_rows(w1, 1, H // 2, H // 2, "w1_raw1_right")
+        lists = (pos1, pos2, pos3, pos4)
+        pos_sb = [load_list("pos_sb%d" % i, lists[i], V) for i in range(4)]
+        w2_raw = load_rows(w2, 0, 0, N, "w2_raw")
 
-        identity = sb([P, P], F32, "identity")
-        make_identity(nc, identity[:])
+        def regroup(mover, grouped, raw, m0, first, count):
+            dealt = grouped[:].rearrange("p (t m j) -> p m j t", t=PACK, j=PACK)
+            source = raw[:].rearrange("p j (m t) -> p m j t", t=PACK)
+            mover(dealt[:, m0 + first : m0 + first + count], source[:, first : first + count])
 
+        def quantise(codes, plane, grouped):
+            nc.vector.quantize_mx(codes.bitcast(FP8X4), plane, grouped)
+
+        w1_grouped = [sb([P, H * PACK], BF16, "w1_grouped%d" % g) for g in range(PASSES)]
+        w1_codes = [sb([P, H], U32, "w1_codes%d" % g) for g in range(PASSES)]
+        w1_plane = [sb([P, H], U8, "w1_plane%d" % g) for g in range(PASSES)]
         x_codes = [sb([P, S], U32, "x_codes%d" % g) for g in range(PASSES)]
-        x_spread = sb([P, PASSES * S], U8, "x_spread")
-        for g in range(PASSES):
-            nc.vector.tensor_copy(x_spread[:, g * S : (g + 1) * S], scale_tables[g][:].indirect(offs_sb[:]))
-        for r in range(4):
-            nc.scalar.dma_start(x_plane[r:P:32, :].bitcast(I32), x_spread[SPREAD * r : P : 32, :].bitcast(I32))
+        x_plane = sb([P, S], U8, "x_plane")
+
+        regroup(nc.scalar.copy, w1_grouped[0], w1_first, 0, 0, P)
         nc.vector.tensor_copy(x_codes[0][:], word_tables[0][:].indirect(offs_sb[:]))
+        quantise(w1_codes[0][:], w1_plane[0][:], w1_grouped[0][:])
+        regroup(nc.scalar.copy, w1_grouped[1], w1_left, 0, 0, P // 2)
+        nc.vector.tensor_copy(x_plane[:], scale_table[:].indirect(offs_sb[:]))
 
-        def regroup_w1(c, g, out, runs=slice(0, P // RUN)):
-            nc.scalar.copy(
-                out.bitcast(BF16).rearrange("p (b a i j) -> p b a j i", a=RUN // LINE, i=LINE, j=PACK)[:, runs],
-                w1_raw[c][g].rearrange("p j b (a i) -> p b a j i", i=LINE)[:, runs],
-            )
+        pieces = [[(banks[0], 0, S // 2), (banks[1], S // 2, S // 2)]] + [[(banks[1 + c], 0, S)] for c in range(1, PACK)]
 
-        def quantise_w1(name, grouped, in_place_of=None):
-            width = grouped.shape[1] // 2
-            codes = sb([P, width], U32, "w1_codes" + name, in_place_of)
-            plane = sb([P, width], U8, "w1_plane" + name)
-            nc.vector.quantize_mx(codes[:].bitcast(FP8X4), plane[:], grouped.bitcast(BF16))
-            return [(codes[:, n : n + P], plane[:, n : n + P]) for n in range(0, width, P)]
-
-        def work_tile(name, width):
-            return sb([P, width], F32, name)[:]
-
-        def both_passes(c):
-            tile = sb([P, PASSES * V], F32, "w1_grouped%d" % c)
-            return tile[:], [tile[:, g * V : (g + 1) * V] for g in range(PASSES)]
-
-        def first_product(c, operand, pieces, mover, by_pass=False, in_place_of=None):
-            h = sb([P, S], F32, "h%d" % c, in_place_of)
-            starts = [sum(width for bank, width in pieces[:i]) for i in range(len(pieces))]
-            steps = [(i, g) for i in range(len(pieces)) for g in range(PASSES)]
-            for i, g in sorted(steps, key=lambda step: step[1]) if by_pass else steps:
-                bank, width = pieces[i]
-                cols = slice(starts[i], starts[i] + width)
+        def first_product(c, g):
+            for bank, start, width in pieces[c]:
                 nc.tensor.matmul_mx(
                     bank[:, 0:width],
-                    lhsT=operand[g][0].bitcast(FP8X4),
-                    lhsT_scale=operand[g][1],
-                    rhs=x_codes[g][:, cols].bitcast(FP8X4),
-                    rhs_scale=x_plane[:, g * S + cols.start : g * S + cols.stop],
+                    lhsT=w1_codes[g][:, c * P : (c + 1) * P].bitcast(FP8X4),
+                    lhsT_scale=w1_plane[g][:, c * P : (c + 1) * P],
+                    rhs=x_codes[g][:, start : start + width].bitcast(FP8X4),
+                    rhs_scale=x_plane[4 * g : P, start : start + width],
                     start=(g == 0),
                     stop=(g == PASSES - 1),
                 )
-                if g == PASSES - 1:
-                    mover(h[:, cols], bank[:, 0:width])
-            return h
 
-        grouped0, spent0 = both_passes(0)
-        for g in range(PASSES):
-            regroup_w1(0, g, spent0[g])
-        operand0 = quantise_w1("0", grouped0)
-
-        w1_raw.append(by_runs(load_w1(1, 1, ("word_table0", "w1_raw0_1"))))
-        lists = (pos1, pos2, pos3, pos4)
-        loaded_lists = {i: load_list(i, lists[i]) for i in (0, 2, 3, 1)}
-        pos_sb = [loaded_lists[i] for i in range(4)]
-        for piece in range(2):
-            width = S // 2
-            nc.vector.tensor_copy(
-                x_codes[1][:, piece * width : (piece + 1) * width],
-                word_tables[1][:].indirect(offs_sb[:, piece * width // ENTRIES : (piece + 1) * width // ENTRIES]),
+        for c in range(PACK):
+            first_product(c, 0)
+        nc.vector.tensor_copy(x_codes[1][:], word_tables[1][:].indirect(offs_sb[:]))
+        regroup(nc.scalar.copy, w1_grouped[1], w1_right, P // 2, 0, 24)
+        regroup(nc.vector.tensor_copy, w1_grouped[1], w1_right, P // 2, 24, 40)
+        for c in range(PACK):
+            quantise(
+                w1_codes[1][:, c * P : (c + 1) * P],
+                w1_plane[1][:, c * P : (c + 1) * P],
+                w1_grouped[1][:, c * K_PASS : (c + 1) * K_PASS],
             )
-        wide = load_w1(2, 2, ("w1_grouped0", "word_table1"))
-        wide = [raw.rearrange("p j (b u r) -> p j b u r", u=2, r=RUN) for raw in wide]
-        w1_raw.extend([[raw[:, :, :, u, :] for raw in wide] for u in range(2)])
-        pieces0 = [(banks[0], S // 2), (banks[1], S // 4), (banks[7], S // 4)]
-        h_tiles = [first_product(0, operand0, pieces0, nc.vector.tensor_copy, by_pass=True)]
-        w2_raw = sb([P, PACK, N], F32, "w2_raw", "w1_codes0")
-        w2_rows = w2.rearrange("(b u r e) c -> u b r (e c)", u=2, r=8, e=2)
-        for u in range(2):
-            nc.sync.dma_start(w2_raw[:, 2 * u : 2 * u + 2, :].rearrange("p e c -> p (e c)"), w2_rows[u])
-        pieces1 = [(banks[2], S // 2), (banks[4], S // 2)]
-        spent1 = [sb([P, V], F32, "w1_grouped1_%d" % g)[:] for g in range(PASSES)]
-        for g in range(PASSES):
-            regroup_w1(1, g, spent1[g])
-        operand1 = quantise_w1("1_0", spent1[0], "w1_plane0")
-        grouped_early = work_tile("w1_grouped_early", 2 * V)
-        spent3 = [grouped_early[:, V : 2 * V], second_edges[2, 1][:, V : 2 * V]]
+            first_product(c, 1)
 
-        z_flat = [sb([P, H], BF16, "z_rows%d" % half)[:] for half in range(V // P)]
-        z_rows = [rows.rearrange("v (u n) -> v u n", u=2) for rows in z_flat]
+        h_tiles = [sb([P, S], F32, "h%d" % c) for c in range(PACK)]
 
-        def pick(i, c, v0, count):
-            return h_tiles[c][:].indirect(pos_sb[i][:, v0 // ENTRIES : (v0 + count) // ENTRIES])
+        def halve_on_scalar(out, bank):
+            nc.scalar.activation(out, bank, COPY, scale=0.5)
 
-        def fetch_base(base, c):
-            nc.vector.tensor_copy(base, pick(0, c, 0, V))
+        def halve_on_vector(out, bank):
+            nc.vector.tensor_scalar(out, bank, 0.5, None, ALU.mult)
 
-        def fetch_gap(gap, i, base, c, v0, count):
-            nc.vector.tensor_tensor(gap, pick(i, c, v0, count), base, ALU.subtract)
+        def fetch_on_scalar(out, window):
+            nc.scalar.activation(out, window, COPY)
 
-        def lesser(low, gap_c, gap_d):
-            nc.vector.tensor_tensor(low, gap_c, gap_d, ALU.min)
+        lower = sb([P, 2, PACK, HALF], F32, "lower")
+        upper = sb([P, 2, PACK, HALF], F32, "upper")
 
-        def greater(high, gap_c, gap_d):
-            nc.vector.tensor_tensor(high, gap_c, gap_d, ALU.max)
+        def picked_tile(c, v0, count):
+            return sb([P, 2, 2, count], F32, "picked%d_%d" % (c, v0))
 
-        def lower_middle(out, gap_b, low):
-            nc.vector.scalar_tensor_tensor(out, gap_b, 0.0, low, ALU.min, ALU.max)
+        def fetch(mover, picked, i, c, v0, count):
+            window = h_tiles[c][:].indirect(pos_sb[i][:, v0 // ENTRIES : (v0 + count) // ENTRIES])
+            mover(picked[:, i % 2, i // 2, :], window)
 
-        def upper_middle(out, gap_b, high):
-            nc.vector.scalar_tensor_tensor(out, gap_b, 0.0, high, ALU.max, ALU.min)
+        def compare(picked, c, v0, count):
+            small = sb([P, 2, count], F32, "small%d_%d" % (c, v0))
+            large = sb([P, 2, count], F32, "large%d_%d" % (c, v0))
+            nc.vector.tensor_tensor(small[:], picked[:, 0], picked[:, 1], ALU.min)
+            nc.vector.tensor_tensor(large[:], picked[:, 0], picked[:, 1], ALU.max)
+            halves = slice(v0 // HALF, (v0 + count) // HALF)
 
-        def sum_up(total, c, half, terms):
-            for i, term in enumerate(terms):
-                nc.tensor.matmul(total, term, identity[:], start=(i == 0), stop=(i == len(terms) - 1), is_transpose=True)
-            if c < 2:
-                rows = z_rows[half][:, :, 4 * RUN * c : 4 * RUN * (c + 1)].rearrange("v u (b r) -> v u b r", r=RUN)
-                nc.scalar.activation(rows, total.rearrange("v (b u r) -> v u b r", u=2, r=RUN), COPY, scale=0.5)
-            else:
-                rows = z_flat[half][:, (c - 2) * U_WIDTH + U_WIDTH // 2 : (c - 1) * U_WIDTH]
-                nc.scalar.activation(rows, total, COPY, scale=0.5)
+            def side(tile, n):
+                return tile[:, n, :].rearrange("p (r v) -> p r v", v=HALF)
 
-        def group_z(half, bank):
-            turned = bank[:, 0 : 2 * P].rearrange("p (u v) -> p u v", u=2)
-            for u in range(2):
-                words = z_flat[half][:, u * U_WIDTH : (u + 1) * U_WIDTH].bitcast(F32)
-                nc.tensor.transpose(turned[:, u, :], words, identity[:])
-            grouped = sb([P, P * PACK], BF16, "z_grouped%d" % half)
-            nc.scalar.copy(grouped[:].bitcast(F32).rearrange("p (v u) -> p v u", u=2), turned.rearrange("p u v -> p v u"))
+            nc.vector.tensor_tensor(lower[:, halves, c, :], side(small, 0), side(small, 1), ALU.max)
+            nc.vector.tensor_tensor(upper[:, halves, c, :], side(large, 0), side(large, 1), ALU.min)
+
+        def add_up(half):
+            grouped = sb([P, HALF * PACK], BF16, "z_grouped%d" % half)
+            nc.vector.tensor_tensor(
+                grouped[:].rearrange("p (c i t) -> p c t i", i=LINE, t=PACK),
+                lower[:, half].rearrange("p t (c i) -> p c t i", i=LINE),
+                upper[:, half].rearrange("p t (c i) -> p c t i", i=LINE),
+                ALU.add,
+            )
             return grouped
 
-        def work(name, width=V):
-            return sb([P, width], F32, name)[:]
+        def fetch_all(c, v0, count):
+            picked = picked_tile(c, v0, count)
+            for i in range(4):
+                fetch(fetch_on_scalar, picked, i, c, v0, count)
+            return picked
 
-        first, second = slice(0, P), slice(P, V)
+        halve_on_vector(h_tiles[0][:, 0 : S // 2], banks[0][:, 0 : S // 2])
+        halve_on_scalar(h_tiles[0][:, S // 2 : S], banks[1][:, 0 : S // 2])
+        picked0 = picked_tile(0, 0, V)
+        for i in range(4):
+            fetch(nc.vector.tensor_copy if i % 2 else fetch_on_scalar, picked0, i, 0, 0, V)
+        halve_on_scalar(h_tiles[1][:], banks[2][:])
+        picked1 = fetch_all(1, 0, V)
+        compare(picked0, 0, 0, V)
 
-        def sum_all(c, terms, sum_banks):
-            for half, cols in enumerate((first, second)):
-                sum_up(sum_banks[half][:, cols], c, half, [term[:, cols] for term in terms])
-
-        def flanked(tile):
-            return tile[:, V // 2 : V // 2 + V], tile[:, 0:V], tile[:, V : 2 * V]
-
-        def shortfall(out, gap_b):
-            nc.scalar.activation(out, gap_b, RELU, scale=-1.0)
-
-        def spread(out, gap_b):
-            nc.scalar.activation(out, gap_b, ABS)
-
-        def least(out, base, short):
-            nc.gpsimd.tensor_tensor(out, base, short, ALU.subtract)
-
-        halves2 = [(banks[3], S // 2), (banks[5], S // 2)]
-        halves3 = halves2
-
-        base0 = work("base0")
-        fetch_base(base0, 0)
-        operand1 = operand1 + quantise_w1("1_1", spent1[1], "w1_grouped1_0")
-        grouped2_0 = grouped_early[:, 0:V]
-        grouped2_1, low0, high0 = flanked(work("w1_grouped2_1", 2 * V))
-        regroup_w1(2, 0, grouped2_0)
-        regroup_w1(3, 0, spent3[0])
-        gap_c0, gap_d0, gap_b0 = edges[1, 1][0], spent1[1], edges[1, 1][1]
-        fetch_gap(gap_c0, 2, base0, 0, 0, V)
-        fetch_gap(gap_d0, 3, base0, 0, 0, V)
-        fetch_gap(gap_b0, 1, base0, 0, 0, V)
-        early2, early3 = quantise_w1("_early", grouped_early)
-        h_tiles.append(first_product(1, operand1, pieces1, nc.scalar.copy, by_pass=True, in_place_of="w1_grouped0"))
-        regroup_w1(2, 1, grouped2_1, slice(7, 8))
-        regroup_w1(2, 1, grouped2_1, slice(0, 7))
-        regroup_w1(3, 1, spent3[1])
-
-        gap_b1, upper0, gap_c1 = flanked(wide_edges[2, 1])
-        base1, lower0, short1, least1 = work("base1"), edges[2, 1][1], work("short1"), low0
-        fetch_base(base1, 1)
-        operand2 = [early2] + quantise_w1("2_1", grouped2_1)
-        fetch_gap(gap_b1, 1, base1, 1, 0, V)
-        lesser(low0, gap_c0, gap_d0)
-        greater(high0, gap_c0, gap_d0)
-        lower_middle(lower0, gap_b0, low0)
-        shortfall(short1, gap_b1)
-        h_tiles.append(first_product(2, operand2, halves2, nc.scalar.copy, by_pass=True))
-        spread1 = sb([P, V], F32, "spread1", "w1_codes2_1")[:]
-        spread(spread1, gap_b1)
-
-        operand3 = [early3] + quantise_w1("3_1", spent3[1])
-        base2 = work("base2")
-        gap_b2, high1, low1 = flanked(work("gap_b2", 2 * V))
-        short2, least2 = work("short2"), work("least2")
-        gap_d1 = gap_b0
-        fetch_base(base2, 2)
-        least(least1, base1, short1)
-        upper_middle(upper0, gap_b0, high0)
-        fetch_gap(gap_b2, 1, base2, 2, 0, V)
-        shortfall(short2, gap_b2)
-        h_tiles.append(first_product(3, operand3, halves3, nc.scalar.copy))
-        spread2 = sb([P, V], F32, "spread2", "w1_codes3_1")[:]
-        spread(spread2, gap_b2)
-        fetch_gap(gap_c1, 2, least1, 1, 0, V)
-        fetch_gap(gap_d1, 3, least1, 1, 0, V)
-        sum_all(0, (base0, base0, lower0, upper0), [banks[3]] * 2)
-
-        base3 = spent3[1]
-        lower1, upper1 = work("lower1"), work("upper1")
-        fetch_base(base3, 3)
-        least(least2, base2, short2)
-        greater(high1, gap_c1, gap_d1)
-        lesser(low1, gap_c1, gap_d1)
-        lesser(upper1, spread1, high1)
-        nc.scalar.activation(lower1, low1, RELU)
-        sum_all(1, (least1, least1, lower1, upper1), [banks[0]] * 2)
-
-        w2_grouped = sb([P, N * PACK], BF16, "w2_grouped", "w1_grouped0")
-        dealt = w2_grouped[:].rearrange("p (t m j) -> p m j t", t=PACK, j=PACK)
-        source = w2_raw[:].rearrange("p j (m t) -> p m j t", t=PACK)
-        for piece in range(W2_PIECES):
-            part = slice(piece * P // W2_PIECES, (piece + 1) * P // W2_PIECES)
-            nc.scalar.copy(dealt[:, part], source[:, part])
-
-        gap_c2, gap_d2 = work("gap_c2"), work("gap_d2")
-        high2, low2, lower2, upper2 = work("high2"), work("low2"), work("lower2"), work("upper2")
-        gap_c3, gap_d3, gap_b3 = short2[:, first], base2[:, first], gap_c2[:, first]
-        early = [work("early%d" % i, P) for i in range(4)]
-        late = [work("late%d" % i, P) for i in range(4)]
-
-        def fetch_last(gap, i, half):
-            fetch_gap(gap, i, base3[:, (first, second)[half]], 3, half * P, P)
-
-        def finish_half(half, gap_b, tiles, bank):
-            cols = (first, second)[half]
-            low, high, lower, upper = tiles
-            lesser(low, gap_c3, gap_d3)
-            greater(high, gap_c3, gap_d3)
-            lower_middle(lower, gap_b, low)
-            upper_middle(upper, gap_b, high)
-            sum_up(bank[:, 0:P], 3, half, (base3[:, cols], base3[:, cols], lower, upper))
-
-        fetch_gap(gap_c2, 2, least2, 2, 0, V)
-        fetch_gap(gap_d2, 3, least2, 2, 0, V)
-        fetch_last(gap_c3, 2, 0)
-        greater(high2, gap_c2, gap_d2)
-        lesser(low2, gap_c2, gap_d2)
-        fetch_last(gap_d3, 3, 0)
-        lesser(upper2, spread2, high2)
-        nc.scalar.activation(lower2, low2, RELU)
-        sum_all(2, (least2, least2, lower2, upper2), banks[4:6])
-        fetch_last(gap_b3, 1, 0)
-
-        finish_half(0, gap_b3, early, banks[6])
-        z_grouped = [group_z(0, banks[1])]
-        for gap, i in ((gap_c3, 2), (gap_d3, 3), (early[0], 1)):
-            fetch_last(gap, i, 1)
-        finish_half(1, early[0], late, banks[6])
-        z_grouped.append(group_z(1, banks[2]))
-
-        w2_codes = sb([P, N], U32, "w2_codes", "late0")
+        w2_grouped = sb([P, N * PACK], BF16, "w2_grouped")
+        regroup(nc.vector.tensor_copy, w2_grouped, w2_raw, 0, 0, P)
+        halve_on_scalar(h_tiles[2][:], banks[3][:])
+        picked20 = fetch_all(2, 0, HALF)
+        compare(picked1, 1, 0, V)
+        w2_codes = sb([P, N], U32, "w2_codes")
         w2_plane = sb([P, N], U8, "w2_plane")
-        nc.vector.quantize_mx(w2_codes[:].bitcast(FP8X4), w2_plane[:], w2_grouped[:])
+        quantise(w2_codes[:], w2_plane[:], w2_grouped[:])
+        halve_on_scalar(h_tiles[3][:], banks[4][:])
+        picked30 = fetch_all(3, 0, HALF)
+        compare(picked20, 2, 0, HALF)
+        picked21 = fetch_all(2, HALF, HALF)
+        compare(picked30, 3, 0, HALF)
+        z_grouped = [add_up(0)]
+        picked31 = fetch_all(3, HALF, HALF)
+        compare(picked21, 2, HALF, HALF)
 
         out_codes = sb([P, V], U32, "out_codes")
         out_plane = sb([P, V], U8, "out_plane")
         out_rows = out_0.rearrange("(p t) v -> p t v", t=PACK)
         out_words = out_1[0].rearrange("p n t -> p (n t)").bitcast(I32)
+        columns = (slice(0, HALF), slice(HALF, V))
 
-        def quantise_z(half, in_place_of=None):
-            codes = sb([P, P], U32, "z_codes%d" % half, in_place_of)
-            plane = sb([P, P], U8, "z_plane%d" % half)
-            nc.vector.quantize_mx(codes[:].bitcast(FP8X4), plane[:], z_grouped[half][:])
+        def quantise_z(half):
+            codes = sb([P, HALF], U32, "z_codes%d" % half)
+            plane = sb([P, HALF], U8, "z_plane%d" % half)
+            quantise(codes[:], plane[:], z_grouped[half][:])
             return codes, plane
 
         def second_product(operand, bank, count):
@@ -376,26 +225,29 @@ def tile_picked_ytrim_none_po_kernel(
             return acc
 
         def group_y(half, acc, mover):
-            grouped = sb([P, P * PACK], BF16, "y_grouped%d" % half)
+            grouped = sb([P, HALF * PACK], BF16, "y_grouped%d" % half)
             mover(grouped[:].rearrange("p (v t) -> p v t", t=PACK), acc.rearrange("p t v -> p v t"))
             return grouped
 
         def store_y(half, y, acc, rows, queue):
             nc.scalar.copy(y[:, rows, :], acc[:, rows, :])
-            queue.dma_start(out_rows[:, rows, (first, second)[half]], y[:, rows, :])
+            queue.dma_start(out_rows[:, rows, columns[half]], y[:, rows, :])
 
         def quantise_y(half, grouped):
-            cols = (first, second)[half]
-            nc.vector.quantize_mx(out_codes[:, cols].bitcast(FP8X4), out_plane[:, cols], grouped[:])
+            quantise(out_codes[:, columns[half]], out_plane[:, columns[half]], grouped[:])
 
-        acc = second_product(quantise_z(0, "late1"), banks[6], PACK)
-        store_y(0, sb([P, PACK, P], F32, "y0"), acc, slice(0, PACK), nc.sync)
-        quantise_y(0, group_y(0, acc, nc.scalar.copy))
+        acc = second_product(quantise_z(0), banks[5], PACK)
+        store_y(0, sb([P, PACK, HALF], F32, "y0"), acc, slice(0, PACK), nc.sync)
+        y0_grouped = group_y(0, acc, nc.scalar.copy)
+
+        compare(picked31, 3, HALF, HALF)
+        z_grouped.append(add_up(1))
+        quantise_y(0, y0_grouped)
 
         operand = quantise_z(1)
-        acc = second_product(operand, banks[5], PACK)
+        acc = second_product(operand, banks[6], PACK)
         grouped = group_y(1, acc, nc.vector.tensor_copy)
-        y = sb([P, PACK, P], F32, "y1")
+        y = sb([P, PACK, HALF], F32, "y1")
         store_y(1, y, second_product(operand, banks[7], 2), slice(0, 2), nc.sync)
         store_y(1, y, acc, slice(2, PACK), nc.scalar)
         quantise_y(1, grouped)

@@ -24,6 +24,7 @@ ENTRIES = 16
 LINE = 4
 BANK = 512
 HALF = V // 2
+QUARTER = V // 4
 
 
 def tile_picked_ytrim_none_po_kernel(
@@ -72,12 +73,16 @@ def tile_picked_ytrim_none_po_kernel(
         w1_right = load_rows(w1, 1, H // 2, H // 2, "w1_raw1_right")
         lists = (pos1, pos2, pos3, pos4)
         pos_sb = [load_list("pos_sb%d" % i, lists[i], V) for i in range(4)]
-        w2_raw = load_rows(w2, 0, 0, N, "w2_raw")
+        w2_raw = [load_rows(w2, 0, c0, N // 2, "w2_raw%d" % c0) for c0 in (0, N // 2)]
 
         def regroup(mover, grouped, raw, m0, first, count):
             dealt = grouped[:].rearrange("p (t m j) -> p m j t", t=PACK, j=PACK)
             source = raw[:].rearrange("p j (m t) -> p m j t", t=PACK)
             mover(dealt[:, m0 + first : m0 + first + count], source[:, first : first + count])
+
+        def regroup_by_words(mover, grouped, raw, m0, count):
+            dealt = grouped[:].rearrange("p (t m j) -> p m t j", t=PACK, j=PACK)
+            mover(dealt[:, m0 : m0 + count], raw[:].rearrange("p j (m t) -> p m t j", t=PACK))
 
         def quantise(codes, plane, grouped):
             nc.vector.quantize_mx(codes.bitcast(FP8X4), plane, grouped)
@@ -121,7 +126,7 @@ def tile_picked_ytrim_none_po_kernel(
             )
             first_product(c, 1)
 
-        h_tiles = [sb([P, S], F32, "h%d" % c) for c in range(PACK)]
+        h_tiles = [sb([P, S], F32, "h%d" % c) for c in range(2)]
 
         def halve_on_scalar(out, bank):
             nc.scalar.activation(out, bank, COPY, scale=0.5)
@@ -129,89 +134,65 @@ def tile_picked_ytrim_none_po_kernel(
         def halve_on_vector(out, bank):
             nc.vector.tensor_scalar(out, bank, 0.5, None, ALU.mult)
 
+        def round_on_gpsimd(out, source):
+            nc.gpsimd.tensor_scalar(out, source, 1.0, 0.0, ALU.mult, ALU.add)
+
         def fetch_on_scalar(out, window):
             nc.scalar.activation(out, window, COPY)
 
-        lower = sb([P, 2, PACK, HALF], F32, "lower")
-        upper = sb([P, 2, PACK, HALF], F32, "upper")
-
-        def picked_tile(c, v0, count):
-            return sb([P, 2, 2, count], F32, "picked%d_%d" % (c, v0))
+        lower = sb([P, PACK, V], F32, "lower")
+        upper = sb([P, PACK, V], F32, "upper")
 
         def fetch(mover, picked, i, c, v0, count):
             window = h_tiles[c][:].indirect(pos_sb[i][:, v0 // ENTRIES : (v0 + count) // ENTRIES])
-            mover(picked[:, i % 2, i // 2, :], window)
+            mover(picked[i % 2][:, i // 2, :], window)
 
-        def compare(picked, c, v0, count):
+        def fetch_all(c, v0, count, movers=(fetch_on_scalar,) * 4):
+            picked = [sb([P, 2, count], F32, "picked%d_%d_%d" % (c, v0, side)) for side in range(2)]
+            for i in range(4):
+                fetch(movers[i], picked, i, c, v0, count)
+            return picked, c, v0, count
+
+        def sort_pairs(unit):
+            picked, c, v0, count = unit
             small = sb([P, 2, count], F32, "small%d_%d" % (c, v0))
             large = sb([P, 2, count], F32, "large%d_%d" % (c, v0))
-            nc.vector.tensor_tensor(small[:], picked[:, 0], picked[:, 1], ALU.min)
-            nc.vector.tensor_tensor(large[:], picked[:, 0], picked[:, 1], ALU.max)
-            halves = slice(v0 // HALF, (v0 + count) // HALF)
+            nc.vector.tensor_tensor(small[:], picked[0][:], picked[1][:], ALU.min)
+            nc.vector.tensor_tensor(large[:], picked[0][:], picked[1][:], ALU.max)
+            return small, large, c, slice(v0, v0 + count)
 
-            def side(tile, n):
-                return tile[:, n, :].rearrange("p (r v) -> p r v", v=HALF)
+        def middles(pairs):
+            small, large, c, cols = pairs
+            nc.vector.tensor_tensor(lower[:, c, cols], small[:, 0], small[:, 1], ALU.max)
+            nc.vector.tensor_tensor(upper[:, c, cols], large[:, 0], large[:, 1], ALU.min)
 
-            nc.vector.tensor_tensor(lower[:, halves, c, :], side(small, 0), side(small, 1), ALU.max)
-            nc.vector.tensor_tensor(upper[:, halves, c, :], side(large, 0), side(large, 1), ALU.min)
-
-        def add_up(half):
-            grouped = sb([P, HALF * PACK], BF16, "z_grouped%d" % half)
+        def add_up(cols):
+            grouped = sb([P, (cols.stop - cols.start) * PACK], BF16, "z_grouped%d" % cols.start)
             nc.vector.tensor_tensor(
                 grouped[:].rearrange("p (c i t) -> p c t i", i=LINE, t=PACK),
-                lower[:, half].rearrange("p t (c i) -> p c t i", i=LINE),
-                upper[:, half].rearrange("p t (c i) -> p c t i", i=LINE),
+                lower[:, :, cols].rearrange("p t (c i) -> p c t i", i=LINE),
+                upper[:, :, cols].rearrange("p t (c i) -> p c t i", i=LINE),
                 ALU.add,
             )
             return grouped
 
-        def fetch_all(c, v0, count):
-            picked = picked_tile(c, v0, count)
-            for i in range(4):
-                fetch(fetch_on_scalar, picked, i, c, v0, count)
-            return picked
-
-        halve_on_vector(h_tiles[0][:, 0 : S // 2], banks[0][:, 0 : S // 2])
-        halve_on_scalar(h_tiles[0][:, S // 2 : S], banks[1][:, 0 : S // 2])
-        picked0 = picked_tile(0, 0, V)
-        for i in range(4):
-            fetch(nc.vector.tensor_copy if i % 2 else fetch_on_scalar, picked0, i, 0, 0, V)
-        halve_on_scalar(h_tiles[1][:], banks[2][:])
-        picked1 = fetch_all(1, 0, V)
-        compare(picked0, 0, 0, V)
-
-        w2_grouped = sb([P, N * PACK], BF16, "w2_grouped")
-        regroup(nc.vector.tensor_copy, w2_grouped, w2_raw, 0, 0, P)
-        halve_on_scalar(h_tiles[2][:], banks[3][:])
-        picked20 = fetch_all(2, 0, HALF)
-        compare(picked1, 1, 0, V)
+        w2_grouped = sb([P, N * PACK], BF16, "w2_grouped", "w1_grouped1")
         w2_codes = sb([P, N], U32, "w2_codes")
         w2_plane = sb([P, N], U8, "w2_plane")
-        quantise(w2_codes[:], w2_plane[:], w2_grouped[:])
-        halve_on_scalar(h_tiles[3][:], banks[4][:])
-        picked30 = fetch_all(3, 0, HALF)
-        compare(picked20, 2, 0, HALF)
-        picked21 = fetch_all(2, HALF, HALF)
-        compare(picked30, 3, 0, HALF)
-        z_grouped = [add_up(0)]
-        picked31 = fetch_all(3, HALF, HALF)
-        compare(picked21, 2, HALF, HALF)
-
         out_codes = sb([P, V], U32, "out_codes")
         out_plane = sb([P, V], U8, "out_plane")
         out_rows = out_0.rearrange("(p t) v -> p t v", t=PACK)
         out_words = out_1[0].rearrange("p n t -> p (n t)").bitcast(I32)
-        columns = (slice(0, HALF), slice(HALF, V))
 
-        def quantise_z(half):
-            codes = sb([P, HALF], U32, "z_codes%d" % half)
-            plane = sb([P, HALF], U8, "z_plane%d" % half)
-            quantise(codes[:], plane[:], z_grouped[half][:])
+        def quantise_z(grouped, cols):
+            codes = sb([P, cols.stop - cols.start], U32, "z_codes%d" % cols.start)
+            plane = sb([P, cols.stop - cols.start], U8, "z_plane%d" % cols.start)
+            quantise(codes[:], plane[:], grouped[:])
             return codes, plane
 
         def second_product(operand, bank, count):
             z_codes, z_plane = operand
-            acc = bank[:].rearrange("p (t v) -> p t v", t=PACK)
+            acc = bank[:, 0 : PACK * z_plane.shape[1]].rearrange("p (t v) -> p t v", t=PACK)
             for t in range(count):
                 nc.tensor.matmul_mx(
                     acc[:, t, :],
@@ -224,33 +205,68 @@ def tile_picked_ytrim_none_po_kernel(
                 )
             return acc
 
-        def group_y(half, acc, mover):
-            grouped = sb([P, HALF * PACK], BF16, "y_grouped%d" % half)
+        def group_y(cols, acc, mover):
+            grouped = sb([P, (cols.stop - cols.start) * PACK], BF16, "y_grouped%d" % cols.start)
             mover(grouped[:].rearrange("p (v t) -> p v t", t=PACK), acc.rearrange("p t v -> p v t"))
             return grouped
 
-        def store_y(half, y, acc, rows, queue):
+        def y_tile(cols):
+            return sb([P, PACK, cols.stop - cols.start], F32, "y%d" % cols.start)
+
+        def store_y(cols, y, acc, rows, queue):
             nc.scalar.copy(y[:, rows, :], acc[:, rows, :])
-            queue.dma_start(out_rows[:, rows, columns[half]], y[:, rows, :])
+            queue.dma_start(out_rows[:, rows, cols], y[:, rows, :])
 
-        def quantise_y(half, grouped):
-            quantise(out_codes[:, columns[half]], out_plane[:, columns[half]], grouped[:])
+        def quantise_y(cols, grouped):
+            quantise(out_codes[:, cols], out_plane[:, cols], grouped[:])
 
-        acc = second_product(quantise_z(0), banks[5], PACK)
-        store_y(0, sb([P, PACK, HALF], F32, "y0"), acc, slice(0, PACK), nc.sync)
-        y0_grouped = group_y(0, acc, nc.scalar.copy)
+        def finish_on_scalar(cols, z_grouped, bank):
+            acc = second_product(quantise_z(z_grouped, cols), bank, PACK)
+            store_y(cols, y_tile(cols), acc, slice(0, PACK), nc.sync)
+            return group_y(cols, acc, nc.scalar.copy)
 
-        compare(picked31, 3, HALF, HALF)
-        z_grouped.append(add_up(1))
-        quantise_y(0, y0_grouped)
+        first, second, third = slice(0, HALF), slice(HALF, HALF + QUARTER), slice(HALF + QUARTER, V)
 
-        operand = quantise_z(1)
-        acc = second_product(operand, banks[6], PACK)
-        grouped = group_y(1, acc, nc.vector.tensor_copy)
-        y = sb([P, PACK, HALF], F32, "y1")
-        store_y(1, y, second_product(operand, banks[7], 2), slice(0, 2), nc.sync)
-        store_y(1, y, acc, slice(2, PACK), nc.scalar)
-        quantise_y(1, grouped)
+        halve_on_vector(h_tiles[0][:, 0 : S // 2], banks[0][:, 0 : S // 2])
+        halve_on_scalar(h_tiles[0][:, S // 2 : S], banks[1][:, 0 : S // 2])
+        for side in range(2):
+            regroup_by_words(round_on_gpsimd, w2_grouped, w2_raw[side], side * P // 2, P // 2)
+        halve_on_vector(h_tiles[1][:], banks[2][:])
+        unit0 = fetch_all(0, 0, V, (fetch_on_scalar, nc.vector.tensor_copy) * 2)
+        unit1 = fetch_all(1, 0, V)
+        middles(sort_pairs(unit0))
+        for side in range(2):
+            h_tiles.append(sb([P, S], F32, "h%d" % (2 + side), "picked0_0_%d" % side))
+            halve_on_scalar(h_tiles[2 + side][:], banks[3 + side][:])
+        unit20 = fetch_all(2, 0, HALF)
+        middles(sort_pairs(unit1))
+        unit30 = fetch_all(3, 0, HALF)
+        middles(sort_pairs(unit20))
+        quantise(w2_codes[:], w2_plane[:], w2_grouped[:])
+        unit21 = fetch_all(2, HALF, HALF)
+        middles(sort_pairs(unit30))
+        unit31 = fetch_all(3, HALF, QUARTER)
+        unit32 = fetch_all(3, HALF + QUARTER, QUARTER)
+        pairs21 = sort_pairs(unit21)
+        z_first = add_up(first)
+        middles(pairs21)
+        y_first = finish_on_scalar(first, z_first, banks[5])
+        middles(sort_pairs(unit31))
+        pairs32 = sort_pairs(unit32)
+        z_second = add_up(second)
+        middles(pairs32)
+        y_second = finish_on_scalar(second, z_second, banks[6])
+        z_third = add_up(third)
+        quantise_y(first, y_first)
+
+        operand = quantise_z(z_third, third)
+        quantise_y(second, y_second)
+        acc = second_product(operand, banks[7], PACK)
+        grouped = group_y(third, acc, nc.vector.tensor_copy)
+        y = y_tile(third)
+        store_y(third, y, second_product(operand, banks[0], 2), slice(0, 2), nc.sync)
+        store_y(third, y, acc, slice(2, PACK), nc.scalar)
+        quantise_y(third, grouped)
 
         nc.sync.dma_start(out_words, out_codes[:].bitcast(I32))
         for q in range(QUADRANTS):

@@ -137,42 +137,42 @@ def tile_picked_ytrim_none_po_kernel(
         def round_on_gpsimd(out, source):
             nc.gpsimd.tensor_scalar(out, source, 1.0, 0.0, ALU.mult, ALU.add)
 
-        def fetch_on_scalar(out, window):
-            nc.scalar.activation(out, window, COPY)
+        def fetch_on_scalar(out, window, sign):
+            nc.scalar.activation(out, window, COPY, scale=sign)
 
-        lower = sb([P, PACK, V], F32, "lower")
-        upper = sb([P, PACK, V], F32, "upper")
+        def fetch_on_vector(out, window, sign):
+            nc.vector.tensor_copy(out, window)
 
-        def fetch(mover, picked, i, c, v0, count):
-            window = h_tiles[c][:].indirect(pos_sb[i][:, v0 // ENTRIES : (v0 + count) // ENTRIES])
-            mover(picked[i % 2][:, i // 2, :], window)
+        middle = sb([P, 2, PACK, V], F32, "middle")
 
-        def fetch_all(c, v0, count, movers=(fetch_on_scalar,) * 4):
-            picked = [sb([P, 2, count], F32, "picked%d_%d_%d" % (c, v0, side)) for side in range(2)]
+        def fetch_all(c, v0, count, plain_mover=fetch_on_scalar):
+            picked = sb([P, 2, 2, count], F32, "picked%d_%d" % (c, v0))
             for i in range(4):
-                fetch(movers[i], picked, i, c, v0, count)
+                window = h_tiles[c][:].indirect(pos_sb[i][:, v0 // ENTRIES : (v0 + count) // ENTRIES])
+                mover = fetch_on_scalar if i % 2 else plain_mover
+                mover(picked[:, i % 2, i // 2, :], window, -1.0 if i % 2 else 1.0)
             return picked, c, v0, count
 
         def sort_pairs(unit):
             picked, c, v0, count = unit
-            small = sb([P, 2, count], F32, "small%d_%d" % (c, v0))
-            large = sb([P, 2, count], F32, "large%d_%d" % (c, v0))
-            nc.vector.tensor_tensor(small[:], picked[0][:], picked[1][:], ALU.min)
-            nc.vector.tensor_tensor(large[:], picked[0][:], picked[1][:], ALU.max)
-            return small, large, c, slice(v0, v0 + count)
+            ends = sb([P, 2, 2, count], F32, "ends%d_%d" % (c, v0))
+            sides = picked[:].rearrange("p s q v -> p s (q v)")
+            nc.vector.scalar_tensor_tensor(
+                ends[:].rearrange("p s q v -> p s (q v)"), sides, -1.0, sides[:, ::-1, :], ALU.mult, ALU.min
+            )
+            return ends, c, slice(v0, v0 + count)
 
         def middles(pairs):
-            small, large, c, cols = pairs
-            nc.vector.tensor_tensor(lower[:, c, cols], small[:, 0], small[:, 1], ALU.max)
-            nc.vector.tensor_tensor(upper[:, c, cols], large[:, 0], large[:, 1], ALU.min)
+            ends, c, cols = pairs
+            nc.vector.tensor_tensor(middle[:, :, c, cols], ends[:, :, 0, :], ends[:, :, 1, :], ALU.max)
 
         def add_up(cols):
             grouped = sb([P, (cols.stop - cols.start) * PACK], BF16, "z_grouped%d" % cols.start)
             nc.vector.tensor_tensor(
                 grouped[:].rearrange("p (c i t) -> p c t i", i=LINE, t=PACK),
-                lower[:, :, cols].rearrange("p t (c i) -> p c t i", i=LINE),
-                upper[:, :, cols].rearrange("p t (c i) -> p c t i", i=LINE),
-                ALU.add,
+                middle[:, 1, :, cols].rearrange("p t (c i) -> p c t i", i=LINE),
+                middle[:, 0, :, cols].rearrange("p t (c i) -> p c t i", i=LINE),
+                ALU.subtract,
             )
             return grouped
 
@@ -232,27 +232,33 @@ def tile_picked_ytrim_none_po_kernel(
         for side in range(2):
             regroup_by_words(round_on_gpsimd, w2_grouped, w2_raw[side], side * P // 2, P // 2)
         halve_on_vector(h_tiles[1][:], banks[2][:])
-        unit0 = fetch_all(0, 0, V, (fetch_on_scalar, nc.vector.tensor_copy) * 2)
+        unit0 = fetch_all(0, 0, V, fetch_on_vector)
+        h_tiles.append(sb([P, S], F32, "h2"))
+        h_tiles.append(sb([P, S], F32, "h3", "h0"))
+        halve_on_vector(h_tiles[2][:], banks[3][:])
         unit1 = fetch_all(1, 0, V)
-        middles(sort_pairs(unit0))
-        for side in range(2):
-            h_tiles.append(sb([P, S], F32, "h%d" % (2 + side), "picked0_0_%d" % side))
-            halve_on_scalar(h_tiles[2 + side][:], banks[3 + side][:])
-        unit20 = fetch_all(2, 0, HALF)
-        middles(sort_pairs(unit1))
-        unit30 = fetch_all(3, 0, HALF)
-        middles(sort_pairs(unit20))
+        pairs0 = sort_pairs(unit0)
         quantise(w2_codes[:], w2_plane[:], w2_grouped[:])
+        middles(pairs0)
+        halve_on_scalar(h_tiles[3][:], banks[4][:])
+        unit20 = fetch_all(2, 0, HALF)
+        pairs1 = sort_pairs(unit1)
+        unit30 = fetch_all(3, 0, HALF)
+        pairs20 = sort_pairs(unit20)
+        middles(pairs1)
         unit21 = fetch_all(2, HALF, HALF)
-        middles(sort_pairs(unit30))
+        pairs30 = sort_pairs(unit30)
+        middles(pairs20)
+        middles(pairs30)
         unit31 = fetch_all(3, HALF, QUARTER)
         unit32 = fetch_all(3, HALF + QUARTER, QUARTER)
         pairs21 = sort_pairs(unit21)
         z_first = add_up(first)
         middles(pairs21)
         y_first = finish_on_scalar(first, z_first, banks[5])
-        middles(sort_pairs(unit31))
+        pairs31 = sort_pairs(unit31)
         pairs32 = sort_pairs(unit32)
+        middles(pairs31)
         z_second = add_up(second)
         middles(pairs32)
         y_second = finish_on_scalar(second, z_second, banks[6])

@@ -53,10 +53,11 @@ def tile_picked_ytrim_none_po_kernel(
             nc.sync.dma_start(table[:].bitcast(I32), x_words[g].rearrange("p n t -> p (n t)").bitcast(I32))
             return table
 
-        def load_scales(g):
-            for q in range(QUADRANTS):
-                rows = scale_table[32 * q + 4 * g : 32 * q + 4 * g + 4, :]
-                nc.sync.dma_start(rows.bitcast(I32), x_scales[g][4 * q : 4 * q + 4, :].bitcast(I32))
+        def load_scales(rows):
+            for r in rows:
+                for g in range(PASSES):
+                    place = scale_table[4 * g + r : P : 32, :]
+                    nc.sync.dma_start(place.bitcast(I32), x_scales[g][r : 4 * QUADRANTS : 4, :].bitcast(I32))
 
         def load_list(name, pos, entries):
             list_tile = sb([P, entries // ENTRIES], U16, name)
@@ -65,20 +66,20 @@ def tile_picked_ytrim_none_po_kernel(
 
         w1_first = load_rows(w1, 0, 0, H, "w1_raw0")
         offs_sb = load_list("offs_sb", offs, S)
-        load_scales(0)
+        load_scales((0, 1))
         word_tables = [load_words(0)]
         w1_left = load_rows(w1, 1, 0, H // 2, "w1_raw1_left")
-        load_scales(1)
+        load_scales((2, 3))
         word_tables.append(load_words(1))
         w1_right = load_rows(w1, 1, H // 2, H // 2, "w1_raw1_right")
         lists = (pos1, pos2, pos3, pos4)
         pos_sb = [load_list("pos_sb%d" % i, lists[i], V) for i in range(4)]
         w2_raw = [load_rows(w2, 0, c0, N // 2, "w2_raw%d" % c0) for c0 in (0, N // 2)]
 
-        def regroup(mover, grouped, raw, m0, first, count):
+        def regroup(mover, grouped, raw, m0, first, count, tiles=slice(0, PACK)):
             dealt = grouped[:].rearrange("p (t m j) -> p m j t", t=PACK, j=PACK)
             source = raw[:].rearrange("p j (m t) -> p m j t", t=PACK)
-            mover(dealt[:, m0 + first : m0 + first + count], source[:, first : first + count])
+            mover(dealt[:, m0 + first : m0 + first + count, :, tiles], source[:, first : first + count, :, tiles])
 
         def regroup_by_words(mover, grouped, raw, m0, count):
             dealt = grouped[:].rearrange("p (t m j) -> p m t j", t=PACK, j=PACK)
@@ -88,7 +89,7 @@ def tile_picked_ytrim_none_po_kernel(
             nc.vector.quantize_mx(codes.bitcast(FP8X4), plane, grouped)
 
         w1_grouped = [sb([P, H * PACK], BF16, "w1_grouped%d" % g) for g in range(PASSES)]
-        w1_codes = [sb([P, H], U32, "w1_codes%d" % g) for g in range(PASSES)]
+        w1_codes = [sb([P, H], U32, "w1_codes0")]
         w1_plane = [sb([P, H], U8, "w1_plane%d" % g) for g in range(PASSES)]
         x_codes = [sb([P, S], U32, "x_codes%d" % g) for g in range(PASSES)]
         x_plane = sb([P, S], U8, "x_plane")
@@ -99,7 +100,10 @@ def tile_picked_ytrim_none_po_kernel(
         regroup(nc.scalar.copy, w1_grouped[1], w1_left, 0, 0, P // 2)
         nc.vector.tensor_copy(x_plane[:], scale_table[:].indirect(offs_sb[:]))
 
-        pieces = [[(banks[0], 0, S // 2), (banks[1], S // 2, S // 2)]] + [[(banks[1 + c], 0, S)] for c in range(1, PACK)]
+        w1_codes.append(sb([P, H], U32, "w1_codes1", "scale_table"))
+        quarter = S // 4
+        pieces = [[(banks[(0, 1, 5, 6)[i]], i * quarter, quarter) for i in range(4)]]
+        pieces += [[(banks[1 + c], 0, S)] for c in range(1, PACK)]
 
         def first_product(c, g):
             for bank, start, width in pieces[c]:
@@ -115,16 +119,20 @@ def tile_picked_ytrim_none_po_kernel(
 
         for c in range(PACK):
             first_product(c, 0)
+        def quantise_w1(start, stop):
+            quantise(w1_codes[1][:, start:stop], w1_plane[1][:, start:stop], w1_grouped[1][:, PACK * start : PACK * stop])
+
+        quantise_w1(0, P // 2)
         nc.vector.tensor_copy(x_codes[1][:], word_tables[1][:].indirect(offs_sb[:]))
-        regroup(nc.scalar.copy, w1_grouped[1], w1_right, P // 2, 0, 24)
-        regroup(nc.vector.tensor_copy, w1_grouped[1], w1_right, P // 2, 24, 40)
-        for c in range(PACK):
-            quantise(
-                w1_codes[1][:, c * P : (c + 1) * P],
-                w1_plane[1][:, c * P : (c + 1) * P],
-                w1_grouped[1][:, c * K_PASS : (c + 1) * K_PASS],
-            )
-            first_product(c, 1)
+        regroup(nc.vector.tensor_copy, w1_grouped[1], w1_right, P // 2, 0, P // 2, slice(0, 2))
+        regroup(nc.scalar.copy, w1_grouped[1], w1_right, P // 2, 0, P // 2, slice(2, PACK))
+        quantise_w1(P // 2, P)
+        first_product(0, 1)
+        quantise_w1(P, 2 * P)
+        first_product(1, 1)
+        quantise_w1(2 * P, H)
+        first_product(2, 1)
+        first_product(3, 1)
 
         h_tiles = [sb([P, S], F32, "h%d" % c) for c in range(2)]
 
@@ -205,8 +213,8 @@ def tile_picked_ytrim_none_po_kernel(
                 )
             return acc
 
-        def group_y(cols, acc, mover):
-            grouped = sb([P, (cols.stop - cols.start) * PACK], BF16, "y_grouped%d" % cols.start)
+        def group_y(cols, acc, mover, in_place_of=None):
+            grouped = sb([P, (cols.stop - cols.start) * PACK], BF16, "y_grouped%d" % cols.start, in_place_of)
             mover(grouped[:].rearrange("p (v t) -> p v t", t=PACK), acc.rearrange("p t v -> p v t"))
             return grouped
 
@@ -220,15 +228,10 @@ def tile_picked_ytrim_none_po_kernel(
         def quantise_y(cols, grouped):
             quantise(out_codes[:, cols], out_plane[:, cols], grouped[:])
 
-        def finish_on_scalar(cols, z_grouped, bank):
-            acc = second_product(quantise_z(z_grouped, cols), bank, PACK)
-            store_y(cols, y_tile(cols), acc, slice(0, PACK), nc.sync)
-            return group_y(cols, acc, nc.scalar.copy)
-
         first, second, third = slice(0, HALF), slice(HALF, HALF + QUARTER), slice(HALF + QUARTER, V)
 
-        halve_on_vector(h_tiles[0][:, 0 : S // 2], banks[0][:, 0 : S // 2])
-        halve_on_scalar(h_tiles[0][:, S // 2 : S], banks[1][:, 0 : S // 2])
+        for i, (bank, start, width) in enumerate(pieces[0]):
+            (halve_on_scalar if i % 2 else halve_on_vector)(h_tiles[0][:, start : start + width], bank[:, 0:width])
         for side in range(2):
             regroup_by_words(round_on_gpsimd, w2_grouped, w2_raw[side], side * P // 2, P // 2)
         halve_on_vector(h_tiles[1][:], banks[2][:])
@@ -255,18 +258,21 @@ def tile_picked_ytrim_none_po_kernel(
         pairs21 = sort_pairs(unit21)
         z_first = add_up(first)
         middles(pairs21)
-        y_first = finish_on_scalar(first, z_first, banks[5])
+        y_first = y_tile(first)
+        store_y(first, y_first, second_product(quantise_z(z_first, first), banks[5], PACK), slice(0, PACK), nc.sync)
         pairs31 = sort_pairs(unit31)
         pairs32 = sort_pairs(unit32)
         middles(pairs31)
         z_second = add_up(second)
         middles(pairs32)
-        y_second = finish_on_scalar(second, z_second, banks[6])
+        acc = second_product(quantise_z(z_second, second), banks[6], PACK)
+        store_y(second, y_tile(second), acc, slice(0, PACK), nc.sync)
+        rounded_second = group_y(second, acc, nc.scalar.copy)
         z_third = add_up(third)
-        quantise_y(first, y_first)
-
         operand = quantise_z(z_third, third)
-        quantise_y(second, y_second)
+        rounded_first = group_y(first, y_first[:], nc.vector.tensor_copy, "z_grouped%d" % third.start)
+        quantise_y(second, rounded_second)
+        quantise_y(first, rounded_first)
         acc = second_product(operand, banks[7], PACK)
         grouped = group_y(third, acc, nc.vector.tensor_copy)
         y = y_tile(third)

@@ -198,10 +198,10 @@ def tile_picked_ytrim_none_po_kernel(
             quantise(codes[:], plane[:], grouped[:])
             return codes, plane
 
-        def second_product(operand, bank, count):
+        def second_product(operand, bank, rows=slice(0, PACK)):
             z_codes, z_plane = operand
             acc = bank[:, 0 : PACK * z_plane.shape[1]].rearrange("p (t v) -> p t v", t=PACK)
-            for t in range(count):
+            for t in range(rows.start, rows.stop):
                 nc.tensor.matmul_mx(
                     acc[:, t, :],
                     lhsT=w2_codes[:, t * P : (t + 1) * P].bitcast(FP8X4),
@@ -213,10 +213,8 @@ def tile_picked_ytrim_none_po_kernel(
                 )
             return acc
 
-        def group_y(cols, acc, mover, in_place_of=None):
-            grouped = sb([P, (cols.stop - cols.start) * PACK], BF16, "y_grouped%d" % cols.start, in_place_of)
-            mover(grouped[:].rearrange("p (v t) -> p v t", t=PACK), acc.rearrange("p t v -> p v t"))
-            return grouped
+        def round_y(grouped, values, mover):
+            mover(grouped.rearrange("p (v t) -> p v t", t=PACK), values.rearrange("p t v -> p v t"))
 
         def y_tile(cols):
             return sb([P, PACK, cols.stop - cols.start], F32, "y%d" % cols.start)
@@ -259,26 +257,28 @@ def tile_picked_ytrim_none_po_kernel(
         z_first = add_up(first)
         middles(pairs21)
         y_first = y_tile(first)
-        store_y(first, y_first, second_product(quantise_z(z_first, first), banks[5], PACK), slice(0, PACK), nc.sync)
+        store_y(first, y_first, second_product(quantise_z(z_first, first), banks[5]), slice(0, PACK), nc.sync)
         pairs31 = sort_pairs(unit31)
         pairs32 = sort_pairs(unit32)
         middles(pairs31)
         z_second = add_up(second)
         middles(pairs32)
-        acc = second_product(quantise_z(z_second, second), banks[6], PACK)
+        acc = second_product(quantise_z(z_second, second), banks[6])
         store_y(second, y_tile(second), acc, slice(0, PACK), nc.sync)
-        rounded_second = group_y(second, acc, nc.scalar.copy)
+        last_two = slice(second.start, third.stop)
+        rounded_last = sb([P, HALF * PACK], BF16, "y_grouped_last")
+        round_y(rounded_last[:, 0 : QUARTER * PACK], acc, nc.scalar.copy)
         z_third = add_up(third)
         operand = quantise_z(z_third, third)
-        rounded_first = group_y(first, y_first[:], nc.vector.tensor_copy, "z_grouped%d" % third.start)
-        quantise_y(second, rounded_second)
+        rounded_first = sb([P, HALF * PACK], BF16, "y_grouped_first", "z_grouped%d" % third.start)
+        round_y(rounded_first[:], y_first[:], nc.vector.tensor_copy)
         quantise_y(first, rounded_first)
-        acc = second_product(operand, banks[7], PACK)
-        grouped = group_y(third, acc, nc.vector.tensor_copy)
+        acc = second_product(operand, banks[7])
+        round_y(rounded_last[:, QUARTER * PACK : HALF * PACK], acc, nc.vector.tensor_copy)
         y = y_tile(third)
-        store_y(third, y, second_product(operand, banks[0], 2), slice(0, 2), nc.sync)
+        store_y(third, y, second_product(operand, banks[0], slice(0, 2)), slice(0, 2), nc.sync)
         store_y(third, y, acc, slice(2, PACK), nc.scalar)
-        quantise_y(third, grouped)
+        quantise_y(last_two, rounded_last)
 
         nc.sync.dma_start(out_words, out_codes[:].bitcast(I32))
         for q in range(QUADRANTS):

@@ -257,7 +257,9 @@ def tile_picked_ytrim_none_po_kernel(
         z_first = add_up(first)
         middles(pairs21)
         y_first = y_tile(first)
-        store_y(first, y_first, second_product(quantise_z(z_first, first), banks[5]), slice(0, PACK), nc.sync)
+        operand_first = quantise_z(z_first, first)
+        store_y(first, y_first, second_product(operand_first, banks[5]), slice(0, PACK), nc.sync)
+        first_again = second_product(operand_first, banks[1])
         pairs31 = sort_pairs(unit31)
         pairs32 = sort_pairs(unit32)
         middles(pairs31)
@@ -271,7 +273,7 @@ def tile_picked_ytrim_none_po_kernel(
         z_third = add_up(third)
         operand = quantise_z(z_third, third)
         rounded_first = sb([P, HALF * PACK], BF16, "y_grouped_first", "z_grouped%d" % third.start)
-        round_y(rounded_first[:], y_first[:], nc.vector.tensor_copy)
+        round_y(rounded_first[:], first_again, nc.vector.tensor_copy)
         quantise_y(first, rounded_first)
         acc = second_product(operand, banks[7])
         round_y(rounded_last[:, QUARTER * PACK : HALF * PACK], acc, nc.vector.tensor_copy)

from contextlib import ExitStack

import concourse.mybir as mybir

K, T, S, V, H, N = 1024, 2048, 512, 256, 512, 512
FLOPS = 2 * K * H * S + 2 * H * N * V

F32 = mybir.dt.float32
BF16 = mybir.dt.bfloat16
I32 = mybir.dt.int32
U32 = mybir.dt.uint32
U16 = mybir.dt.uint16
U8 = mybir.dt.uint8
FP8X4 = mybir.dt.float8_e4m3fn_x4
ALU = mybir.AluOpType
COPY = mybir.ActivationFunctionType.Copy

P = 128
PACK = 4
K_PASS = P * PACK
PASSES = K // K_PASS
QUADRANTS = 4
ENTRIES = 16
LINE = 4
BANK = 512
HALF = V // 2
QUARTER = V // 4


def tile_picked_ytrim_none_po_kernel(
    tc, x_words, x_scales, w1, w2, offs, pos1, pos2, pos3, pos4, out_0, out_1, out_2
):
    nc = tc.nc
    with ExitStack() as ctx:
        keep = ctx.enter_context(tc.tile_pool(name="keep", bufs=1))
        psum = ctx.enter_context(tc.psum_pool(name="psum", bufs=1))

        def sb(shape, dtype, name, in_place_of=None):
            return keep.tile(shape, dtype, name=name, tag=in_place_of or name, align_bytes=256)

        banks = [psum.tile([P, BANK], F32, name="bank%d" % i) for i in range(8)]

        scale_table = sb([P, T], U8, "scale_table")
        nc.vector.memset(scale_table[:].bitcast(I32), 0)

        def load_rows(w, g, c0, width, name):
            raw = sb([P, PACK, width], F32, name)
            nc.sync.dma_start(raw[:], w[g * K_PASS : (g + 1) * K_PASS, c0 : c0 + width].rearrange("(p j) c -> p j c", j=PACK))
            return raw

        def load_words(g):
            table = sb([P, T], U32, "word_table%d" % g)
            nc.sync.dma_start(table[:].bitcast(I32), x_words[g].rearrange("p n t -> p (n t)").bitcast(I32))
            return table

        def load_scales(rows):
            for r in rows:
                for g in range(PASSES):
                    place = scale_table[4 * g + r : P : 32, :]
                    nc.sync.dma_start(place.bitcast(I32), x_scales[g][r : 4 * QUADRANTS : 4, :].bitcast(I32))

        def load_list(name, pos, entries):
            list_tile = sb([P, entries // ENTRIES], U16, name)
            nc.sync.dma_start(list_tile[:], pos)
            return list_tile

        w1_first = load_rows(w1, 0, 0, H, "w1_raw0")
        offs_sb = load_list("offs_sb", offs, S)
        load_scales((0, 1))
        word_tables = [load_words(0)]
        w1_left = load_rows(w1, 1, 0, H // 2, "w1_raw1_left")
        load_scales((2, 3))
        word_tables.append(load_words(1))
        w1_right = load_rows(w1, 1, H // 2, H // 2, "w1_raw1_right")
        lists = (pos1, pos2, pos3, pos4)
        pos_sb = [load_list("pos_sb%d" % i, lists[i], V) for i in range(4)]
        w2_raw = [load_rows(w2, 0, c0, N // 2, "w2_raw%d" % c0) for c0 in (0, N // 2)]

        def regroup(mover, grouped, raw, m0, first, count, tiles=slice(0, PACK)):
            dealt = grouped[:].rearrange("p (t m j) -> p m j t", t=PACK, j=PACK)
            source = raw[:].rearrange("p j (m t) -> p m j t", t=PACK)
            mover(dealt[:, m0 + first : m0 + first + count, :, tiles], source[:, first : first + count, :, tiles])

        def regroup_by_words(mover, grouped, raw, m0, count):
            dealt = grouped[:].rearrange("p (t m j) -> p m t j", t=PACK, j=PACK)
            mover(dealt[:, m0 : m0 + count], raw[:].rearrange("p j (m t) -> p m t j", t=PACK))

        def quantise(codes, plane, grouped):
            nc.vector.quantize_mx(codes.bitcast(FP8X4), plane, grouped)

        w1_grouped = [sb([P, H * PACK], BF16, "w1_grouped%d" % g) for g in range(PASSES)]
        w1_codes = [sb([P, H], U32, "w1_codes0")]
        w1_plane = [sb([P, H], U8, "w1_plane%d" % g) for g in range(PASSES)]
        x_codes = [sb([P, S], U32, "x_codes%d" % g) for g in range(PASSES)]
        x_plane = sb([P, S], U8, "x_plane")

        regroup(nc.scalar.copy, w1_grouped[0], w1_first, 0, 0, P)
        nc.vector.tensor_copy(x_codes[0][:], word_tables[0][:].indirect(offs_sb[:]))
        quantise(w1_codes[0][:], w1_plane[0][:], w1_grouped[0][:])
        regroup(nc.scalar.copy, w1_grouped[1], w1_left, 0, 0, P // 2)
        nc.vector.tensor_copy(x_plane[:], scale_table[:].indirect(offs_sb[:]))

        w1_codes.append(sb([P, H], U32, "w1_codes1", "scale_table"))
        quarter = S // 4
        pieces = [[(banks[(0, 1, 5, 6)[i]], i * quarter, quarter) for i in range(4)]]
        pieces += [[(banks[1 + c], 0, S)] for c in range(1, PACK)]

        def first_product(c, g):
            for bank, start, width in pieces[c]:
                nc.tensor.matmul_mx(
                    bank[:, 0:width],
                    lhsT=w1_codes[g][:, c * P : (c + 1) * P].bitcast(FP8X4),
                    lhsT_scale=w1_plane[g][:, c * P : (c + 1) * P],
                    rhs=x_codes[g][:, start : start + width].bitcast(FP8X4),
                    rhs_scale=x_plane[4 * g : P, start : start + width],
                    start=(g == 0),
                    stop=(g == PASSES - 1),
                )

        for c in range(PACK):
            first_product(c, 0)
        def quantise_w1(start, stop):
            quantise(w1_codes[1][:, start:stop], w1_plane[1][:, start:stop], w1_grouped[1][:, PACK * start : PACK * stop])

        quantise_w1(0, P // 2)
        nc.vector.tensor_copy(x_codes[1][:], word_tables[1][:].indirect(offs_sb[:]))
        regroup(nc.vector.tensor_copy, w1_grouped[1], w1_right, P // 2, 0, P // 2, slice(0, 2))
        regroup(nc.scalar.copy, w1_grouped[1], w1_right, P // 2, 0, P // 2, slice(2, PACK))
        quantise_w1(P // 2, P)
        first_product(0, 1)
        quantise_w1(P, 2 * P)
        first_product(1, 1)
        quantise_w1(2 * P, H)
        first_product(2, 1)
        first_product(3, 1)

        h_tiles = [sb([P, S], F32, "h%d" % c) for c in range(2)]

        def halve_on_scalar(out, bank):
            nc.scalar.activation(out, bank, COPY, scale=0.5)

        def halve_on_vector(out, bank):
            nc.vector.tensor_scalar(out, bank, 0.5, None, ALU.mult)

        def round_on_gpsimd(out, source):
            nc.gpsimd.tensor_scalar(out, source, 1.0, 0.0, ALU.mult, ALU.add)

        def fetch_on_scalar(out, window, sign):
            nc.scalar.activation(out, window, COPY, scale=sign)

        def fetch_on_vector(out, window, sign):
            nc.vector.tensor_copy(out, window)

        middle = sb([P, 2, PACK, V], F32, "middle")

        def fetch_all(c, v0, count, plain_mover=fetch_on_scalar):
            picked = sb([P, 2, 2, count], F32, "picked%d_%d" % (c, v0))
            for i in range(4):
                window = h_tiles[c][:].indirect(pos_sb[i][:, v0 // ENTRIES : (v0 + count) // ENTRIES])
                mover = fetch_on_scalar if i % 2 else plain_mover
                mover(picked[:, i % 2, i // 2, :], window, -1.0 if i % 2 else 1.0)
            return picked, c, v0, count

        def sort_pairs(unit):
            picked, c, v0, count = unit
            ends = sb([P, 2, 2, count], F32, "ends%d_%d" % (c, v0))
            sides = picked[:].rearrange("p s q v -> p s (q v)")
            nc.vector.scalar_tensor_tensor(
                ends[:].rearrange("p s q v -> p s (q v)"), sides, -1.0, sides[:, ::-1, :], ALU.mult, ALU.min
            )
            return ends, c, slice(v0, v0 + count)

        def middles(pairs):
            ends, c, cols = pairs
            nc.vector.tensor_tensor(middle[:, :, c, cols], ends[:, :, 0, :], ends[:, :, 1, :], ALU.max)

        def add_up(cols):
            grouped = sb([P, (cols.stop - cols.start) * PACK], BF16, "z_grouped%d" % cols.start)
            nc.vector.tensor_tensor(
                grouped[:].rearrange("p (c i t) -> p c t i", i=LINE, t=PACK),
                middle[:, 1, :, cols].rearrange("p t (c i) -> p c t i", i=LINE),
                middle[:, 0, :, cols].rearrange("p t (c i) -> p c t i", i=LINE),
                ALU.subtract,
            )
            return grouped

        w2_grouped = sb([P, N * PACK], BF16, "w2_grouped", "w1_grouped1")
        w2_codes = sb([P, N], U32, "w2_codes")
        w2_plane = sb([P, N], U8, "w2_plane")
        out_codes = sb([P, V], U32, "out_codes")
        out_plane = sb([P, V], U8, "out_plane")
        out_rows = out_0.rearrange("(p t) v -> p t v", t=PACK)
        out_words = out_1[0].rearrange("p n t -> p (n t)").bitcast(I32)

        def quantise_z(grouped, cols):
            codes = sb([P, cols.stop - cols.start], U32, "z_codes%d" % cols.start)
            plane = sb([P, cols.stop - cols.start], U8, "z_plane%d" % cols.start)
            quantise(codes[:], plane[:], grouped[:])
            return codes, plane

        def second_product(operand, bank, rows=slice(0, PACK)):
            z_codes, z_plane = operand
            acc = bank[:, 0 : PACK * z_plane.shape[1]].rearrange("p (t v) -> p t v", t=PACK)
            for t in range(rows.start, rows.stop):
                nc.tensor.matmul_mx(
                    acc[:, t, :],
                    lhsT=w2_codes[:, t * P : (t + 1) * P].bitcast(FP8X4),
                    lhsT_scale=w2_plane[:, t * P : (t + 1) * P],
                    rhs=z_codes[:].bitcast(FP8X4),
                    rhs_scale=z_plane[:],
                    start=True,
                    stop=True,
                )
            return acc

        def round_y(grouped, values, mover):
            mover(grouped.rearrange("p (v t) -> p v t", t=PACK), values.rearrange("p t v -> p v t"))

        def y_tile(cols):
            return sb([P, PACK, cols.stop - cols.start], F32, "y%d" % cols.start)

        def store_y(cols, y, acc, rows, queue):
            nc.scalar.copy(y[:, rows, :], acc[:, rows, :])
            queue.dma_start(out_rows[:, rows, cols], y[:, rows, :])

        def quantise_y(cols, grouped):
            quantise(out_codes[:, cols], out_plane[:, cols], grouped[:])

        first, second, third = slice(0, HALF), slice(HALF, HALF + QUARTER), slice(HALF + QUARTER, V)

        for i, (bank, start, width) in enumerate(pieces[0]):
            (halve_on_scalar if i % 2 else halve_on_vector)(h_tiles[0][:, start : start + width], bank[:, 0:width])
        for side in range(2):
            regroup_by_words(round_on_gpsimd, w2_grouped, w2_raw[side], side * P // 2, P // 2)
        halve_on_vector(h_tiles[1][:], banks[2][:])
        unit0 = fetch_all(0, 0, V, fetch_on_vector)
        h_tiles.append(sb([P, S], F32, "h2"))
        h_tiles.append(sb([P, S], F32, "h3", "h0"))
        halve_on_vector(h_tiles[2][:], banks[3][:])
        unit1 = fetch_all(1, 0, V)
        pairs0 = sort_pairs(unit0)
        quantise(w2_codes[:], w2_plane[:], w2_grouped[:])
        middles(pairs0)
        halve_on_scalar(h_tiles[3][:], banks[4][:])
        unit20 = fetch_all(2, 0, HALF)
        pairs1 = sort_pairs(unit1)
        unit30 = fetch_all(3, 0, HALF)
        pairs20 = sort_pairs(unit20)
        middles(pairs1)
        unit21 = fetch_all(2, HALF, HALF)
        pairs30 = sort_pairs(unit30)
        middles(pairs20)
        middles(pairs30)
        unit31 = fetch_all(3, HALF, QUARTER)
        unit32 = fetch_all(3, HALF + QUARTER, QUARTER)
        pairs21 = sort_pairs(unit21)
        z_first = add_up(first)
        middles(pairs21)
        y_first = y_tile(first)
        operand_first = quantise_z(z_first, first)
        store_y(first, y_first, second_product(operand_first, banks[5]), slice(0, PACK), nc.sync)
        first_again = second_product(operand_first, banks[1])
        pairs31 = sort_pairs(unit31)
        pairs32 = sort_pairs(unit32)
        middles(pairs31)
        z_second = add_up(second)
        middles(pairs32)
        acc = second_product(quantise_z(z_second, second), banks[6])
        store_y(second, y_tile(second), acc, slice(0, PACK), nc.sync)
        last_two = slice(second.start, third.stop)
        rounded_last = sb([P, HALF * PACK], BF16, "y_grouped_last")
        round_y(rounded_last[:, 0 : QUARTER * PACK], acc, nc.scalar.copy)
        z_third = add_up(third)
        operand = quantise_z(z_third, third)
        rounded_first = sb([P, HALF * PACK], BF16, "y_grouped_first", "z_grouped%d" % third.start)
        round_y(rounded_first[:], first_again, nc.vector.tensor_copy)
        quantise_y(first, rounded_first)
        acc = second_product(operand, banks[7])
        round_y(rounded_last[:, QUARTER * PACK : HALF * PACK], acc, nc.vector.tensor_copy)
        y = y_tile(third)
        store_y(third, y, second_product(operand, banks[0], slice(0, 2)), slice(0, 2), nc.sync)
        store_y(third, y, acc, slice(2, PACK), nc.scalar)
        quantise_y(last_two, rounded_last)

        nc.sync.dma_start(out_words, out_codes[:].bitcast(I32))
        for q in range(QUADRANTS):
            queue = nc.scalar if q >= QUADRANTS // 2 else nc.sync
            queue.dma_start(out_2[0][4 * q : 4 * q + 4, :].bitcast(I32), out_plane[32 * q : 32 * q + 4, :].bitcast(I32))
